import numpy as np, ml_dtypes
CORES = [2,6,10,14,18,22,26,30]
N = 8
BF = ml_dtypes.bfloat16
def gentries(a):
    return np.ascontiguousarray(a.reshape(8, 16, -1).transpose(0, 2, 1)).reshape(8, -1)
def gtable(e):
    e = np.asarray(e); return np.ascontiguousarray(e.reshape(8, -1, 16).transpose(0, 2, 1)).reshape(128, -1).astype(np.int32)
C, T, G, K1, K2, SC, ST, EPS, RO, BO = 448, 896, 128, 176, 256, 160, 192, 8, 3, 1792
H = (N - 1) * G
WB = 16 * C + H
def ghosts(a):
    r, g = np.arange(N), np.arange(8)
    return np.concatenate([a[..., (d - 1) * G:d * G][r ^ d][:, g ^ d] for d in range(1, N)], axis=-1)
def ghostly(rng, c):
    u = np.ones(16 * H, bool); u[c[c >= 16 * T] - 16 * T] = False
    i = np.flatnonzero(c < 0); c[i] = 16 * T + rng.permutation(np.flatnonzero(u))[:len(i)]
    return c
def links(rng, room, share, far):
    ct = np.full((N, 8, 16 * C), -1, np.int64); tv = np.full((N, 8, 16 * T), WB, np.int64)
    for q in range(N):
        for g in range(8):
            for d in range(1, N):
                h = (d - 1) * G + np.flatnonzero(rng.random(G) < share); s = 16 * (d - 1) * G + rng.permutation(16 * G)[:len(h)]
                ct[q, g, h] = 16 * T + s; tv[q ^ d, g ^ d, s] = 16 * C + h
    for q in range(N):
        for g in range(8):
            o = rng.permutation(np.flatnonzero(ct[q, g] < 0)); nf = int(far * len(o))
            rk = np.argsort(rng.random((T, 16)), axis=1)
            own = rng.permutation(np.flatnonzero((rk < room[q, g][:, None]).reshape(-1) & (tv[q, g] == WB)))[:len(o) - nf]
            o = o[:len(own)]; ct[q, g, o] = own; tv[q, g, own] = o
            ct[q, g] = ghostly(rng, ct[q, g])
    return ct, tv
def stir(rng, tv, share):
    for q in range(N):
        for g in range(8):
            s = np.flatnonzero((tv[q, g] < WB) & (rng.random(16 * T) < share)); tv[q, g, s] = rng.permutation(tv[q, g, s])
    return tv
def see(x, ct):
    return np.take_along_axis(np.concatenate([x, ghosts(x)], axis=3), (ct >> 4)[:, :, None, :], 3)
def whole(rng, lo, hi, *shape):
    return rng.integers(lo, hi, shape, dtype=np.int16)
def geo(rng, ct):
    x = whole(rng, 60, 192, N, 8, 16, T); pose = np.repeat(whole(rng, -60, 61, N, 8, 16, C), 16, axis=3)
    e = (whole(rng, -64, 65, N, 8, 16, 16 * C) * whole(rng, 0, EPS + 4, N, 8, 1, 16 * C)) >> 6
    bad = rng.random((N, 8, 1, 16 * C)) < np.repeat(rng.choice(np.array([0.03, 0.1, 0.2, 0.75]), (N, 8, 1, C), p=[0.35, 0.35, 0.2, 0.1]), 16, axis=3)
    o = np.where(bad, whole(rng, 0, 256, N, 8, 16, 16 * C), see(x, ct) - pose + e)
    x0 = np.where(rng.random((N, 8, 1, T)) < 0.15, whole(rng, 0, 256, N, 8, 16, T), x + whole(rng, -2, 3, N, 8, 16, T))
    return o, x0
def pack(o, x, ct, tv):
    return {"obs": np.clip(o, 0, 255).reshape(N, 128, 16 * C).astype(np.float32).astype(BF), "x0": np.clip(x, 0, 255).reshape(N, 128, T).astype(np.float32).astype(BF),
            "ct": np.stack([gtable(a) for a in ct]), "tv": np.stack([gtable(a) for a in tv])}
def setup_inputs(rng):
    ct, tv = links(rng, np.minimum(rng.integers(2, 24, (N, 8, T)), 16), 0.6, 0.08); tv = stir(rng, tv, 0.06)
    o, x0 = geo(rng, ct)
    return pack(o, x0, ct, tv)
def setup_inputs_spread(rng):
    ct, tv = links(rng, rng.integers(1, 17, (N, 8, T)), 0.8, 0.15); tv = stir(rng, tv, 0.1)
    x = np.minimum(np.exp2(8 * rng.random((N, 8, 1, T))) * rng.random((N, 8, 16, T)), 255).astype(np.int16)
    pose = np.repeat((np.exp2(6 * rng.random((N, 8, 1, C))) * (rng.random((N, 8, 16, C)) - 0.6)).astype(np.int16), 16, axis=3)
    e = (np.exp2(6 * rng.random((N, 8, 1, 16 * C), dtype=np.float32)) * (rng.random((N, 8, 16, 16 * C), dtype=np.float32) - 0.5)).astype(np.int16)
    o = see(x, ct) - pose + e; o = np.where(rng.random((N, 8, 1, 16 * C)) < 0.1, whole(rng, 0, 256, N, 8, 16, 16 * C), o)
    x = np.where(rng.random((N, 8, 1, T)) < 0.1, whole(rng, 0, 256, N, 8, 16, T), x)
    return pack(o, x, ct, tv)
def setup_inputs_ends(rng):
    a = 16 * (C // 3); top = 16 * (T + H); sl = np.concatenate([np.arange(a), np.arange(16 * T - a, 16 * T), np.arange(top - (16 * C - 2 * a), top)])
    ct = np.zeros((N, 8, 16 * C), np.int64); tv = np.full((N, 8, 16 * T), WB, np.int64)
    for q in range(N):
        for g in range(8):
            p = rng.permutation(16 * C); j = int(np.argmin(p)); p[j] = p[0]; p[0] = 0
            ct[q, g, p] = sl; tv[q, g, sl[:2 * a]] = p[:2 * a]
            s = 1 + rng.permutation(2 * a - 1)[:H // 2]; tv[q, g, sl[s]] = WB - 1 - rng.permutation(H // 2)[:len(s)]
    rk = np.argsort(rng.random((N, 8, 16)), axis=2)[..., None]
    x = (255 * (rng.random((N, 8, 16, T)) < np.where(rk == 0, 0.875, np.where(rk == 1, 0.125, 0.5)))).astype(np.int16)
    s = see(x, ct); pf = rng.choice(np.array([0.0, 0.0, 0.05, 0.1, 0.15, 0.8]), (N, 8, 1, 16 * C))
    o = np.where(rng.random(s.shape, dtype=np.float32) < pf, 255 - s, s)
    cs = np.repeat(rng.random((N, 8, 16, C)) < np.where(rk == 0, 0.25, np.where(rk == 1, 0.75, 0.5)), 16, axis=3) ^ (rng.random(s.shape, dtype=np.float32) < 0.1)
    o = np.where(rk < 4, 255 * cs, o); last = 255 * (np.arange(16) == 15)
    for c in (0, C - 1):
        o[..., 16 * c:16 * c + 16] = np.where(rk == 0, last, np.where(rk == 1, 255 - last, s[..., 16 * c:16 * c + 16]))
    return pack(o, x, ct, tv)
def setup_inputs_corners(rng):
    ct = np.full((N, 8, 16 * C), -1, np.int64); tv = np.full((N, 8, 16 * T), WB, np.int64); far = np.zeros((N, 8, T), bool)
    pa = [16 * int(rng.integers(G // 16, G // 8)) + rng.permutation(16) for q in range(N)]; plant = []
    for q in range(N):
        for g in range(8):
            k = (g + q) % 8
            if 1 <= k <= 3:
                rf = k if q % 2 else 3 * K1 - C + (0, -1, 1)[k - 1]
                t = rng.permutation(T)[:(rf + 11) // 12]; far[q, g, t] = True; cs = rng.permutation(SC); s = 16 * t[:, None] + np.arange(16)
                ct[q, g, 16 * cs[:len(t)] + rng.integers(0, 16, len(t))] = 16 * t + rng.integers(0, 16, len(t))
                tv[q, g, s[:, :12].reshape(-1)[:rf]] = 16 * cs[:rf] + rng.integers(0, 16, rf)
                tv[q, g, s[:, 12:].reshape(-1)] = 16 * C + rng.permutation(H)[:4 * len(t)]
            elif 4 <= k <= 6:
                t = rng.permutation(T)[:K2 + k - 5]; s = (16 * t[:, None] + np.argsort(rng.random((len(t), 16)), axis=1))
                s = np.concatenate([s[:, 0], rng.permutation(s[:, 1:].reshape(-1))])[:8 * K1]
                p = rng.permutation(16 * K1)[:len(s)]; ct[q, g, p] = s; tv[q, g, s] = p
            elif k == 7:
                room = rng.choice(np.array([0, 1, 2, 3, 15, 16]), T); rk = np.argsort(rng.random((T, 16)), axis=1)
                s = np.flatnonzero((rk < room[:, None]).reshape(-1))[:16 * C]; p = rng.permutation(16 * C)[:len(s)]
                ct[q, g, p] = s; tv[q, g, s] = p
            elif q % 2:
                t = rng.permutation(T)[:6]; z = rng.permutation(16); a = pa[q]; f = 16 * int(rng.integers(G // 8, SC)) + rng.permutation(16)
                e = 16 * int(rng.integers(2 * K1, C)) + rng.permutation(16)[:3]; s = 16 * t[:, None] + np.argsort(rng.random((6, 16)), axis=1)
                ct[q, g, z[:10]] = s[0, :10]; ct[q, g, z[10:]] = s[1, :6]; ct[q, g, a[:10]] = s[1, 6:]; ct[q, g, f] = s[2]; ct[q, g, e] = s[3:, 0]
                s = 16 * t[:, None] + np.argsort(rng.random((6, 16)), axis=1)
                tv[q, g, s[0, :5]] = z[:5]; tv[q, g, s[1, :4]] = f[:4]; tv[q, g, s[2, 0]] = a[0]; tv[q, g, s[3, :4]] = f[4:8]; tv[q, g, s[4, :4]] = 16 * C + pa[q ^ 2][:4]
                plant.append((q, g, t, z, a, f))
            ct[q, g] = ghostly(rng, ct[q, g])
    o, x0 = geo(rng, ct); x0 = np.where(far[:, :, None, :], 255, x0)
    for q, g, t, z, a, f in plant:
        m = 80 * rng.integers(0, 2, 16); w = rng.integers(70, 100, (3, 16)); w[1] += m; w[2] += 80 - m; pose = rng.integers(-60, 61, (3, 16))
        x0[q, g][:, t[:3]] = w.T
        for p, j, c in ((z[:10], 0, 0), (z[10:], 1, 0), (a[:10], 1, 1), (f, 2, 2)):
            o[q, g][:, p] = (w[j] - pose[c])[:, None]
    return pack(o, x0, ct, tv)
def setup_inputs_crowd(rng):
    ct, tv = links(rng, np.full((N, 8, T), 16), 0.6, 0.05)
    for q in range(N):
        for g in range(0, 8, 2):
            c = (16 * rng.permutation(T)[:C, None] + np.argsort(rng.random((C, 16)), axis=1)).reshape(-1)
            tv[q, g] = WB; tv[q, g, c] = np.arange(16 * C)
            m = np.flatnonzero(rng.random(C) < 0.5); p = 16 * m + rng.integers(0, 16, len(m))
            tv[q, g, c[p]] = WB; c[p] = -1; ct[q, g] = ghostly(rng, c)
    o, x0 = geo(rng, ct)
    return pack(o, x0, ct, tv)
def setup_inputs_ties(rng):
    ct, tv = links(rng, rng.choice(np.array([1, 2, 3, 4, 8, 16]), (N, 8, T)), 0.7, 0.05)
    x = whole(rng, 80, 171, N, 8, 16, T); pose = np.repeat(whole(rng, -50, 51, N, 8, 16, C), 16, axis=3)
    nf = rng.choice(np.array([0, 5, 6, 7, 10, 16]), (N, 8, C, 1), p=[0.05, 0.15, 0.25, 0.15, 0.2, 0.2])
    m = np.where(np.argsort(rng.random((N, 8, C, 16)), axis=3) < nf, 4, 5).reshape(N, 8, 1, 16 * C)
    r = np.argsort(rng.random((N, 8, 16 * C, 16), dtype=np.float32), axis=3).transpose(0, 1, 3, 2)
    sg = 2 * whole(rng, 0, 2, N, 8, 16, 16 * C) - 1
    e = np.where(r < m, sg * (EPS + 1), np.where(rng.random(sg.shape, dtype=np.float32) < 0.8, 0, sg * EPS))
    return pack(see(x, ct) - pose + e, x, ct, tv)
def check_inputs(d):
    bad = []
    for k, hi in (("obs", 255), ("x0", 255), ("ct", 16 * (T + H) - 1), ("tv", WB)):
        v = np.asarray(d[k]).astype(np.float64)
        if not np.all((v >= 0) & (v <= hi) & (v == np.floor(v))): bad.append("range of " + k)
    s = np.sort(np.stack([gentries(a) for a in d["ct"]]), axis=-1)
    if np.any(s[..., 1:] == s[..., :-1]): bad.append("entries of ct differ")
    s = np.sort(np.stack([gentries(a) for a in d["tv"]]), axis=-1)
    if np.any((s[..., 1:] == s[..., :-1]) & (s[..., 1:] < WB)): bad.append("entries of tv that are not empty differ")
    return bad
def first(flag, start, k):
    f = np.roll(flag, -start, axis=-1); ix = np.argsort(~f, axis=-1, kind="stable")[..., :k]
    return (ix + start) % flag.shape[-1], np.take_along_axis(f, ix, -1)
def med(v, e):
    n = np.sum(e.reshape(N, 8, -1, 16), axis=3)
    s = np.sort(np.where(e[:, :, None, :], v, np.int16(9999)).reshape(N, 8, 16, -1, 16), axis=4)
    i = np.maximum((n + 1) // 2 - 1, 0)
    return np.take_along_axis(s, i[:, :, None, :, None], 4)[..., 0], n
def reference(obs, x0, ct, tv):
    o = obs.astype(np.int16).reshape(N, 8, 16, 16 * C); x = x0.astype(np.int16).reshape(N, 8, 16, T); xe = np.ones((N, 8, T), bool)
    lk = np.stack([gentries(a) for a in ct]).astype(np.int64); vw = np.stack([gentries(a) for a in tv]).astype(np.int64)
    live = np.ones((N, 8, 16 * C), bool); b = np.zeros((N, 8, 16, 16 * C), np.int16); be = np.zeros((N, 8, 16 * C), bool)
    fc = np.ones((N, 8, C), bool); ft = np.zeros((N, 8, T), bool)
    qi = np.arange(N)[:, None, None]; gi = np.arange(8)[None, :, None]; s16 = np.arange(16)
    for u in range(RO):
        ix, ok = first(fc, u * SC, K1); okp = np.repeat(ok, 16, axis=2)
        pt = (16 * ix[..., None] + s16).reshape(N, 8, 16 * K1); pt4 = pt[:, :, None, :]
        tr = np.take_along_axis(lk, pt, 2) >> 4
        wx = np.concatenate([x, ghosts(x)], axis=3); we = np.concatenate([xe, ghosts(xe)], axis=2)
        op = np.take_along_axis(o, pt4, 3); al = np.take_along_axis(live, pt, 2)
        ex = al & np.take_along_axis(we, tr, 2)
        dif = np.take_along_axis(wx, tr[:, :, None, :], 3) - op
        p, n = med(dif, ex); pp = np.repeat(p, 16, axis=3)
        fit = ex & (np.sum(np.abs(dif - pp) <= EPS, axis=2) >= 12)
        good = np.repeat(np.sum(fit.reshape(N, 8, K1, 16), axis=3) >= 6, 16, axis=2)
        al2 = al & ~(good & ex & ~fit)
        np.put_along_axis(live, pt, np.where(okp, al2, al), 2)
        np.put_along_axis(be, pt, np.where(okp, good & al2, np.take_along_axis(be, pt, 2)), 2)
        np.put_along_axis(b, pt4, np.where(okp[:, :, None, :], np.clip(pp + op, 0, 255), np.take_along_axis(b, pt4, 3)), 3)
        np.put_along_axis(fc, ix, False, 2)
        mk = np.zeros((N, 8, T + H), bool); mk[qi, gi, np.where(okp, tr, T)] = True
        ft = ft | mk[..., :T]
        ix, ok = first(ft, u * ST, K2); okp = np.repeat(ok, 16, axis=2); ix4 = ix[:, :, None, :]
        sl = (16 * ix[..., None] + s16).reshape(N, 8, 16 * K2); v = np.take_along_axis(vw, sl, 2)
        wb = np.concatenate([b, ghosts(b), np.zeros((N, 8, 16, 1), np.int16)], axis=3)
        we = np.concatenate([be, ghosts(be), np.zeros((N, 8, 1), bool)], axis=2)
        ex = np.take_along_axis(we, v, 2); bv = np.take_along_axis(wb, v[:, :, None, :], 3)
        m, n = med(bv, ex); has = n >= 3
        fit = np.sum(np.abs(bv - np.repeat(m, 16, axis=3)) <= EPS, axis=2) >= 12
        rej = okp & np.repeat(has, 16, axis=2) & ex & ~fit
        ox = np.take_along_axis(x, ix4, 3); oe = np.take_along_axis(xe, ix, 2)
        chg = ok & ((has != oe) | (has & oe & np.any(m != ox, axis=2)))
        np.put_along_axis(x, ix4, np.where((ok & has)[:, :, None, :], m, ox), 3)
        np.put_along_axis(xe, ix, np.where(ok, has, oe), 2)
        np.put_along_axis(vw, sl, np.where(rej, WB, v), 2)
        kill = np.zeros((N, 8, WB + 1), bool); kill[qi, gi, np.where(rej, v, WB)] = True
        live = live & ~kill[..., :16 * C]; be = be & ~kill[..., :16 * C]
        np.put_along_axis(ft, ix, False, 2)
        mk = np.zeros((N, 8, WB + 1), bool); mk[qi, gi, np.where(np.repeat(chg, 16, axis=2), v, WB)] = True
        fc = fc | np.any(mk[..., :16 * C].reshape(N, 8, C, 16), axis=3)
    yx = np.where(xe[:, :, None, :], x, 512).reshape(N, 128, T)
    yb = np.where(be[:, :, None, 16 * C - BO:], b[..., 16 * C - BO:], 512).reshape(N, 128, BO)
    yc = np.sum(live.reshape(N, 8, C, 16), axis=3) + 32 * fc
    yt = np.sum((vw < WB).reshape(N, 8, T, 16), axis=3) + 32 * ft
    return {"yx": yx.astype(np.float32).astype(BF), "yb": yb.astype(np.float32).astype(BF), "yc": yc.astype(np.float32), "yt": yt.astype(np.float32)}

@@ -1,0 +1,884 @@
+import numpy as np
+from concourse.bass import DstId, RemoteDMATransfer
+from concourse.mybir import AluOpType as OP, ActivationFunctionType as AF
+
+NC, NT, GH = 448, 896, 128
+F32, BF, I32, U16 = "float32", "bfloat16", "int32", "uint16"
+XG1, XD, XO, XG0, XE = 0, 896, 1152, 2048, 2944
+BG1, BE1, BD, BO, BG0, BE0, BE = 0, 896, 912, 2192, 9360, 10256, 10272
+CD = 80
+W1N, W2N = 14336 + 512, 8064 + 512
+EMPTY = 16128.0
+
+CFG = dict(
+    s1=[[[(0, 112)], [(112, 64)]],
+        [[(176, 96)], [(272, 64), (-1, 16)]],
+        [[(-1, 80)], [(352, 96)]]],
+    s2=[[64, 128, 64], [64, 128, 64], [64, 128, 64]],
+    bad1="dve", bad2="dve", spass="aaa", kd=(14, 15), conv=("da", "dada", "aaaa"), np_sets=2, w1=(6, 13), off=(0, 1), tail=True,
+    exact=True, win=20.0, hold=(10, 3),
+)
+
+SCRATCH = {}
+SHAPE = {}
+
+
+def _decl(name, shape, dt, where="sbuf"):
+    SCRATCH[name] = (where, [128] + list(shape), dt)
+    SHAPE[name] = list(shape)
+
+
+for _n, _s, _d in [
+    ("OB", [7168], BF), ("XW", [XE], BF), ("BW", [BE], BF), ("W1", [W1N], BF), ("W2", [W2N], F32), ("W2b", [3584], BF),
+    ("CTi", [448], I32), ("TVi", [896], I32), ("TRW", [CD + NC], F32), ("EW", [CD + NC], F32), ("DD", [CD + NC], BF),
+    ("TVW", [256 + NT], F32), ("TRu", [NC], U16), ("EOu", [NC], U16), ("tmpB", [NC], F32),
+    ("COL", [128], BF), ("PI", [8], I32), ("PF", [16], F32), ("KX", [8], F32), ("KEY", [16], F32), ("DK", [16], F32),
+    ("K16", [16], F32), ("SUM", [2048], BF), ("BC", [2048], BF), ("PM", [1024], BF), ("NI", [128], BF), ("ONES", [128], BF),
+    ("H17", [512], BF), ("WL", [128], BF), ("NU", [128], BF), ("mt", [128], BF), ("mt2", [128], BF),
+    ("J2", [128], F32), ("J1", [128], F32), ("DM", [256], F32), ("RS", [256], F32), ("ONE", [64], F32), ("DJ", [256], F32),
+    ("IDS", [NT], F32), ("LW", [256 + NT], F32), ("LM", [256], F32), ("LS", [256], F32), ("Li", [CD], I32), ("OT", [16], U16),
+    ("OC", [8], U16), ("PO", [56], U16), ("FT", [56], BF), ("FC", [28], BF), ("FR", [56], BF), ("RK", [56], F32), ("RK2", [56], F32),
+    ("SEL", [56], F32), ("IT", [56], F32), ("CS", [3, 256], BF), ("v", [256], F32), ("w", [256], F32), ("w2", [256], F32), ("vo", [256], U16), ("wo", [256], U16),
+    ("xo", [256], BF), ("DGl", [CD], BF), ("tE", [128], F32), ("SX", [896], BF), ("SB", [896], BF),
+    ("OG", [16 * CD], BF), ("BT", [16 * CD], BF), ("PP", [CD], U16), ("OP_", [CD], U16), ("TD", [CD], U16), ("ED", [CD], U16),
+    ("tD", [CD], F32), ("tD2", [CD], F32), ("DG", [CD], BF), ("DN", [CD], BF), ("SS", [2048], F32), ("EQ", [NC], BF), ("KL", [NC], BF),
+    ("Ra", [128, 10], BF), ("Rb", [128, 10], BF), ("Fa", [1152], BF), ("Fb", [1152], BF),
+]:
+    _decl(_n, _s, _d)
+for _s in "01":
+    for _n, _sh, _d in [("G", [2048], BF), ("RR", [2048], BF), ("AB", [2048], BF), ("S0a", [512], BF), ("S0b", [512], BF),
+                        ("FO", [1152], BF), ("un", [128], BF), ("FF", [128], BF), ("ft", [128], BF), ("gd", [128], BF),
+                        ("MM", [128], BF), ("nF", [128], BF), ("ym", [128], BF)]:
+        _decl(_n + _s, _sh, _d)
+    for _c in "ab":
+        _decl("Z" + _s + _c, [128, 4], BF)
+        _decl("Q" + _s + _c, [128, 6], BF)
+NPB = 2 * CFG["np_sets"]
+for _i in range(NPB):
+    _decl("P%d" % _i, [128, 4], F32, "psum")
+for _i in range(8 - NPB):
+    _decl("K%d" % _i, [512], F32, "psum")
+DTYPE = {k: v[2] for k, v in SCRATCH.items()}
+IOS = {"obs": [7168], "x0": [896], "ct": [448], "tv": [896], "yx": [896], "yb": [1792], "yc": [448], "yt": [896]}
+SHAPE.update(IOS)
+NDMA = 20
+SEMAPHORES = ["pe", "dve", "act", "gp"] + ["d%d" % i for i in range(NDMA)] + ["snt%d" % i for i in range(6)] + ["arr%d" % i for i in range(6)]
+
+
+def sl(a, n, s=1):
+    return slice(a, a + (n - 1) * s + 1, s)
+
+
+def A(name, *idx, p=None):
+    return ("ap", name, p, idx)
+
+
+def IND(win, off):
+    return ("ind", win, off)
+
+
+def shp(name):
+    return SHAPE[name] if name in SHAPE else ([128, 4] if name[0] == "p" else [512])
+
+
+def region(ap):
+    s = shp(ap[1]); idx = list(ap[3]) + [slice(None)] * (len(s) - len(ap[3]))
+    lo = hi = 0; n = 1; st = 1
+    for d in range(len(s) - 1, -1, -1):
+        i = idx[d]
+        r = range(*i.indices(s[d])) if isinstance(i, slice) else range(i, i + 1)
+        lo += r[0] * st; hi += r[-1] * st; n *= len(r); st *= s[d]
+    return ap[1], lo, hi + 1, n
+
+
+def bits(ap):
+    name, lo, hi, n = region(ap)
+    if n == hi - lo or not CFG["exact"]:
+        return ((1 << (hi - lo)) - 1) << lo
+    z = np.zeros(shp(name), np.uint8); z[tuple(ap[3])] = 1
+    return int.from_bytes(np.packbits(z.reshape(-1), bitorder="little").tobytes(), "little")
+
+
+def isap(x):
+    return isinstance(x, tuple) and len(x) > 0 and x[0] in ("ap", "ind")
+
+
+def psum(ap):
+    return ap[0] == "ap" and ap[1] not in SHAPE
+
+
+def two(ap):
+    return DTYPE.get(ap[1], F32) in (BF, U16)
+
+
+CYC, PEC, GAT, SCA = 1.0, 0.5, 1.56, 3.8
+
+
+def build():
+    ops = []; recs = {}; cnt = {"t": 0, "d": 0, "tag": "i"}
+
+    def tile(kind="k"):
+        cnt["t"] += 1
+        return "%s%d_" % (kind, cnt["t"])
+
+    def touch(i, ap, wr, deps):
+        name, lo, hi, n = region(ap)
+        if name in IOS:
+            return
+        L = recs.setdefault(name, []); keep = []
+        ps = name not in SHAPE; mk = bits(ap)
+        for r in L:
+            j, w, a = r
+            if j != i:
+                if a & mk and (w or wr):
+                    deps[j] = deps.get(j, False) or (w and not wr)
+                elif ps and ops[j]["e"] != ops[i]["e"]:
+                    deps[j] = deps.get(j, False)
+                if wr and not ps:
+                    a &= ~mk
+            if a:
+                keep.append((j, w, a))
+        keep.append((i, wr, mk)); recs[name] = keep
+
+    def op(e, calls, lat=0.0, sem=None):
+        i = len(ops); o = dict(e=e, calls=calls, deps={}, lat=lat, sem=sem, tiles=[]); ops.append(o)
+        cost = 0.0
+        for c in calls:
+            k = c[0]; out = c[1]; ins = [x for x in c[2:] if isap(x)]
+            if k == "mm" and not c[4]:
+                ins = ins + [out]
+            for x in ins:
+                for y in ((x[1], x[2]) if x[0] == "ind" else (x,)):
+                    touch(i, y, False, o["deps"])
+            if out[0] == "ind":
+                touch(i, out[2], False, o["deps"]); touch(i, out[1], False, o["deps"]); touch(i, out[1], True, o["deps"])
+            elif k != "send":
+                touch(i, out, True, o["deps"])
+            else:
+                touch(i, out, False, o["deps"])
+            for x in [out] + ins:
+                if psum(x) and x[1] not in o["tiles"]:
+                    o["tiles"].append(x[1])
+            sc = out[0] == "ind"; ga = any(x[0] == "ind" for x in ins)
+            n = 16 * region(out[2])[3] if sc else region(out)[3]
+            if k == "mm":
+                cost += max(64, n) * PEC
+            elif k in ("dma", "send", "recv"):
+                cost += {"dma": 1000 if e == "gp" else 60, "send": 1200, "recv": 0}[k]
+            elif e == "gp":
+                cost += 150 + 2 * n * CYC
+            else:
+                f = 1.0
+                if sc:
+                    f = SCA
+                elif ga:
+                    f = GAT
+                elif k == "tt":
+                    f = 1.0 if psum(ins[0]) or psum(ins[1]) else 2.0
+                elif e == "dve" and all(two(x) for x in [out] + ins if region(x)[3] > 1):
+                    f = 0.5
+                cost += 50 + max(64, n * f) * CYC
+        o["cost"] = cost
+        w_ = calls[0][1]
+        o["tag"] = "%s%s%s" % (cnt["tag"], e[0], (w_[1][1] + "s" if w_[0] == "ind" else w_[1][0] if psum(w_) else w_[1])[:3])
+        return i
+
+    def ts(out, a, s1, o0, s2=None, o1=None):
+        return op("dve", [("ts", out, a, s1, s2, o0, o1)])
+
+    def tt(out, a, b, o):
+        return op("dve", [("tt", out, a, b, o)])
+
+    def cp(out, a):
+        return op("dve", [("cp", out, a)])
+
+    def ms(out, v):
+        return op("dve", [("ms", out, float(v))])
+
+    def act(out, a, f, bias=0.0, scale=1.0):
+        return op("act", [("act", out, a, f, bias, scale)])
+
+    def iota(out, pat, base, cm):
+        return op("gp", [("iota", out, pat, base, cm)])
+
+    def mm(groups):
+        c = []
+        for g_ in groups:
+            out, terms = g_[0], g_[1]
+            for j, (l, r) in enumerate(terms):
+                c.append(("mm", out, l, r, j == 0 and "<" in (g_ + ("<>",))[2], j == len(terms) - 1 and ">" in (g_ + ("<>",))[2]))
+        return op("pe", c)
+
+    def dma(out, a, q="sp", lat=2500.0):
+        cnt["d"] += 1
+        return op(q, [("dma", out, a)], lat=lat, sem=("d%d" % (cnt["d"] - 1), 16))
+
+    def SUMk(k):
+        return A("SUM", sl(128 * k, 128))
+
+    def BCk(k):
+        return A("BC", sl(128 * k, 128))
+    ID, NI, ONES = A("PM", sl(0, 128)), A("NI"), A("ONES")
+
+    def exchange(x, src, off, buf, dst):
+        for b0, nb in ((0, 4), (4, 3)):
+            t = tile()
+            mm([(A(t, sl(128 * j, 128)), [(A("PM", sl(128 * (b0 + j + 1), 128)), A(src, sl(off + 128 * (b0 + j), 128)))]) for j in range(nb)])
+            act(A(buf, sl(128 * b0, 128 * nb)), A(t, sl(0, 128 * nb)), AF.Identity)
+        s = op("gp", [("send", A(buf), x, src, dst)], lat=6000.0, sem=("snt%d" % x, 0))
+        r = op("arr", [("recv", A(src, sl(dst, 896)))], lat=500.0, sem=("arr%d" % x, 0))
+        ops[r]["deps"][s] = False
+        return s
+
+    dma(A("XW", sl(XO, NT)), A("x0"))
+    dma(A("CTi"), A("ct"))
+    dma(A("OB", sl(0, 2816)), A("obs", sl(0, 2816)), lat=3500.0)
+    dma(A("TVi"), A("tv"))
+    dma(A("OB", sl(2816, 4352)), A("obs", sl(2816, 4352)), lat=6000.0)
+    iota(A("PI", sl(0, 1)), [[0, 1]], 0, 1)
+    iota(A("COL"), [[1, 128]], 0, 0)
+    iota(A("K16"), [[1, 16]], 0, 0)
+    p_ = A("PI", sl(0, 1))
+    cp(A("KX", sl(0, 1)), p_)
+    for b in range(3):
+        ts(A("PI", sl(1 + b, 1)), p_, 4 + b, OP.arith_shift_right, 1, OP.bitwise_and)
+        ts(A("PF", sl(b, 1)), A("PI", sl(1 + b, 1)), float(-32 << b), OP.mult, float(16 << b), OP.add)
+        ts(A("KX", sl(1 << b, 1 << b)), A("KX", sl(0, 1 << b)), A("PF", sl(b, 1)), OP.add)
+    for d in range(8):
+        ts(A("PM", sl(128 * d, 128)), A("COL"), A("KX", sl(d, 1)), OP.is_equal)
+    exchange(0, "XW", XO, "SX", XG0)
+    ts(A("PI", sl(4, 1)), p_, 15, OP.bitwise_and)
+    PK, PG = A("PF", sl(4, 1)), A("PF", sl(5, 1))
+    cp(PK, A("PI", sl(4, 1)))
+    ts(PG, A("KX", sl(0, 1)), PK, OP.subtract)
+    ts(A("KEY"), A("K16"), PG, OP.add)
+    ts(A("DK"), A("K16"), PK, OP.is_equal)
+    ts(A("NI"), ID, -1.0, OP.mult)
+    ts(A("mt"), A("COL"), PG, OP.is_ge)
+    ts(A("mt2"), A("COL"), A("KEY", sl(15, 1)), OP.is_le)
+    tt(ONES, A("mt"), A("mt2"), OP.mult)
+    for k in range(16):
+        ts(SUMk(k), A("COL"), A("KEY", sl(k, 1)), OP.is_equal)
+        act(BCk(k), ONES, AF.Copy, scale=A("DK", sl(k, 1)))
+    p32 = A("KX", sl(0, 1))
+    ts(A("mt"), A("COL"), p32, OP.is_le, -1.0, OP.mult)
+    tt(A("NU"), A("mt"), ONES, OP.mult)
+    ts(A("mt2"), A("COL"), p32, OP.is_gt, 1.0, OP.mult)
+    ts(A("mt"), A("COL"), p32, OP.is_lt, -1.0, OP.mult)
+    tt(A("mt"), A("mt"), A("mt2"), OP.add)
+    tt(A("mt"), A("mt"), ONES, OP.mult)
+    ts(A("mt2"), ID, 63.0, OP.mult)
+    tt(A("WL"), A("mt2"), A("mt"), OP.subtract)
+    act(A("H17", sl(256, 128)), ID, AF.Copy, scale=17.0)
+    act(A("H17", sl(384, 128)), ID, AF.Copy, scale=-17.0)
+    tt(A("H17", sl(0, 128)), ONES, A("H17", sl(256, 128)), OP.add)
+    tt(A("H17", sl(128, 128)), ONES, A("H17", sl(384, 128)), OP.add)
+    iota(A("J2"), [[0, 4], [16, 32]], 8064, 0)
+    ts(A("J2"), A("J2"), PK, OP.add)
+    ts(A("J1"), A("J2"), float(14336 - 8064), OP.add)
+    iota(A("DJ"), [[1, 256]], 0, 0)
+    iota(A("RS"), [[0, 16], [1, 16]], 0, 0)
+    ts(A("DM"), A("RS"), PK, OP.is_equal)
+    ts(A("RS"), A("RS"), 0.5, OP.is_gt)
+    iota(A("IT"), [[16, 56]], 256, 0)
+    ts(A("IT"), A("IT"), PK, OP.add)
+    ms(A("ONE"), 1)
+    for u in range(3):
+        ms(A("CS", u), 32 ** u)
+    ms(A("Fa", sl(0, 128, 9)), -30000)
+    for h in range(16):
+        if h < CFG["w1"][0]:
+            ms(A("W1", sl(896 * h, 896)), 0)
+        elif h < CFG["w1"][1]:
+            act(A("W1", sl(896 * h, 896)), A("XW", sl(XO, NT)), AF.Copy, scale=0.0)
+        else:
+            iota(A("W1", sl(896 * h, 896)), [[0, 896]], 0, 0)
+    ms(A("W1", sl(14336, 512)), 0)
+    ms(A("FT"), 0); ms(A("FC"), 1); ms(A("DD"), 0)
+    ms(A("XW", sl(XD, 256)), 512); ms(A("TVW", sl(0, 256)), EMPTY)
+    ms(A("TRW", sl(0, CD)), 0); ms(A("EW", sl(0, CD)), 60000)
+    iota(A("BW", sl(BE1, 16 + 1280)), [[0, 1296]], 512, 0); ms(A("BW", sl(BE0, 16)), 512)
+    iota(A("LW"), [[0, 256 + NT]], 0, 0)
+    for h in range(4):
+        iota(A("BW", sl(BO + 2816 + 1088 * h, 1088)), [[0, 1088]], 512, 0)
+    for h in range(8):
+        iota(A("W2", sl(1072 * h, 1072)), [[0, 1072]], 0, 0)
+    ts(A("SS", sl(0, NT)), A("TVi"), 8063.5, OP.is_gt, 8064.0, OP.mult)
+    tt(A("TVW", sl(256, NT)), A("TVi"), A("SS", sl(0, NT)), OP.add)
+    ts(A("tmpB"), A("CTi"), 14335.5, OP.is_gt, 60000.0, OP.mult)
+    tt(A("EW", sl(CD, NC)), A("CTi"), A("tmpB"), OP.max)
+    ts(A("CTi"), A("CTi"), 4, OP.arith_shift_right)
+    cp(A("TRu", sl(0, 176)), A("CTi", sl(0, 176)))
+    cp(A("TRu", sl(352, 96)), A("CTi", sl(352, 96)))
+    cp(A("TRW", sl(CD, NC)), A("CTi"))
+
+    def odd_tr(out, src, t, n):
+        ts(t, src, 895.5, OP.is_gt, -2048.0, OP.mult)
+        tt(t, t, src, OP.add)
+        ts(out, t, 1152.0, OP.add)
+    odd_tr(A("TRu", sl(176, 160)), A("TRW", sl(CD + 176, 160)), A("tmpB", sl(0, 160)), 160)
+
+    def flag_static(u, c0, n):
+        for a in range(c0, c0 + n, 128):
+            m = min(128, c0 + n - a)
+            tt(A("tE", sl(0, m)), A("EW", sl(CD + a, m)), A("J1", sl(0, m)), OP.min)
+            cp(A("EOu", sl(a, m)), A("tE", sl(0, m)))
+        return [cp(IND(A("W1"), A("EOu", sl(a, 16))), A("CS", u)) for a in range(c0, c0 + n, 16)]
+
+    def worklist(F, cols, K, idbase, otile):
+        n = len(cols); runs = []
+        for j, c in enumerate(cols):
+            if runs and runs[-1][1] + runs[-1][2] == c:
+                runs[-1][2] += 1
+            else:
+                runs.append([j, c, 1])
+        for j, c, m in runs:
+            cp(A("FR", sl(j, m)), A(F, sl(c, m)))
+            iota(A("IDS", sl(16 * j, 16 * m)), [[1, 16 * m]], idbase + 16 * c, 0)
+        act(A("LW", sl(0, K)), A("DJ", sl(0, K)), AF.Identity)
+        fr = A("FR", sl(0, n)); t = tile()
+        mm([(A(t, sl(0, n)), [(ONES, fr)]), (A(t, sl(64, n)), [(A("NU"), fr)])])
+        rk, rk2, se = A("RK", sl(0, n)), A("RK2", sl(0, n)), A("SEL", sl(0, n))
+        op("dve", [("scan", rk, A("ONE", sl(0, n)), A(t, sl(0, n)), 0.0, OP.mult, OP.add)])
+        tt(rk, A(t, sl(64, n)), rk, OP.add)
+        ts(se, rk, K - 0.5, OP.is_lt)
+        tt(se, se, fr, OP.mult)
+        tt(rk2, rk, A("IT", sl(0, n)), OP.subtract)
+        tt(rk2, rk2, se, OP.mult)
+        tt(rk2, rk2, A("IT", sl(0, n)), OP.add)
+        cp(A("PO", sl(0, n)), rk2)
+        for a in range(0, n, 14):
+            m = min(14, n - a)
+            act(IND(A("LW"), A("PO", sl(a, m))), A("IDS", sl(16 * a, 16 * m)), AF.Silu)
+        tt(A("LM", sl(0, K)), A("LW", sl(0, K)), A("DM", sl(0, K)), OP.mult)
+        op("dve", [("scan", A("LS", sl(0, K)), A("RS", sl(0, K)), A("LM", sl(0, K)), 0.0, OP.mult, OP.add)])
+        cp(A("Li", sl(0, K // 16)), A("LS", sl(15, K // 16, 16)))
+        cp(A(otile, sl(0, K // 16)), A("Li", sl(0, K // 16)))
+        for j, c, m in runs:
+            tt(A(F, sl(c, m)), A("FR", sl(j, m)), A("SEL", sl(j, m)), OP.subtract)
+
+    def median(n, s, terms, flip=False, off=0, neg=None):
+        N_ = slice(0, n); P = {}
+        Qn = "Q" + s; Zn = "Z" + s
+        if cnt.get("flip") != flip:
+            cnt["flip"] = flip
+            ms(A("Fb", sl(0, 128, 9)), 30000 if flip else -30000)
+        for h, c in enumerate("ab" if off else ""):
+            up = (c == "b") == flip
+
+            def layer(xs, ys, buf):
+                t = tile()
+                mm([(A(t, sl(j, n, 4)), xs[j] + neg(ys[j])) for j in range(4)])
+                act(A(buf, N_) if buf[0] == "Z" else A(buf, sl(0, 4 * n)), A(t, sl(0, 4 * n)), AF.Relu)
+                d = [A(buf, N_, j) if buf[0] == "Z" else A(buf, sl(j, n, 4)) for j in range(4)]
+                mn = [xs[j] + [(NI, d[j])] for j in range(4)]; mx = [ys[j] + [(ID, d[j])] for j in range(4)]
+                return (mx, mn) if up else (mn, mx)
+            lo, hi = layer([terms(8 * h + j) for j in range(4)], [terms(8 * h + 4 + j) for j in range(4)], "S0" + c + s)
+            pw, sw = [lo[0], hi[1], lo[2], hi[3]], [lo[1], hi[0], lo[3], hi[2]]
+            if off == 2:
+                lo, hi = layer(pw, sw, Zn + c)
+                pw, sw = [lo[0], lo[1], hi[2], hi[3]], [hi[0], hi[1], lo[2], lo[3]]
+            t = tile()
+            mm([(A(t, sl(j, n, 4)), sw[j]) for j in range(4)])
+            if off == 1:
+                act(A(Zn + c, N_), A(t, sl(0, 4 * n)), AF.Identity)
+            else:
+                op("act", [("act", A(Qn + c, N_, (0, 4, 1, 5)[j]), A(t, sl(j, n, 4)), AF.Identity, 0.0, 1.0) for j in range(4)])
+            P[c] = tile("p")
+            mm([(A(P[c], N_, j), pw[j]) for j in range(4)])
+        for h, c in enumerate("" if off else "ab"):
+            P[c] = tile("p")
+            mm([(A(P[c], N_, j), terms(8 * h + j)) for j in range(4)])
+            t = tile()
+            mm([(A(t, sl(j, n, 4)), terms(8 * h + 4 + j)) for j in range(4)])
+            act(A("S0" + c + s, sl(0, 4 * n)), A(t, sl(0, 4 * n)), AF.Identity)
+        seq = {}
+        for c in "ab":
+            lo, hi = (OP.min, OP.max) if (c == "b") != flip else (OP.max, OP.min)
+            p = lambda a, b=None, st=1, c=c: A(P[c], N_, a if b is None else slice(a, b, st))
+            q = lambda a, b=None, st=1, c=c: A(Qn + c, N_, a if b is None else slice(a, b, st))
+            r = lambda a, b=None, st=1, c=c: A("R" + c, N_, a if b is None else slice(a, b, st))
+            f = lambda a, c=c: A("F" + c, sl(a, n, 9))
+            s0 = lambda a, c=c: A("S0" + c + s, sl(a, 2 * n, 2))
+            z = lambda a, b, st=1, c=c: A(Zn + c, N_, slice(a, b, st))
+            seq[c] = [
+                (z(1, 4, 2), p(0, 4, 2), s0(0), hi), (z(0, 4, 2), p(1, 4, 2), s0(1), lo), (p(0, 4, 2), p(0, 4, 2), s0(0), lo), (p(1, 4, 2), p(1, 4, 2), s0(1), hi),
+                (q(0, 5, 4), p(0, 2), z(0, 2), hi), (q(1, 6, 4), p(2, 4), z(2, 4), lo), (p(0, 2), p(0, 2), z(0, 2), lo), (p(2, 4), p(2, 4), z(2, 4), hi),
+                (q(3), p(1), q(0), hi), (q(2), p(2), q(5), lo), (p(1), p(1), q(0), lo), (p(2), p(2), q(5), hi),
+                (r(0, 7, 3), p(0, 3), q(1, 4), hi), (f(8), p(3), q(4), hi), (f(1), p(0), q(1), lo), (p(1, 4), p(1, 4), q(2, 5), lo),
+                (r(4, 6), p(2, 4), r(0, 4, 3), lo), (p(2, 4), p(2, 4), r(0, 4, 3), hi),
+                (f(2), p(1), r(4), lo), (f(4), p(2), r(5), lo), (f(6), p(3), r(6), lo),
+                (f(3), p(1), r(4), hi), (f(5), p(2), r(5), hi), (f(7), p(3), r(6), hi)]
+        for x, y in zip(seq["a"][4 * off:], seq["b"][4 * off:]):
+            tt(*x); tt(*y)
+        n9 = sl(0, 9 * n)
+        if flip:
+            op("dve", [("scan", A("FO" + s, n9), A("Fa", n9), A("Fb", n9), 30000.0, OP.min, OP.max)])
+        else:
+            op("dve", [("scan", A("FO" + s, n9), A("Fa", n9), A("Fb", n9), -30000.0, OP.max, OP.min)])
+        return A("FO" + s, sl(8, n, 9))
+
+    def staged(n, terms, fn):
+        per = min(16, 512 // n)
+        for k0 in range(0, 16, per):
+            m = min(per, 16 - k0); t = tile()
+            mm([(A(t, sl(j * n, n)), terms(k0 + j)) for j in range(m)])
+            fn(t, k0, m)
+
+    def badpass(eng, s, n):
+        for h in range(2):
+            a = A("AB" + s, sl(8 * n * h, 8 * n))
+            if eng == "dve":
+                ts(a, a, 8.5, OP.is_gt)
+            else:
+                act(a, a, AF.Sign, bias=-8.5)
+        return 4.5 if eng == "dve" else -7.0
+
+    nchunk = [0]
+
+    def step1(u, segs):
+        s = str(nchunk[0] % 2); nchunk[0] += 1; cnt["tag"] = "c%d" % nchunk[0]
+        n = sum(m for _, m in segs); N_ = sl(0, n); G = "G" + s
+        win = A("XW", sl(XO, 1792)) if u != 1 else A("XW", sl(0, 2048))
+        pos = []; j = 0
+        for c0, m in segs:
+            pos.append((c0, m, j)); j += m
+        dyn = [x for x in pos if x[0] < 0]
+        for c0, m, j in pos:
+            act(A(G, sl(16 * j, 16 * m)), IND(win, A("TRu", sl(c0, m)) if c0 >= 0 else A("TD", sl(0, m))), AF.Identity)
+        if len(segs) > 1:
+            for c0, m, j in pos:
+                if c0 >= 0:
+                    act(A("OG", sl(16 * j, 16 * m)), A("OB", sl(16 * c0, 16 * m)), AF.Identity)
+        for c0, m, j in dyn:
+            act(A("OG", sl(16 * j, 16 * m)), IND(A("OB"), A("OP_", sl(0, m))), AF.Identity)
+        ob, o0 = ("OG", 0) if dyn else ("OB", 16 * segs[0][0])
+        gk = lambda k: A(G, sl(k, n, 16))
+        ok = lambda k: A(ob, sl(o0 + k, n, 16))
+        un, FF, ft, gd, MM = (A(x + s, N_) for x in ("un", "FF", "ft", "gd", "MM"))
+        dg = A("DG" if len(segs) > 1 else "DGl", N_)
+        if dyn:
+            if len(segs) > 1:
+                ms(dg, 0)
+                for c0, m, j in dyn:
+                    cp(A("DG", sl(j, m)), A("DGl", sl(0, m)))
+        if u > 0:
+            t = tile()
+            mm([(A(t, N_), [(SUMk(k), gk(k)) for k in range(16)] + ([(ID, dg)] if dyn else []))])
+            ts(un, A(t, N_), 4095.0, OP.is_gt, 64.0, OP.mult)
+            t = tile()
+            mm([(A(t, N_), [(A("WL"), un)])])
+            ts(FF, A(t, N_), 63.5 * 64, OP.is_gt, -16384.0, OP.mult)
+            if dyn:
+                tt(FF, FF, dg, OP.add)
+        P = median(n, s, lambda k: [(ID, gk(k)), (NI, ok(k))] + ([(BCk(k), FF)] if u > 0 else []))
+
+        def after(t, k0, m):
+            act(A("RR" + s, sl(k0 * n, m * n)), A(t, sl(0, m * n)), AF.Relu, bias=255.0, scale=-1.0)
+        staged(n, lambda k: [(ID, P), (ID, ok(k)), (NI, gk(k))], lambda t, k0, m: act(A("AB" + s, sl(k0 * n, m * n)), A(t, sl(0, m * n)), AF.Abs))
+        staged(n, lambda k: [(ID, P), (ID, ok(k))], after)
+        th = badpass(CFG["bad1"], s, n)
+        t = tile()
+        mm([(A(t, N_), [(SUMk(k), A("AB" + s, sl(k * n, n))) for k in range(16)] + ([(ID, un)] if u > 0 else []))])
+        ts(ft, A(t, N_), th, OP.is_lt, 64.0, OP.mult)
+        t = tile(); H = lambda j: A("H17", sl(128 * j, 128))
+        e1 = [(H(3), un)] if u > 0 else []; e2 = [(H(2), un)] if u > 0 else []
+        mm([(A(t, N_), [(H(0), ft)] + e2 + ([(NI, dg)] if dyn else [])), (A(t, sl(128, n)), [(H(1), ft)] + e1)])
+        ts(MM, A(t, N_), 22.5 * 64, OP.is_lt, 32768.0, OP.mult)
+        for c0, m, j in pos:
+            if c0 >= 0 and u == 0:
+                ts(A("DD", sl(CD + c0, m)), A(t, sl(128 + j, m)), 5.5 * 64, OP.is_gt, 8192.0, OP.mult)
+            elif c0 >= 0:
+                ts(A("FF" + s, sl(0, m)), A(t, sl(128 + j, m)), 5.5 * 64, OP.is_gt, 8192.0, OP.mult)
+                cp(A("DD", sl(CD + c0, m)), A("FF" + s, sl(0, m)))
+            else:
+                ts(A("DN", sl(0, m)), A(t, sl(128 + j, m)), 5.5 * 64, OP.is_gt, 8192.0, OP.mult)
+                tt(A("DN", sl(0, m)), A("DN", sl(0, m)), A("DGl", sl(0, m)), OP.max)
+                cp(IND(A("DD"), A("OC", sl(0, m // 16))), A("DN", sl(0, m)))
+
+        for c0, m, j in pos:
+            for a in range(0, m, 32):
+                z = min(32, m - a); t = tile()
+                mm([(A(t, sl(k, z, 16)), [(NI, A("RR" + s, sl(k * n + j + a, z))), (BCk(k), A("MM" + s, sl(j + a, z)))]) for k in range(16)])
+                act(A("BW", sl(BO + 16 * (c0 + a), 16 * z)) if c0 >= 0 else A("BT", sl(16 * a, 16 * z)), A(t, sl(0, 16 * z)), AF.Relu, bias=255.0)
+                if c0 < 0:
+                    cp(IND(A("BW", sl(BD, BG0 - BD)), A("PP", sl(a, z))), A("BT", sl(16 * a, 16 * z)))
+
+    def camlist(u):
+        K = 16 if u == 1 else CD
+        worklist("FC", [10, 21] if u == 1 else [20, 21] + list(range(20)), K, CD, "OC")
+        ms(A("FC", sl(11, 10)) if u == 1 else A("FC", sl(22, 6)), 0)
+        k_ = sl(0, K); oc = A("OC", sl(0, K // 16))
+        cp(A("DGl", k_), IND(A("DD"), oc))
+        cp(A("Li", k_), A("LW", k_))
+        ts(A("tD", k_), A("Li", k_), 16.0, OP.mult, PK, OP.add)
+        cp(A("PP", k_), A("tD", k_))
+        ts(A("OP_", k_), A("tD", k_), -1280.0, OP.add, 0.0, OP.max)
+        if u == 1:
+            cp(A("tD", k_), IND(A("TRW"), oc))
+            odd_tr(A("TD", k_), A("tD", k_), A("tD2", k_), K)
+        else:
+            cp(A("TD", k_), IND(A("TRW"), oc))
+        tt(A("tD2", k_), IND(A("EW"), oc), A("J1", k_), OP.min)
+        cp(A("ED", k_), A("tD2", k_))
+        for a in range(0, K, 16):
+            cp(IND(A("W1"), A("ED", sl(a, 16))), A("CS", u))
+
+    def tracklist(u):
+        t = tile()
+        for r in range(0, 16, 2):
+            mm([(A(t, sl(0, 56)), [(SUMk(r + q), A("W1", sl(16 * (r + q) + s_, 56, 256))) for q in range(2) for s_ in range(16)],
+                 "<" if r == 0 else ">" if r == 14 else "")])
+        ts(A("FR"), A(t, sl(0, 56)), 16.0 * 32 ** u - 0.5, OP.is_gt)
+        tt(A("FT"), A("FT"), A("FR"), OP.max)
+        worklist("FT", [(12 * u + j) % 56 for j in range(56)], 256, 256, "OT")
+
+    xw = A("XW", sl(XD, XG0 - XD))
+
+    def views(u):
+        v, w, w2 = A("v"), A("w"), A("w2")
+        act(v, IND(A("TVW"), A("OT")), AF.Identity)
+        if u != 1:
+            ts(A("vo"), v, 8064.0, OP.min)
+        else:
+            ts(w, v, 7167.5, OP.is_gt, -9360.0, OP.mult)
+            ts(w2, v, 8064.0, OP.min, 2192.0, OP.add)
+            tt(w, w, w2, OP.add)
+            cp(A("vo"), w)
+        for h in range(2):
+            tt(A("w2", sl(128 * h, 128)), A("v", sl(128 * h, 128)), A("J2"), OP.min)
+        cp(A("wo"), w2)
+        act(A("xo"), IND(xw, A("OT")), AF.Identity)
+
+    def step2(u, j0, n, ondve):
+        s = str(nchunk[0] % 2); nchunk[0] += 1; cnt["tag"] = "c%d" % nchunk[0]
+        N_ = sl(0, n); G = "G" + s; ot = A("OT", sl(j0 // 16, n // 16))
+        un, FF, xn, nh, ne = (A(x + s, N_) for x in ("un", "FF", "ft", "gd", "MM"))
+        w, w2, xo = (A(x, sl(j0, n)) for x in ("w", "w2", "xo"))
+        win = A("BW", sl(BO, BE - BO)) if u != 1 else A("BW", sl(0, BG0))
+        for h in range(0, n, 64):
+            m = min(64, n - h)
+            act(A(G, sl(16 * h, 16 * m)), IND(win, A("vo", sl(j0 + h, m))), AF.Relu, bias=256.0, scale=-1.0)
+        gk = lambda k: A(G, sl(k, n, 16))
+        t = tile()
+        mm([(A(t, N_), [(SUMk(k), gk(k)) for k in range(16)])])
+        ts(un, A(t, N_), 0.5, OP.is_lt, 64.0, OP.mult)
+        t = tile(); off = CFG["off"][j0 > 0]; nF, ym = A("nF" + s, N_), A("ym" + s, N_)
+        mm([(A(t, N_), [(A("WL"), un)]), (A(t, sl(128, n)), [(ONES, un)])])
+        ts(FF, A(t, N_), 63.5 * 64, OP.is_gt, 256.0, OP.mult)
+        if off:
+            act(nF, FF, AF.Copy, scale=-1.0)
+        ts(nh, A(t, sl(128, n)), 13.5 * 64, OP.is_gt, 512.0, OP.mult)
+
+        def neg(ts_):
+            return [(NI, r) if l is ID else (ID, r) if l is NI else (l, nF if r is FF else FF) for l, r in ts_]
+        m_ = median(n, s, lambda k: [(ID, gk(k)), (BCk(k), FF)], True, off, neg)
+        ts(ym, m_, -1.0, OP.mult, 256.0, OP.add)
+        tt(xn, ym, nh, OP.max)
+        cnt["xn"] = cp(IND(xw, ot), xn)
+        tt(ne, xn, xo, OP.not_equal)
+        staged(n, lambda k: [(ID, gk(k)), (NI, m_)], lambda t, k0, m: act(A("AB" + s, sl(k0 * n, m * n)), A(t, sl(0, m * n)), AF.Abs))
+        th = badpass(CFG["bad2"], s, n)
+        t = tile()
+        mm([(A(t, N_), [(SUMk(k), A("AB" + s, sl(k * n, n))) for k in range(16)] + [(NI, un), (NI, nh)]), (A(t, sl(128, n)), [(ONES, ne)])])
+        ts(w, A(t, N_), th, OP.is_gt, EMPTY, OP.mult)
+        ts(w2, A(t, sl(128, n)), 0.5, OP.is_gt, 64.0 * (u + 1), OP.mult)
+        if ondve:
+            tt(ne, w2, w, OP.add)
+            for k0 in range(0, 16, 8):
+                op("dve", [("ts", A("RR" + s, sl(k, n, 16)), ne, A("DK", sl(k, 1)), None, OP.mult, None) for k in range(k0, k0 + 8)])
+            for h in range(0, n, 32):
+                cp(IND(A("W1", sl(0, W2N)), A("wo", sl(j0 + h, 32))), A("RR" + s, sl(16 * h, 512)))
+            return
+        tt(w2, w2, w, OP.add)
+        for k0 in range(0, 16, 4):
+            if CFG["spass"][0 if j0 == 0 else 2 if j0 + n == 256 else 1] == "a":
+                op("act", [("act", A("SS", sl(k, n, 16)), w2, AF.Copy, 0.0, A("DK", sl(k, 1))) for k in range(k0, k0 + 4)])
+            else:
+                op("dve", [("ts", A("SS", sl(k, n, 16)), w2, A("DK", sl(k, 1)), None, OP.mult, None) for k in range(k0, k0 + 4)])
+        for h in range(0, n, 16):
+            if (j0 + h) // 16 in CFG["kd"]:
+                cp(IND(A("W2"), A("wo", sl(j0 + h, 16))), A("SS", sl(16 * h, 256)))
+            else:
+                act(IND(A("W2"), A("wo", sl(j0 + h, 16))), A("SS", sl(16 * h, 256)), AF.Silu)
+
+    def decode(u):
+        nc = (176, 352, 448)[u]
+        for c0 in range(0, nc, 112):
+            m = min(112, nc - c0); C_ = sl(c0, m)
+            wb = 1792 * (c0 // 112 % 2)
+            if CFG["conv"][u][c0 // 112] == "a":
+                act(A("W2b", sl(wb, 16 * m)), A("W2", sl(16 * c0, 16 * m)), AF.Identity)
+            elif CFG["conv"][u][c0 // 112] == "d":
+                cp(A("W2b", sl(wb, 16 * m)), A("W2", sl(16 * c0, 16 * m)))
+            else:
+                dma(A("W2b", sl(wb, 16 * m)), A("W2", sl(16 * c0, 16 * m)), "gp", 2500.0 + 20 * m)
+            t = tile()
+            mm([(A(t, sl(0, m)), [(SUMk(k), A("W2b", sl(wb + k, m, 16))) for k in range(16)]
+                 + ([(SUMk(k), A("W1", sl(16 * c0 + k, m, 16))) for k in range(16)] if u == 2 and CFG["tail"] else []))])
+            ts(A("KL", C_), A(t, sl(0, m)), 4096.0, OP.is_gt, 8192.0, OP.mult)
+            act(A("tmpB", C_), A(t, sl(0, m)), AF.Abs, bias=A("PF", sl(8 + u, 1)))
+            tt(A("DD", sl(CD + c0, m)), A("DD", sl(CD + c0, m)), A("KL", C_), OP.max)
+            ts(A("EQ", C_), A("tmpB", C_), 8064.0, OP.is_equal)
+        t = tile(); a = nc // 16
+        mm([(A(t, sl(0, a)), [(SUMk(r), A("EQ", sl(r, a, 16))) for r in range(16)])])
+        ts(A("FR", sl(0, a)), A(t, sl(0, a)), 0.5, OP.is_gt)
+        tt(A("FC", sl(0, a)), A("FC", sl(0, a)), A("FR", sl(0, a)), OP.max)
+
+    def kill_border():
+        for c0, m in ((0, 32), (32, 24)):
+            t = tile()
+            mm([(A(t, sl(k, m, 16)), [(ID, A("BW", sl(BO + 16 * c0 + k, m, 16))), (BCk(k), A("DD", sl(CD + c0, m)))]) for k in range(16)])
+            act(A("BW", sl(BO + 16 * c0, 16 * m)), A(t, sl(0, 16 * m)), AF.Identity)
+
+    for u in range(3):
+        ms(A("PF", sl(8 + u, 1)), -(8064 + 64 * (u + 1)))
+    ms(A("FC", sl(0, 11)), 0)
+    flag_static(0, 0, 176)
+    for u in range(3):
+        cnt["tag"] = "k%d" % u
+        if u:
+            decode(u - 1); kill_border(); camlist(u)
+            if u == 1:
+                exchange(3, "BW", BO, "SB", BG1)
+        cnt["tag"] = "t%d" % u
+        tracklist(u)
+        views(u)
+        if u == 2 and CFG["tail"]:
+            for h in range(8):
+                iota(A("W2", sl(896 * h, 896)), [[0, 896]], 0, 0)
+        for ci, segs in enumerate(CFG["s1"][u]):
+            dyn = any(c0 < 0 for c0, m in segs)
+            step1(u, segs)
+            if u == 0 and ci == 0:
+                exchange(1, "BW", BO, "SB", BG0)
+            if u == 2 and dyn:
+                sent = exchange(5, "BW", BO, "SB", BG0)
+                for h in range(8 if CFG["tail"] else 0):
+                    ops[iota(A("W1", sl(896 * h, 896)), [[0, 896]], 0, 0)]["deps"].setdefault(sent, False)
+        j0 = 0
+        for n in CFG["s2"][u]:
+            step2(u, j0, n, u == 2 and CFG["tail"] and j0 + n == 256); j0 += n
+        tt(IND(A("TVW"), A("OT")), A("v"), A("w"), OP.max)
+        cnt["tag"] = "f%d" % u
+        if u < 2:
+            fs = flag_static(u + 1, *((176, 160), (352, 96))[u])
+            for i in fs[len(fs) - CFG["hold"][u]:]:
+                ops[i]["deps"].setdefault(cnt["xn"], False)
+        if u < 2:
+            exchange(2 * u + 2, "XW", XO, "SX", XG1 if u == 0 else XG0)
+    P8 = slice(0, 8); cnt["tag"] = "z"
+    dma(A("yx"), A("XW", sl(XO, NT)))
+    ts(A("SX"), A("TVW", sl(256, NT)), 8064.0, OP.is_lt)
+    ts(A("FR"), A("FT"), 32.0, OP.mult)
+    for h in range(2):
+        t = tile()
+        mm([(A(t, sl(r, 28, 16), p=P8), [(A("ONES", sl(0, 8, 16)), A("SX", sl(448 * h + r, 28, 16))),
+                                         (A("BC", sl(128 * r, 8, 16)), A("FR", sl(28 * h, 28)))]) for r in range(16)])
+        act(A("IDS", sl(448 * h, 448), p=P8), A(t, sl(0, 448), p=P8), AF.Identity)
+    dma(A("yt"), A("IDS", p=P8))
+    decode(2)
+    for q in range(4):
+        c0 = 336 + 32 * q; m = min(32, 448 - c0); t = tile()
+        mm([(A(t, sl(k, m, 16)), [(ID, A("BW", sl(BO + 5376 + 512 * q + k, m, 16))), (BCk(k), A("DD", sl(CD + c0, m)))]) for k in range(16)])
+        ts(A("RR1", sl(512 * q, 16 * m)), A(t, sl(0, 16 * m)), 512.0, OP.min)
+    dma(A("yb"), A("RR1", sl(0, 1792)))
+    ts(A("EQ"), A("DD", sl(CD, NC)), 1.0, OP.is_lt)
+    ts(A("FR", sl(0, 28)), A("FC"), 32.0, OP.mult)
+    t = tile()
+    mm([(A(t, sl(r, 28, 16), p=P8), [(A("ONES", sl(0, 8, 16)), A("EQ", sl(r, 28, 16))),
+                                     (A("BC", sl(128 * r, 8, 16)), A("FR", sl(0, 28)))]) for r in range(16)])
+    act(A("tmpB", p=P8), A(t, sl(0, 448), p=P8), AF.Identity)
+    dma(A("yc"), A("tmpB", p=P8))
+    return ops
+
+
+WAKE = 180.0
+URGE = {'c6aS0b': -6, 'c14aZ1a': 20, 'ig': 20, 'c5aG0': 6, 't2': 20, 'c9dRa': -20, 'iaSX': 20, 'c14dFa': -20, 'idtE': 20, 'c12dRb': -20, 't2pk': 20,
+        'c1dp': 20, 'c6aG1': 20, 'c3aW2s': -20, 'c9aAB0': 20, 'igW1': -20, 'c4dFb': -6, 'c3aG0': 20, 'c1aRR0': -6, 'c1aAB0': 20, 'c6pp': -6,
+        'c3dFb': 20, 'c10aW2s': 20, 'c5dp': -6, 'c9aS0b': 20, 'c13dFa': 20, 'c15aAB0': 20}
+
+
+def backward(ops, deps, fin):
+    n = len(ops); ns = [0] * n; rt = [0.0] * n; et = {}; out = [0.0] * n
+    for i in range(n):
+        for j in deps[i]:
+            ns[j] += 1
+    ready = [i for i in range(n) if ns[i] == 0]
+    while ready:
+        cand = [(max(rt[i] + ops[i]["lat"], et.get(ops[i]["e"], 0.0)), i) for i in ready]
+        m, i0 = min(cand)
+        st, i = max([c for c in cand if c[0] <= m + CFG["win"] and ops[c[1]]["e"] == ops[i0]["e"]], key=lambda c: fin[c[1]])
+        out[i] = et[ops[i]["e"]] = st + ops[i]["cost"]; ready.remove(i)
+        for j in deps[i]:
+            rt[j] = max(rt[j], out[i] + WAKE); ns[j] -= 1
+            if ns[j] == 0:
+                ready.append(j)
+    return out
+
+
+def schedule(ops, rounds=8):
+    n = len(ops); base = [dict(o["deps"]) for o in ops]; prio = [0.0] * n
+    for i in range(n - 1, -1, -1):
+        prio[i] += ops[i]["cost"] + ops[i]["lat"]
+        for j in base[i]:
+            prio[j] = max(prio[j], prio[i] + WAKE)
+    best = None
+    for r in range(rounds):
+        for o, b in zip(ops, base):
+            o["deps"] = dict(b)
+        res = forward(ops, [x + (1e5 if o["sem"] else 0) + 1e3 * URGE.get(o["tag"], 0) + 1e3 * URGE.get(o["tag"][:2], 0) for x, o in zip(prio, ops)])
+        if best is None or max(res[3]) < max(best[0][3]):
+            best = (res, [o["deps"] for o in ops])
+        prio = backward(ops, base, res[3])
+    for o, b in zip(ops, best[1]):
+        o["deps"] = b
+    return best[0]
+
+
+def forward(ops, prio):
+    n = len(ops); succ = [[] for _ in range(n)]
+    for i, o in enumerate(ops):
+        for j in o["deps"]:
+            succ[j].append(i)
+    users = {}
+    for i, o in enumerate(ops):
+        for t in o["tiles"]:
+            users.setdefault(t, []).append(i)
+    left = {t: len(v) for t, v in users.items()}
+    free = {"p": [["P%d" % i, None] for i in range(NPB)], "k": [["K%d" % i, None] for i in range(8 - NPB)]}
+    bank = {}; fin = [0.0] * n; start = [0.0] * n; etime = {}; order = []
+    nd = [len(o["deps"]) for o in ops]; ready = [i for i in range(n) if nd[i] == 0]; rt = [0.0] * n
+
+    def tend(t):
+        return max(fin[j] for j in users[t]) + WAKE if t else 0.0
+    while ready:
+        cand = []
+        for i in ready:
+            o = ops[i]; st = max(rt[i], etime.get(o["e"], 0.0)); pick = None
+            new = [t for t in o["tiles"] if t not in bank]
+            if new:
+                fl = free[new[0][0]]
+                if not fl:
+                    continue
+                pick = min(fl, key=lambda b: tend(b[1])); st = max(st, tend(pick[1]))
+            cand.append((st, i, pick, new))
+        m = min(c[0] for c in cand)
+        e0 = [c for c in cand if c[0] == m][0]
+        st, i, pick, new = max([c for c in cand if c[0] <= m + CFG["win"] and ops[c[1]]["e"] == ops[e0[1]]["e"]], key=lambda c: prio[c[1]])
+        o = ops[i]
+        if pick:
+            free[new[0][0]].remove(pick); bank[new[0]] = pick[0]
+            for j in (users[pick[1]] if pick[1] else []):
+                o["deps"].setdefault(j, False)
+        start[i] = st; etime[o["e"]] = st + o["cost"]; fin[i] = st + o["cost"] + o["lat"]
+        order.append(i); ready.remove(i)
+        for t in o["tiles"]:
+            left[t] -= 1
+            if left[t] == 0:
+                free[t[0]].append([bank[t], t])
+        for j in succ[i]:
+            same = ops[j]["e"] == o["e"] == "pe" and not ops[j]["deps"][i]
+            rt[j] = max(rt[j], fin[i] + (0.0 if same else WAKE)); nd[j] -= 1
+            if nd[j] == 0:
+                ready.append(j)
+    assert len(order) == n
+    return order, bank, start, fin
+
+
+PLAN = {}
+
+
+def lanes(T, topo, src):
+    r = T.rank_of(src); dst = {d: T.cores[r ^ d] for d in range(1, 8)}
+    far = [d for d in dst if topo.chip(dst[d]) != topo.chip(src)]; used = 0; m = {}
+    for d in far:
+        e = [x for x in topo.engines(src, dst[d]) if not used >> x & 1][0]
+        m[d] = 1 << e; used |= m[d]
+    farall = 0
+    for d in far:
+        farall |= topo.mask(src, dst[d])
+    near = [d for d in dst if d not in far]
+    for j, d in enumerate(near):
+        es = [x for x in topo.engines(src, dst[d]) if not farall >> x & 1][j::len(near)]
+        k = 1 << (len(es).bit_length() - 1)
+        m[d] = sum(1 << x for x in es[:k])
+    return m
+
+
+def rank_program(g, core, T, topo):
+    rank = T.rank_of(core)
+    if rank is None:
+        return
+    if not PLAN:
+        ops = build()
+        PLAN["ops"] = ops
+        PLAN["s"] = schedule(ops)
+    ops = PLAN["ops"]; order, bank = PLAN["s"][:2]
+    Q = {"pe": g.tensor, "dve": g.vector, "act": g.scalar, "gp": g, "sp": g.sync}
+    mine = lanes(T, topo, core)
+    nsent = sum(bin(x).count("1") for x in mine.values())
+    narr = sum(bin(lanes(T, topo, T.cores[rank ^ d])[d]).count("1") for d in range(1, 8))
+
+    def R(x):
+        if not isap(x):
+            return x
+        if x[0] == "ind":
+            return R(x[1]).indirect(R(x[2]))
+        return T[bank.get(x[1], x[1])][(x[2] or slice(None),) + tuple(x[3])]
+    count = {"pe": 0, "dve": 0, "act": 0, "gp": 0}; tok = {}; seen = {e: {} for e in Q}; allsem = {}
+    place = {j: x for x, j in enumerate(order)}; known = {}
+
+    def wait(e, s, v):
+        if seen[e].get(s, 0) < v:
+            Q[e].wait_ge(T.sem[s], v); seen[e][s] = v
+    for i in order:
+        o = ops[i]; e = o["e"]
+        if e == "arr":
+            tok[i] = (o["sem"][0], narr); allsem[o["sem"][0]] = narr
+            continue
+        for j in sorted(o["deps"], key=lambda j: -place[j]):
+            s, v = tok[j]
+            if seen[e].get(s, 0) < v:
+                wait(e, s, v)
+                for s2, v2 in known.get(j, {}).items():
+                    seen[e][s2] = max(seen[e].get(s2, 0), v2)
+        known[i] = dict(seen[e])
+        q = Q[e]
+        for c in o["calls"]:
+            k = c[0]; a = [R(x) for x in c[1:]]
+            if k == "dma":
+                q.dma_start(a[0], a[1]).then_inc(T.sem[o["sem"][0]], 16); tok[i] = o["sem"]
+                continue
+            if k == "send":
+                tr = []
+                for d in range(1, 8):
+                    rid, pid, _ = topo.addr(T.cores[rank ^ d])
+                    tr.append(RemoteDMATransfer(dst_ids=[DstId(rid=rid, pnc=pid)], dma_engine_mask=mine[d], remote_sem=T.sem["arr%d" % c[2]],
+                                                src=T[c[1][1]][:, GH * (d - 1):GH * d], dst=T[c[3]][:, c[4] + GH * (d - 1):c[4] + GH * d]))
+                q.remote_dma_fused(tr, local_sem=T.sem[o["sem"][0]]); tok[i] = (o["sem"][0], nsent)
+                continue
+            if k == "mm":
+                x = q.matmul(a[0], a[1], a[2], a[3], a[4])
+            elif k == "tt":
+                x = q.tensor_tensor(a[0], a[1], a[2], a[3])
+            elif k == "ts":
+                x = q.tensor_scalar(a[0], a[1], a[2], a[3], a[4]) if a[5] is None else q.tensor_scalar(a[0], a[1], a[2], a[3], a[4], a[5])
+            elif k == "cp":
+                x = q.tensor_copy(a[0], a[1])
+            elif k == "ms":
+                x = q.memset(a[0], a[1])
+            elif k == "scan":
+                x = q.tensor_tensor_scan(a[0], a[1], a[2], a[3], a[4], a[5])
+            elif k == "iota":
+                x = q.iota(a[0], a[1], a[2], a[3]) if DTYPE[c[1][1]] == I32 else q.iota(a[0], a[1], a[2], a[3], allow_small_or_imprecise_dtypes=True)
+            elif c[1][0] == "ind":
+                x = q.activation(a[0], a[1], a[2])
+            else:
+                x = q.activation(a[0], a[1], a[2], bias=a[3], scale=a[4])
+            if e != "pe" or c is o["calls"][-1]:
+                x.then_inc(T.sem[e], 1); count[e] += 1
+            tok[i] = (e, count[e])
+        allsem[tok[i][0]] = max(allsem.get(tok[i][0], 0), tok[i][1])
+    for s, v in allsem.items():
+        g.wait_ge(T.sem[s], v)

@@ -4,19 +4,21 @@ from concourse.mybir import AluOpType as OP, ActivationFunctionType as AF
 
 NC, NT, GH = 448, 896, 128
 F32, BF, I32, U16 = "float32", "bfloat16", "int32", "uint16"
-XG1, XD, XO, XG0, XE = 0, 896, 1152, 2048, 2944
-BG1, BE1, BD, BO, BG0, BE0, BE = 0, 896, 912, 2192, 9360, 10256, 10272
+XD, XO, XG, XE = 0, 256, 1152, 2048
+BD, BO, BG, BN, BE = 0, 1280, 8448, 9344, 9360
 CD = 80
-W1N, W2N = 14336 + 512, 8064 + 512
-EMPTY = 16128.0
+W1N, W2N = 14336 + 256, 8064 + 512
+EMPTY = 8704.0
+ULP = 1.5 * 2 ** 23
 
 CFG = dict(
-    s1=[[[(0, 112)], [(112, 64)]],
+    s1=[[[(0, 64)], [(64, 112)]],
         [[(176, 96)], [(272, 64), (-1, 16)]],
         [[(-1, 80)], [(352, 96)]]],
-    s2=[[64, 128, 64], [64, 128, 64], [64, 128, 64]],
-    bad1="dve", bad2="dve", spass="aaa", kd=(14, 15), conv=("da", "dada", "aaaa"), np_sets=2, w1=(6, 13), off=(0, 1), tail=True,
-    exact=True, win=20.0, hold=(10, 3),
+    s2=[[80, 80, 96], [80, 80, 96], [80, 80, 96]],
+    look=1.0, marg=6000.0, boost=0.0, small=150.0, rounds=6, tries=1500, seed=1,
+    fit="adaad" "adaad" "daaad" "d", lw=56, conv=("aaaap", "aaapapa", "apaaapaa"), np_sets=2, w1=(3, 13), ondve=(160, 160, 160),
+    exact=True, hold=(0, 0), obq="sp", onact="hn", border=False, blocks=((160, 16, 0, 64, 64, 96), (0, 112, 112, 112, 224, 128), (224, 224, 0, 224)), off2=((0, 1, 1, 1), (0, 1, 1, 1), (0, 1, 1, 1)),
 )
 
 SCRATCH = {}
@@ -29,26 +31,24 @@ def _decl(name, shape, dt, where="sbuf"):
 
 
 for _n, _s, _d in [
-    ("OB", [7168], BF), ("XW", [XE], BF), ("BW", [BE], BF), ("W1", [W1N], BF), ("W2", [W2N], F32), ("W2b", [3584], BF),
-    ("CTi", [448], I32), ("TVi", [896], I32), ("TRW", [CD + NC], F32), ("EW", [CD + NC], F32), ("DD", [CD + NC], BF),
+    ("OB", [7168], BF), ("XW", [XE], BF), ("BW", [BE], BF), ("W1", [W1N], BF), ("W2", [W2N], F32), ("W2b", [3584], BF), ("W3", [W2N], BF), ("PY", [128], F32),
+    ("CTi", [CD + NC], I32), ("TVi", [896], I32), ("NV", [128], BF), ("EW", [CD + NC], F32), ("DD", [CD + NC], BF),
     ("TVW", [256 + NT], F32), ("TRu", [NC], U16), ("EOu", [NC], U16), ("tmpB", [NC], F32),
-    ("COL", [128], BF), ("PI", [8], I32), ("PF", [16], F32), ("KX", [8], F32), ("KEY", [16], F32), ("DK", [16], F32),
-    ("K16", [16], F32), ("SUM", [2048], BF), ("BC", [2048], BF), ("PM", [1024], BF), ("NI", [128], BF), ("ONES", [128], BF),
+    ("COL", [144], BF), ("PI", [8], I32), ("PF", [16], F32), ("KX", [1], F32), ("KEY", [16], F32), ("DK", [16], F32),
+    ("K16", [16], F32), ("SUM", [144], BF), ("BC", [2048], BF), ("ID", [128], BF), ("PX", [128], BF), ("O8", [8], BF), ("EX", [128], BF), ("NI", [128], BF), ("ONES", [128], BF),
     ("H17", [512], BF), ("WL", [128], BF), ("NU", [128], BF), ("mt", [128], BF), ("mt2", [128], BF),
-    ("J2", [128], F32), ("J1", [128], F32), ("DM", [256], F32), ("RS", [256], F32), ("ONE", [64], F32), ("DJ", [256], F32),
-    ("IDS", [NT], F32), ("LW", [256 + NT], F32), ("LM", [256], F32), ("LS", [256], F32), ("Li", [CD], I32), ("OT", [16], U16),
-    ("OC", [8], U16), ("PO", [56], U16), ("FT", [56], BF), ("FC", [28], BF), ("FR", [56], BF), ("RK", [56], F32), ("RK2", [56], F32),
-    ("SEL", [56], F32), ("IT", [56], F32), ("CS", [3, 256], BF), ("v", [256], F32), ("w", [256], F32), ("w2", [256], F32), ("vo", [256], U16), ("wo", [256], U16),
-    ("xo", [256], BF), ("DGl", [CD], BF), ("tE", [128], F32), ("SX", [896], BF), ("SB", [896], BF),
-    ("OG", [16 * CD], BF), ("BT", [16 * CD], BF), ("PP", [CD], U16), ("OP_", [CD], U16), ("TD", [CD], U16), ("ED", [CD], U16),
-    ("tD", [CD], F32), ("tD2", [CD], F32), ("DG", [CD], BF), ("DN", [CD], BF), ("SS", [2048], F32), ("EQ", [NC], BF), ("KL", [NC], BF),
-    ("Ra", [128, 10], BF), ("Rb", [128, 10], BF), ("Fa", [1152], BF), ("Fb", [1152], BF),
+    ("J2", [128], F32), ("J1", [128], F32), ("DM", [256], BF), ("RS", [256], BF), ("ONE", [64], F32), ("DJ", [256], F32),
+    ("IDS", [NT], F32), ("LW", [2 * NT], F32), ("LM", [256], F32), ("LS", [256], F32), ("Li", [CD], I32), ("OT", [16], U16), ("OU", [18], U16),
+    ("OC", [8], U16), ("PO", [56], U16), ("FT", [56], BF), ("FC", [28], BF), ("FR", [56], BF), ("FQ", [56], BF), ("RK", [56], F32), ("RK2", [56], F32),
+    ("SEL", [56], BF), ("IT", [56], F32), ("CS", [3, 256], BF), ("v", [256], F32), ("w", [256], F32), ("w2", [256], F32), ("vo", [256], U16), ("wo", [256], U16),
+    ("xo", [256], BF), ("DGl", [CD], BF), ("tE", [128], F32), ("G", [4096], BF), ("RR", [4096], BF), ("AB", [4096], BF),
+    ("un", [256], BF), ("FF", [256], BF), ("ft", [256], BF), ("gd", [256], BF), ("MM", [256], BF), ("nF", [256], BF),
+    ("PP", [CD], U16), ("OP_", [CD], U16), ("TD", [CD], U16), ("ED", [CD], U16),
+    ("tD", [CD], F32), ("tD2", [CD], F32), ("DG", [CD], BF), ("DN", [CD], BF), ("SS", [2560], F32), ("EQ", [NC], BF),
 ]:
     _decl(_n, _s, _d)
 for _s in "01":
-    for _n, _sh, _d in [("G", [2048], BF), ("RR", [2048], BF), ("AB", [2048], BF), ("S0a", [512], BF), ("S0b", [512], BF),
-                        ("FO", [1152], BF), ("un", [128], BF), ("FF", [128], BF), ("ft", [128], BF), ("gd", [128], BF),
-                        ("MM", [128], BF), ("nF", [128], BF), ("ym", [128], BF)]:
+    for _n, _sh, _d in [("S0a", [512], BF), ("S0b", [512], BF), ("FO", [1152], BF), ("Fa", [1152], BF), ("Fb", [1152], BF)]:
         _decl(_n + _s, _sh, _d)
     for _c in "ab":
         _decl("Z" + _s + _c, [128, 4], BF)
@@ -111,7 +111,37 @@ def two(ap):
     return DTYPE.get(ap[1], F32) in (BF, U16)
 
 
-CYC, PEC, GAT, SCA = 1.0, 0.5, 1.56, 3.8
+WAKE = 240.0
+FIGURES = [dict(f=1.05, fix=5, gat=1.3, sca=2.6, wake=240, lat=1.1), dict(f=1.15, fix=0, gat=1.1, sca=1.8, wake=280, lat=0.9),
+           dict(f=1.4, fix=10, gat=1.8, sca=4.5, wake=160, lat=1.3)]
+
+
+def price(o, m):
+    e = o["e"]; tot = 0.0
+    for c in o["calls"]:
+        k = c[0]; out = c[1]; ins = [x for x in c[2:] if isap(x)]
+        sc = out[0] == "ind"; ga = any(x[0] == "ind" for x in ins)
+        n = 16 * region(out[2])[3] if sc else region(out)[3]
+        if k == "mm":
+            tot += max(min(64, region(c[2])[3]), n) * 0.417 * m["f"] * (1 if two(c[3]) else 4)
+        elif k in ("dma", "send", "recv"):
+            tot += (5200 if c[3] else 650) if k == "dma" else 2400 if k == "send" else 0
+        elif e == "gp":
+            tot += (150 + 2 * n * 0.83) * m["f"]
+        elif sc or ga:
+            tot += (55 + n * (m["sca"] if sc else m["gat"]) * 0.83) * m["f"]
+        else:
+            f = 1.0
+            if k == "tt":
+                f = 1.0 if psum(ins[0]) or psum(ins[1]) else 2.0
+            elif e == "dve" and all(two(x) for x in [out] + ins if region(x)[3] > 1):
+                f = 0.5
+            tot += (m["fix"] + max(64, n * f) * 0.83) * m["f"]
+    return tot
+
+
+def waits(ops, i, j):
+    return not ops[i]["e"] == ops[j]["e"] == "pe"
 
 
 def build():
@@ -142,7 +172,6 @@ def build():
 
     def op(e, calls, lat=0.0, sem=None):
         i = len(ops); o = dict(e=e, calls=calls, deps={}, lat=lat, sem=sem, tiles=[]); ops.append(o)
-        cost = 0.0
         for c in calls:
             k = c[0]; out = c[1]; ins = [x for x in c[2:] if isap(x)]
             if k == "mm" and not c[4]:
@@ -151,7 +180,7 @@ def build():
                 for y in ((x[1], x[2]) if x[0] == "ind" else (x,)):
                     touch(i, y, False, o["deps"])
             if out[0] == "ind":
-                touch(i, out[2], False, o["deps"]); touch(i, out[1], False, o["deps"]); touch(i, out[1], True, o["deps"])
+                touch(i, out[2], False, o["deps"]); touch(i, out[1], True, o["deps"])
             elif k != "send":
                 touch(i, out, True, o["deps"])
             else:
@@ -159,27 +188,7 @@ def build():
             for x in [out] + ins:
                 if psum(x) and x[1] not in o["tiles"]:
                     o["tiles"].append(x[1])
-            sc = out[0] == "ind"; ga = any(x[0] == "ind" for x in ins)
-            n = 16 * region(out[2])[3] if sc else region(out)[3]
-            if k == "mm":
-                cost += max(64, n) * PEC
-            elif k in ("dma", "send", "recv"):
-                cost += {"dma": 1000 if e == "gp" else 60, "send": 1200, "recv": 0}[k]
-            elif e == "gp":
-                cost += 150 + 2 * n * CYC
-            else:
-                f = 1.0
-                if sc:
-                    f = SCA
-                elif ga:
-                    f = GAT
-                elif k == "tt":
-                    f = 1.0 if psum(ins[0]) or psum(ins[1]) else 2.0
-                elif e == "dve" and all(two(x) for x in [out] + ins if region(x)[3] > 1):
-                    f = 0.5
-                cost += 50 + max(64, n * f) * CYC
-        o["cost"] = cost
-        w_ = calls[0][1]
+        w_ = calls[0][1]; o["ph"] = cnt["tag"] + e[0]
         o["tag"] = "%s%s%s" % (cnt["tag"], e[0], (w_[1][1] + "s" if w_[0] == "ind" else w_[1][0] if psum(w_) else w_[1])[:3])
         return i
 
@@ -209,62 +218,68 @@ def build():
                 c.append(("mm", out, l, r, j == 0 and "<" in (g_ + ("<>",))[2], j == len(terms) - 1 and ">" in (g_ + ("<>",))[2]))
         return op("pe", c)
 
-    def dma(out, a, q="sp", lat=2500.0):
+    def dma(out, a, q="sp", lat=2000.0, xor=True):
         cnt["d"] += 1
-        return op(q, [("dma", out, a)], lat=lat, sem=("d%d" % (cnt["d"] - 1), 16))
+        return op(q, [("dma", out, a, xor)], lat=lat, sem=("d%d" % (cnt["d"] - 1), 16))
 
     def SUMk(k):
-        return A("SUM", sl(128 * k, 128))
+        return A("SUM", sl(15 - k, 128))
 
     def BCk(k):
         return A("BC", sl(128 * k, 128))
-    ID, NI, ONES = A("PM", sl(0, 128)), A("NI"), A("ONES")
+    ID, NI, ONES = A("ID"), A("NI"), A("ONES")
 
-    def exchange(x, src, off, buf, dst):
-        for b0, nb in ((0, 4), (4, 3)):
-            t = tile()
-            mm([(A(t, sl(128 * j, 128)), [(A("PM", sl(128 * (b0 + j + 1), 128)), A(src, sl(off + 128 * (b0 + j), 128)))]) for j in range(nb)])
-            act(A(buf, sl(128 * b0, 128 * nb)), A(t, sl(0, 128 * nb)), AF.Identity)
-        s = op("gp", [("send", A(buf), x, src, dst)], lat=6000.0, sem=("snt%d" % x, 0))
+    def exchange(x, src, off, dst):
+        s = op("gp", [("send", A(src, sl(off, 896)), x, src, dst)], lat=4500.0, sem=("snt%d" % x, 0))
         r = op("arr", [("recv", A(src, sl(dst, 896)))], lat=500.0, sem=("arr%d" % x, 0))
-        ops[r]["deps"][s] = False
+        ops[r]["deps"][s] = False; cnt["arr"] = r
         return s
 
-    dma(A("XW", sl(XO, NT)), A("x0"))
-    dma(A("CTi"), A("ct"))
-    dma(A("OB", sl(0, 2816)), A("obs", sl(0, 2816)), lat=3500.0)
+    dma(A("RR", sl(0, NT)), A("x0"), xor=False)
+    CT = A("CTi", sl(CD, NC))
+    dma(CT, A("ct"), xor=False)
+    dma(A("OB", sl(0, 2816)), A("obs", sl(0, 2816)), CFG["obq"], lat=3500.0)
     dma(A("TVi"), A("tv"))
     dma(A("OB", sl(2816, 4352)), A("obs", sl(2816, 4352)), lat=6000.0)
+    iota(A("KX"), [[0, 1]], 0, 1)
+    for h in range(2):
+        op("gp", [("iotax", A("mt", sl(64 * h, 64)), h)])
+    PX = A("PX")
+    ts(PX, A("mt"), A("KX"), OP.is_equal)
+    ts(A("PY"), A("mt"), A("KX"), OP.is_equal)
+    for h in range(2):
+        t = tile()
+        mm([(A(t, sl(0, 448)), [(PX, A("RR", sl(448 * h, 448)))])])
+        (cp if h else lambda a, b: act(a, b, AF.Identity))(A("XW", sl(XO + 448 * h, 448)), A(t, sl(0, 448)))
+    exchange(0, "XW", XO, XG)
     iota(A("PI", sl(0, 1)), [[0, 1]], 0, 1)
-    iota(A("COL"), [[1, 128]], 0, 0)
+    iota(A("COL"), [[1, 144]], 0, 0)
+    COL = A("COL", sl(0, 128))
     iota(A("K16"), [[1, 16]], 0, 0)
     p_ = A("PI", sl(0, 1))
-    cp(A("KX", sl(0, 1)), p_)
-    for b in range(3):
-        ts(A("PI", sl(1 + b, 1)), p_, 4 + b, OP.arith_shift_right, 1, OP.bitwise_and)
-        ts(A("PF", sl(b, 1)), A("PI", sl(1 + b, 1)), float(-32 << b), OP.mult, float(16 << b), OP.add)
-        ts(A("KX", sl(1 << b, 1 << b)), A("KX", sl(0, 1 << b)), A("PF", sl(b, 1)), OP.add)
-    for d in range(8):
-        ts(A("PM", sl(128 * d, 128)), A("COL"), A("KX", sl(d, 1)), OP.is_equal)
-    exchange(0, "XW", XO, "SX", XG0)
+    ts(ID, COL, A("KX", sl(0, 1)), OP.is_equal)
     ts(A("PI", sl(4, 1)), p_, 15, OP.bitwise_and)
     PK, PG = A("PF", sl(4, 1)), A("PF", sl(5, 1))
     cp(PK, A("PI", sl(4, 1)))
     ts(PG, A("KX", sl(0, 1)), PK, OP.subtract)
+    ts(A("O8"), A("mt", sl(0, 8, 16)), PG, OP.is_equal)
     ts(A("KEY"), A("K16"), PG, OP.add)
     ts(A("DK"), A("K16"), PK, OP.is_equal)
     ts(A("NI"), ID, -1.0, OP.mult)
-    ts(A("mt"), A("COL"), PG, OP.is_ge)
-    ts(A("mt2"), A("COL"), A("KEY", sl(15, 1)), OP.is_le)
+    ts(A("mt"), COL, PG, OP.is_ge)
+    ts(A("mt2"), COL, A("KEY", sl(15, 1)), OP.is_le)
     tt(ONES, A("mt"), A("mt2"), OP.mult)
+    ts(A("SUM"), A("COL", sl(0, 144)), A("KEY", sl(15, 1)), OP.is_equal)
     for k in range(16):
-        ts(SUMk(k), A("COL"), A("KEY", sl(k, 1)), OP.is_equal)
         act(BCk(k), ONES, AF.Copy, scale=A("DK", sl(k, 1)))
     p32 = A("KX", sl(0, 1))
-    ts(A("mt"), A("COL"), p32, OP.is_le, -1.0, OP.mult)
-    tt(A("NU"), A("mt"), ONES, OP.mult)
-    ts(A("mt2"), A("COL"), p32, OP.is_gt, 1.0, OP.mult)
-    ts(A("mt"), A("COL"), p32, OP.is_lt, -1.0, OP.mult)
+    ts(A("mt"), COL, p32, OP.is_le, -1.0, OP.mult)
+    tt(A("mt"), A("mt"), ONES, OP.mult)
+    ts(A("mt2"), ID, -2048.0, OP.mult)
+    tt(A("NU"), A("mt"), A("mt2"), OP.min)
+    act(A("NV"), A("NU"), AF.Copy, scale=-1.0)
+    ts(A("mt2"), COL, p32, OP.is_gt, 1.0, OP.mult)
+    ts(A("mt"), COL, p32, OP.is_lt, -1.0, OP.mult)
     tt(A("mt"), A("mt"), A("mt2"), OP.add)
     tt(A("mt"), A("mt"), ONES, OP.mult)
     ts(A("mt2"), ID, 63.0, OP.mult)
@@ -275,48 +290,48 @@ def build():
     tt(A("H17", sl(128, 128)), ONES, A("H17", sl(384, 128)), OP.add)
     iota(A("J2"), [[0, 4], [16, 32]], 8064, 0)
     ts(A("J2"), A("J2"), PK, OP.add)
-    ts(A("J1"), A("J2"), float(14336 - 8064), OP.add)
+    iota(A("J1"), [[0, 8], [16, 16]], 14336, 0)
+    ts(A("J1"), A("J1"), PK, OP.add)
     iota(A("DJ"), [[1, 256]], 0, 0)
     iota(A("RS"), [[0, 16], [1, 16]], 0, 0)
     ts(A("DM"), A("RS"), PK, OP.is_equal)
     ts(A("RS"), A("RS"), 0.5, OP.is_gt)
-    iota(A("IT"), [[16, 56]], 256, 0)
+    iota(A("IT"), [[16, 56]], NT, 0)
     ts(A("IT"), A("IT"), PK, OP.add)
     ms(A("ONE"), 1)
     for u in range(3):
         ms(A("CS", u), 32 ** u)
-    ms(A("Fa", sl(0, 128, 9)), -30000)
+    ms(A("Fa0", sl(0, 128, 9)), -30000); ms(A("Fa1", sl(0, 128, 9)), -30000)
     for h in range(16):
         if h < CFG["w1"][0]:
             ms(A("W1", sl(896 * h, 896)), 0)
         elif h < CFG["w1"][1]:
-            act(A("W1", sl(896 * h, 896)), A("XW", sl(XO, NT)), AF.Copy, scale=0.0)
+            act(A("W1", sl(896 * h, 896)), A("W1", sl(0, 896)), AF.Copy)
         else:
             iota(A("W1", sl(896 * h, 896)), [[0, 896]], 0, 0)
-    ms(A("W1", sl(14336, 512)), 0)
-    ms(A("FT"), 0); ms(A("FC"), 1); ms(A("DD"), 0)
+    ms(A("W1", sl(14336, 256)), 0)
+    ms(A("FQ"), 0); ms(A("FC"), 1); ms(A("DD"), 0)
     ms(A("XW", sl(XD, 256)), 512); ms(A("TVW", sl(0, 256)), EMPTY)
-    ms(A("TRW", sl(0, CD)), 0); ms(A("EW", sl(0, CD)), 60000)
-    iota(A("BW", sl(BE1, 16 + 1280)), [[0, 1296]], 512, 0); ms(A("BW", sl(BE0, 16)), 512)
-    iota(A("LW"), [[0, 256 + NT]], 0, 0)
+    ms(A("CTi", sl(0, CD)), 0); ms(A("EW", sl(0, CD)), 60000)
+    iota(A("BW", sl(BD, 1280)), [[0, 1280]], 512, 0); ms(A("BW", sl(BN, 16)), 512)
+    for h in range(2):
+        iota(A("LW", sl(NT * h, NT)), [[0, NT]], 0, 0)
     for h in range(4):
         iota(A("BW", sl(BO + 2816 + 1088 * h, 1088)), [[0, 1088]], 512, 0)
-    for h in range(8):
-        iota(A("W2", sl(1072 * h, 1072)), [[0, 1072]], 0, 0)
-    ts(A("SS", sl(0, NT)), A("TVi"), 8063.5, OP.is_gt, 8064.0, OP.mult)
+    for w in ("W2", "W3"):
+        for h in range(8):
+            iota(A(w, sl(1072 * h, 1072)), [[0, 1072]], 0, 0)
+    ts(A("SS", sl(0, NT)), A("TVi"), 8063.5, OP.is_gt, EMPTY - 8064, OP.mult)
     tt(A("TVW", sl(256, NT)), A("TVi"), A("SS", sl(0, NT)), OP.add)
-    ts(A("tmpB"), A("CTi"), 14335.5, OP.is_gt, 60000.0, OP.mult)
-    tt(A("EW", sl(CD, NC)), A("CTi"), A("tmpB"), OP.max)
-    ts(A("CTi"), A("CTi"), 4, OP.arith_shift_right)
-    cp(A("TRu", sl(0, 176)), A("CTi", sl(0, 176)))
-    cp(A("TRu", sl(352, 96)), A("CTi", sl(352, 96)))
-    cp(A("TRW", sl(CD, NC)), A("CTi"))
-
-    def odd_tr(out, src, t, n):
-        ts(t, src, 895.5, OP.is_gt, -2048.0, OP.mult)
-        tt(t, t, src, OP.add)
-        ts(out, t, 1152.0, OP.add)
-    odd_tr(A("TRu", sl(176, 160)), A("TRW", sl(CD + 176, 160)), A("tmpB", sl(0, 160)), 160)
+    t = tile(); ct = A(t, sl(0, NC))
+    cp(A("tmpB"), CT)
+    mm([(ct, [(A("PY"), A("tmpB"))])])
+    cp(CT, ct)
+    ts(A("tmpB"), ct, 14335.5, OP.is_gt, 60000.0, OP.mult)
+    tt(A("EW", sl(CD, NC)), ct, A("tmpB"), OP.max)
+    ts(CT, CT, 4, OP.arith_shift_right)
+    cp(A("TRu", sl(0, 176)), A("CTi", sl(CD, 176)))
+    cp(A("TRu", sl(176, 272)), A("CTi", sl(CD + 176, 272)))
 
     def flag_static(u, c0, n):
         for a in range(c0, c0 + n, 128):
@@ -325,7 +340,7 @@ def build():
             cp(A("EOu", sl(a, m)), A("tE", sl(0, m)))
         return [cp(IND(A("W1"), A("EOu", sl(a, 16))), A("CS", u)) for a in range(c0, c0 + n, 16)]
 
-    def worklist(F, cols, K, idbase, otile):
+    def worklist(F, cols, K, idbase, otile, new, th):
         n = len(cols); runs = []
         for j, c in enumerate(cols):
             if runs and runs[-1][1] + runs[-1][2] == c:
@@ -333,36 +348,44 @@ def build():
             else:
                 runs.append([j, c, 1])
         for j, c, m in runs:
-            cp(A("FR", sl(j, m)), A(F, sl(c, m)))
+            ts(A("FR", sl(j, m)), new(c, m), th, OP.is_gt)
             iota(A("IDS", sl(16 * j, 16 * m)), [[1, 16 * m]], idbase + 16 * c, 0)
         act(A("LW", sl(0, K)), A("DJ", sl(0, K)), AF.Identity)
-        fr = A("FR", sl(0, n)); t = tile()
-        mm([(A(t, sl(0, n)), [(ONES, fr)]), (A(t, sl(64, n)), [(A("NU"), fr)])])
+        t = tile()
+        op("pe", [("mm", A(t, sl(0, n)), ONES, A("FR", sl(0, n)), True, False), ("mm", A(t, sl(0, n)), A("NU"), A("FR", sl(0, n)), False, False),
+                  ("mm", A(t, sl(1, n - 1)), A("NV"), A("FR", sl(0, n - 1)), False, True)])
         rk, rk2, se = A("RK", sl(0, n)), A("RK2", sl(0, n)), A("SEL", sl(0, n))
-        op("dve", [("scan", rk, A("ONE", sl(0, n)), A(t, sl(0, n)), 0.0, OP.mult, OP.add)])
-        tt(rk, A(t, sl(64, n)), rk, OP.add)
-        ts(se, rk, K - 0.5, OP.is_lt)
-        tt(se, se, fr, OP.mult)
-        tt(rk2, rk, A("IT", sl(0, n)), OP.subtract)
-        tt(rk2, rk2, se, OP.mult)
-        tt(rk2, rk2, A("IT", sl(0, n)), OP.add)
+        op("dve", [("scan", rk, A("ONE", sl(0, n)), A(t, sl(0, n)), 2047.0, OP.mult, OP.add)])
+        tt(rk2, rk, A("IT", sl(0, n)), OP.min)
         cp(A("PO", sl(0, n)), rk2)
-        for a in range(0, n, 14):
-            m = min(14, n - a)
+        ts(se, rk, K - 0.5, OP.is_lt)
+        for a in range(0, n, CFG["lw"]):
+            m = min(CFG["lw"], n - a)
             act(IND(A("LW"), A("PO", sl(a, m))), A("IDS", sl(16 * a, 16 * m)), AF.Silu)
         tt(A("LM", sl(0, K)), A("LW", sl(0, K)), A("DM", sl(0, K)), OP.mult)
         op("dve", [("scan", A("LS", sl(0, K)), A("RS", sl(0, K)), A("LM", sl(0, K)), 0.0, OP.mult, OP.add)])
-        cp(A("Li", sl(0, K // 16)), A("LS", sl(15, K // 16, 16)))
-        cp(A(otile, sl(0, K // 16)), A("Li", sl(0, K // 16)))
+        ts(A(otile, sl(0, K // 16)), A("LS", sl(15, K // 16, 16)), 0.25, OP.add)
         for j, c, m in runs:
             tt(A(F, sl(c, m)), A("FR", sl(j, m)), A("SEL", sl(j, m)), OP.subtract)
 
-    def median(n, s, terms, flip=False, off=0, neg=None):
+    def quad(t, n, whole, each, start=True, stop=True):
+        pt = t[0] == "p"
+        al = A(t, slice(0, n)) if pt else A(t, sl(0, 4 * n))
+        c = [(al, l, r) for l, r in whole]
+        c += [(A(t, slice(0, n), j) if pt else A(t, sl(j, n, 4)), l, r) for j in range(4) for l, r in each(j)]
+        return op("pe", [("mm", o_, l, r, start and x == 0, stop and x == len(c) - 1) for x, (o_, l, r) in enumerate(c)])
+
+    def median(n, s, srcs, FF, flip=False, off=0, direct=None, nF=None):
         N_ = slice(0, n); P = {}
-        Qn = "Q" + s; Zn = "Z" + s
-        if cnt.get("flip") != flip:
-            cnt["flip"] = flip
-            ms(A("Fb", sl(0, 128, 9)), 30000 if flip else -30000)
+        whole = lambda q: [(l, A(b, sl(a + q, 4 * n, 4))) for l, b, a in srcs]
+        each = lambda k: [(BCk(k), FF)] if FF else []
+        wire = lambda k: [(l, A(b, sl(a + k, n, 16))) for l, b, a in srcs] + each(k)
+        neg = lambda ts_: [(NI, r) if l is ID else (ID, r) if l is NI else (l, nF if r is FF else FF) for l, r in ts_]
+        if off and FF:
+            act(nF, FF, AF.Copy, scale=-1.0)
+        if cnt.get("flip" + s) != flip:
+            cnt["flip" + s] = flip
+            ms(A("Fb" + s, sl(0, 128, 9)), 30000 if flip else -30000)
         for h, c in enumerate("ab" if off else ""):
             up = (c == "b") == flip
 
@@ -373,140 +396,146 @@ def build():
                 d = [A(buf, N_, j) if buf[0] == "Z" else A(buf, sl(j, n, 4)) for j in range(4)]
                 mn = [xs[j] + [(NI, d[j])] for j in range(4)]; mx = [ys[j] + [(ID, d[j])] for j in range(4)]
                 return (mx, mn) if up else (mn, mx)
-            lo, hi = layer([terms(8 * h + j) for j in range(4)], [terms(8 * h + 4 + j) for j in range(4)], "S0" + c + s)
+            lo, hi = layer([wire(2 * h + 4 * j) for j in range(4)], [wire(2 * h + 1 + 4 * j) for j in range(4)], "S0" + c + s)
             pw, sw = [lo[0], hi[1], lo[2], hi[3]], [lo[1], hi[0], lo[3], hi[2]]
             if off == 2:
-                lo, hi = layer(pw, sw, Zn + c)
-                pw, sw = [lo[0], lo[1], hi[2], hi[3]], [hi[0], hi[1], lo[2], lo[3]]
+                lo, hi = layer(pw, sw, "Z" + s + c)
+                pw, sw = [lo[0], lo[1], hi[2], hi[3]], [hi[0], lo[2], hi[1], lo[3]]
             t = tile()
             mm([(A(t, sl(j, n, 4)), sw[j]) for j in range(4)])
             if off == 1:
-                act(A(Zn + c, N_), A(t, sl(0, 4 * n)), AF.Identity)
+                act(A("Z" + s + c, N_), A(t, sl(0, 4 * n)), AF.Identity)
             else:
-                op("act", [("act", A(Qn + c, N_, (0, 4, 1, 5)[j]), A(t, sl(j, n, 4)), AF.Identity, 0.0, 1.0) for j in range(4)])
+                op("act", [("act", A("Q" + s + c, N_, slice(j, j + 5, 4)), A(t, sl(j, 2 * n, 2)), AF.Identity, 0.0, 1.0) for j in range(2)])
             P[c] = tile("p")
             mm([(A(P[c], N_, j), pw[j]) for j in range(4)])
         for h, c in enumerate("" if off else "ab"):
             P[c] = tile("p")
-            mm([(A(P[c], N_, j), terms(8 * h + j)) for j in range(4)])
-            t = tile()
-            mm([(A(t, sl(j, n, 4)), terms(8 * h + 4 + j)) for j in range(4)])
-            act(A("S0" + c + s, sl(0, 4 * n)), A(t, sl(0, 4 * n)), AF.Identity)
+            quad(P[c], n, whole(2 * h), lambda j: each(2 * h + 4 * j))
+            if not direct:
+                t = tile()
+                quad(t, n, whole(2 * h + 1), lambda j: each(2 * h + 1 + 4 * j))
+                act(A("S0" + c + s, sl(0, 4 * n)), A(t, sl(0, 4 * n)), AF.Identity)
         seq = {}
-        for c in "ab":
+        for h, c in enumerate("ab"):
             lo, hi = (OP.min, OP.max) if (c == "b") != flip else (OP.max, OP.min)
-            p = lambda a, b=None, st=1, c=c: A(P[c], N_, a if b is None else slice(a, b, st))
-            q = lambda a, b=None, st=1, c=c: A(Qn + c, N_, a if b is None else slice(a, b, st))
-            r = lambda a, b=None, st=1, c=c: A("R" + c, N_, a if b is None else slice(a, b, st))
-            f = lambda a, c=c: A("F" + c, sl(a, n, 9))
-            s0 = lambda a, c=c: A("S0" + c + s, sl(a, 2 * n, 2))
-            z = lambda a, b, st=1, c=c: A(Zn + c, N_, slice(a, b, st))
+            p = lambda a, b=None, st=1: A(P[c], N_, a if b is None else slice(a, b, st))
+            q = lambda a, b=None, st=1: A("Q" + s + c, N_, a if b is None else slice(a, b, st))
+            z = lambda a, b=None, st=1: A("Z" + s + c, N_, a if b is None else slice(a, b, st))
+            f = lambda a: A("F" + c + s, sl(a, n, 9))
+            s0 = lambda a, m: A(direct, sl(2 * h + 1 + 4 * a, m * n, 16 // m)) if direct else A("S0" + c + s, sl(a, m * n, 4 // m))
             seq[c] = [
-                (z(1, 4, 2), p(0, 4, 2), s0(0), hi), (z(0, 4, 2), p(1, 4, 2), s0(1), lo), (p(0, 4, 2), p(0, 4, 2), s0(0), lo), (p(1, 4, 2), p(1, 4, 2), s0(1), hi),
-                (q(0, 5, 4), p(0, 2), z(0, 2), hi), (q(1, 6, 4), p(2, 4), z(2, 4), lo), (p(0, 2), p(0, 2), z(0, 2), lo), (p(2, 4), p(2, 4), z(2, 4), hi),
-                (q(3), p(1), q(0), hi), (q(2), p(2), q(5), lo), (p(1), p(1), q(0), lo), (p(2), p(2), q(5), hi),
-                (r(0, 7, 3), p(0, 3), q(1, 4), hi), (f(8), p(3), q(4), hi), (f(1), p(0), q(1), lo), (p(1, 4), p(1, 4), q(2, 5), lo),
-                (r(4, 6), p(2, 4), r(0, 4, 3), lo), (p(2, 4), p(2, 4), r(0, 4, 3), hi),
-                (f(2), p(1), r(4), lo), (f(4), p(2), r(5), lo), (f(6), p(3), r(6), lo),
-                (f(3), p(1), r(4), hi), (f(5), p(2), r(5), hi), (f(7), p(3), r(6), hi)]
-        for x, y in zip(seq["a"][4 * off:], seq["b"][4 * off:]):
-            tt(*x); tt(*y)
+                ([(z(1, 4, 2), p(0, 4, 2), s0(0, 2), hi), (z(0, 4, 2), p(1, 4, 2), s0(1, 2), lo)],
+                 [(p(0, 4, 2), s0(0, 2), lo), (p(1, 4, 2), s0(1, 2), hi)]),
+                ([(q(0, 5, 4), p(0, 2), z(0, 2), hi), (q(1, 6, 4), p(2, 4), z(2, 4), lo)], [(p(0, 2), z(0, 2), lo), (p(2, 4), z(2, 4), hi)]),
+                ([(q(3), p(1), q(0), hi), (q(2), p(2), q(5), lo)], [(p(1), q(0), lo), (p(2), q(5), hi)]),
+                ([(z(0, 3), p(0, 3), q(1, 4), hi), (f(8), p(3), q(4), hi), (f(1), p(0), q(1), lo)], [(p(1, 4), q(2, 5), lo)]),
+                ([(q(0, 2), p(2, 4), z(0, 2), lo)], [(p(2, 4), z(0, 2), hi)]),
+                ([(f(2), p(1), q(0), lo), (f(4), p(2), q(1), lo), (f(6), p(3), z(2), lo),
+                  (f(3), p(1), q(0), hi), (f(5), p(2), q(1), hi), (f(7), p(3), z(2), hi)], [])]
+        for L in range(off, 6):
+            for c in "ab":
+                outs, stay = seq[c][L]
+                for x in outs:
+                    tt(*x)
+                for x in stay:
+                    tt(x[0], *x)
         n9 = sl(0, 9 * n)
         if flip:
-            op("dve", [("scan", A("FO" + s, n9), A("Fa", n9), A("Fb", n9), 30000.0, OP.min, OP.max)])
+            op("dve", [("scan", A("FO" + s, n9), A("Fa" + s, n9), A("Fb" + s, n9), 30000.0, OP.min, OP.max)])
         else:
-            op("dve", [("scan", A("FO" + s, n9), A("Fa", n9), A("Fb", n9), -30000.0, OP.max, OP.min)])
+            op("dve", [("scan", A("FO" + s, n9), A("Fa" + s, n9), A("Fb" + s, n9), -30000.0, OP.max, OP.min)])
         return A("FO" + s, sl(8, n, 9))
 
-    def staged(n, terms, fn):
-        per = min(16, 512 // n)
-        for k0 in range(0, 16, per):
-            m = min(per, 16 - k0); t = tile()
-            mm([(A(t, sl(j * n, n)), terms(k0 + j)) for j in range(m)])
-            fn(t, k0, m)
+    def plane(b0, k, n):
+        return A("AB", sl(16 * b0 + 4 * n * (k % 4) + k // 4, n, 4))
 
-    def badpass(eng, s, n):
-        for h in range(2):
-            a = A("AB" + s, sl(8 * n * h, 8 * n))
-            if eng == "dve":
-                ts(a, a, 8.5, OP.is_gt)
+    def misfits(b0, n, whole, each, bias, how):
+        for q in range(4):
+            t = tile(); a = A("AB", sl(16 * b0 + 4 * n * q, 4 * n))
+            quad(t, n, whole(q), lambda j: each)
+            if how == "d":
+                ts(a, A(t, sl(0, 4 * n)), 16 * ULP + bias, OP.add, 16 * ULP, OP.not_equal)
             else:
-                act(a, a, AF.Sign, bias=-8.5)
-        return 4.5 if eng == "dve" else -7.0
+                act(a, A(t, sl(0, 4 * n)), AF.Abs, bias=bias)
+                if q % 2:
+                    a = A("AB", sl(16 * b0 + 4 * n * (q - 1), 8 * n))
+                    ts(a, a, 8.5, OP.is_gt)
 
-    nchunk = [0]
+    nchunk = [0]; looks = []
 
-    def step1(u, segs):
+    def step1(u, segs, b0, keep=None, cap=None):
         s = str(nchunk[0] % 2); nchunk[0] += 1; cnt["tag"] = "c%d" % nchunk[0]
-        n = sum(m for _, m in segs); N_ = sl(0, n); G = "G" + s
-        win = A("XW", sl(XO, 1792)) if u != 1 else A("XW", sl(0, 2048))
+        n = sum(m for _, m in segs); N_ = sl(0, n); G = "G"; g0 = 16 * b0
+        win = A("XW", sl(XO, 1792))
         pos = []; j = 0
         for c0, m in segs:
             pos.append((c0, m, j)); j += m
         dyn = [x for x in pos if x[0] < 0]
         for c0, m, j in pos:
-            act(A(G, sl(16 * j, 16 * m)), IND(win, A("TRu", sl(c0, m)) if c0 >= 0 else A("TD", sl(0, m))), AF.Identity)
+            looks.append(act(A(G, sl(g0 + 16 * j, 16 * m)), IND(win, A("TRu", sl(c0, m)) if c0 >= 0 else A("TD", sl(0, m))), AF.Identity))
         if len(segs) > 1:
             for c0, m, j in pos:
                 if c0 >= 0:
-                    act(A("OG", sl(16 * j, 16 * m)), A("OB", sl(16 * c0, 16 * m)), AF.Identity)
+                    act(A("W2b", sl(16 * j, 16 * m)), A("OB", sl(16 * c0, 16 * m)), AF.Identity)
         for c0, m, j in dyn:
-            act(A("OG", sl(16 * j, 16 * m)), IND(A("OB"), A("OP_", sl(0, m))), AF.Identity)
-        ob, o0 = ("OG", 0) if dyn else ("OB", 16 * segs[0][0])
-        gk = lambda k: A(G, sl(k, n, 16))
-        ok = lambda k: A(ob, sl(o0 + k, n, 16))
-        un, FF, ft, gd, MM = (A(x + s, N_) for x in ("un", "FF", "ft", "gd", "MM"))
-        dg = A("DG" if len(segs) > 1 else "DGl", N_)
-        if dyn:
-            if len(segs) > 1:
-                ms(dg, 0)
-                for c0, m, j in dyn:
-                    cp(A("DG", sl(j, m)), A("DGl", sl(0, m)))
+            act(A("W2b", sl(16 * j, 16 * m)), IND(A("OB"), A("OP_", sl(0, m))), AF.Identity)
+        ob, o0 = ("W2b", 0) if dyn else ("OB", 16 * segs[0][0])
+        gk = lambda k: A(G, sl(g0 + k, n, 16))
+        un, FF, ft, MM = (A(x, sl(b0, n)) for x in ("un", "FF", "ft", "MM"))
+        dg = A("DG" if len(segs) > 1 or keep else "DGl", N_); old = dyn or keep
+        if keep:
+            cp(dg, A("DD", sl(CD + segs[0][0], n)))
+        elif dyn and len(segs) > 1:
+            ms(dg, 0)
+            for c0, m, j in dyn:
+                cp(A("DG", sl(j, m)), A("DGl", sl(0, m)))
         if u > 0:
             t = tile()
-            mm([(A(t, N_), [(SUMk(k), gk(k)) for k in range(16)] + ([(ID, dg)] if dyn else []))])
+            mm([(A(t, N_), [(SUMk(k), gk(k)) for k in range(16)] + ([(ID, dg)] if old else []))])
             ts(un, A(t, N_), 4095.0, OP.is_gt, 64.0, OP.mult)
             t = tile()
             mm([(A(t, N_), [(A("WL"), un)])])
             ts(FF, A(t, N_), 63.5 * 64, OP.is_gt, -16384.0, OP.mult)
-            if dyn:
+            if old:
                 tt(FF, FF, dg, OP.add)
-        P = median(n, s, lambda k: [(ID, gk(k)), (NI, ok(k))] + ([(BCk(k), FF)] if u > 0 else []))
-
-        def after(t, k0, m):
-            act(A("RR" + s, sl(k0 * n, m * n)), A(t, sl(0, m * n)), AF.Relu, bias=255.0, scale=-1.0)
-        staged(n, lambda k: [(ID, P), (ID, ok(k)), (NI, gk(k))], lambda t, k0, m: act(A("AB" + s, sl(k0 * n, m * n)), A(t, sl(0, m * n)), AF.Abs))
-        staged(n, lambda k: [(ID, P), (ID, ok(k))], after)
-        th = badpass(CFG["bad1"], s, n)
-        t = tile()
-        mm([(A(t, N_), [(SUMk(k), A("AB" + s, sl(k * n, n))) for k in range(16)] + ([(ID, un)] if u > 0 else []))])
+        g4 = lambda q: A(G, sl(g0 + q, 4 * n, 4))
+        o4 = lambda q: A(ob, sl(o0 + q, 4 * n, 4))
+        P = median(n, s, [(ID, G, g0), (NI, ob, o0)], FF if u > 0 else None)
+        misfits(b0, n, lambda q: [(ID, o4(q)), (NI, g4(q))], [(ID, P)], 0.0, CFG["fit"][nchunk[0] - 1])
+        for q in range(4):
+            t = tile()
+            quad(t, n, [(ID, o4(q))], lambda j: [(ID, P)] + ([(ID, keep)] if keep else []))
+            act(A("RR", sl(g0 + 4 * n * q, 4 * n)), A(t, sl(0, 4 * n)), AF.Relu, bias=255.0, scale=-1.0)
+        t = tile(); th = 4.5
+        mm([(A(t, N_), [(SUMk(k), plane(b0, k, n)) for k in range(16)] + ([(ID, un)] if u > 0 else []))])
         ts(ft, A(t, N_), th, OP.is_lt, 64.0, OP.mult)
         t = tile(); H = lambda j: A("H17", sl(128 * j, 128))
         e1 = [(H(3), un)] if u > 0 else []; e2 = [(H(2), un)] if u > 0 else []
-        mm([(A(t, N_), [(H(0), ft)] + e2 + ([(NI, dg)] if dyn else [])), (A(t, sl(128, n)), [(H(1), ft)] + e1)])
+        mm([(A(t, N_), [(H(0), ft)] + e2 + ([(NI, dg)] if old else []))] + ([] if keep else [(A(t, sl(128, n)), [(H(1), ft)] + e1)]))
         ts(MM, A(t, N_), 22.5 * 64, OP.is_lt, 32768.0, OP.mult)
-        for c0, m, j in pos:
-            if c0 >= 0 and u == 0:
-                ts(A("DD", sl(CD + c0, m)), A(t, sl(128 + j, m)), 5.5 * 64, OP.is_gt, 8192.0, OP.mult)
-            elif c0 >= 0:
-                ts(A("FF" + s, sl(0, m)), A(t, sl(128 + j, m)), 5.5 * 64, OP.is_gt, 8192.0, OP.mult)
-                cp(A("DD", sl(CD + c0, m)), A("FF" + s, sl(0, m)))
+        if keep:
+            tt(MM, MM, cap, OP.min)
+        for c0, m, j in [] if keep else pos:
+            if c0 >= 0:
+                ts(A("DD", sl(CD + c0, m)), A(t, sl(128 + j, m)), 5.5 * 64, OP.is_gt, EMPTY, OP.mult)
             else:
-                ts(A("DN", sl(0, m)), A(t, sl(128 + j, m)), 5.5 * 64, OP.is_gt, 8192.0, OP.mult)
+                ts(A("DN", sl(0, m)), A(t, sl(128 + j, m)), 5.5 * 64, OP.is_gt, EMPTY, OP.mult)
                 tt(A("DN", sl(0, m)), A("DN", sl(0, m)), A("DGl", sl(0, m)), OP.max)
                 cp(IND(A("DD"), A("OC", sl(0, m // 16))), A("DN", sl(0, m)))
 
-        for c0, m, j in pos:
-            for a in range(0, m, 32):
-                z = min(32, m - a); t = tile()
-                mm([(A(t, sl(k, z, 16)), [(NI, A("RR" + s, sl(k * n + j + a, z))), (BCk(k), A("MM" + s, sl(j + a, z)))]) for k in range(16)])
-                act(A("BW", sl(BO + 16 * (c0 + a), 16 * z)) if c0 >= 0 else A("BT", sl(16 * a, 16 * z)), A(t, sl(0, 16 * z)), AF.Relu, bias=255.0)
-                if c0 < 0:
-                    cp(IND(A("BW", sl(BD, BG0 - BD)), A("PP", sl(a, z))), A("BT", sl(16 * a, 16 * z)))
+        for q in range(4):
+            t = tile()
+            quad(t, n, [(NI, A("RR", sl(g0 + 4 * n * q, 4 * n)))] + ([(ID, A("BW", sl(BO + q, 4 * n, 4)))] if keep else []),
+                 lambda j: [(BCk(q + 4 * j), MM)])
+            for c0, m, j in pos:
+                act(A("BW", sl(BO + 16 * c0 + q, 4 * m, 4)) if c0 >= 0 else A("W2b", sl(2048 + q, 4 * m, 4)), A(t, sl(4 * j, 4 * m)), AF.Relu, bias=255.0)
+        for c0, m, j in dyn:
+            cp(IND(A("BW", sl(BD, BG - BD)), A("PP", sl(0, m))), A("W2b", sl(2048, 16 * m)))
 
-    def camlist(u):
+    def camlist(u, new):
         K = 16 if u == 1 else CD
-        worklist("FC", [10, 21] if u == 1 else [20, 21] + list(range(20)), K, CD, "OC")
+        worklist("FC", [10, 21] if u == 1 else [20, 21] + list(range(20)), K, CD, "OC", new, 0.5)
         ms(A("FC", sl(11, 10)) if u == 1 else A("FC", sl(22, 6)), 0)
         k_ = sl(0, K); oc = A("OC", sl(0, K // 16))
         cp(A("DGl", k_), IND(A("DD"), oc))
@@ -514,11 +543,7 @@ def build():
         ts(A("tD", k_), A("Li", k_), 16.0, OP.mult, PK, OP.add)
         cp(A("PP", k_), A("tD", k_))
         ts(A("OP_", k_), A("tD", k_), -1280.0, OP.add, 0.0, OP.max)
-        if u == 1:
-            cp(A("tD", k_), IND(A("TRW"), oc))
-            odd_tr(A("TD", k_), A("tD", k_), A("tD2", k_), K)
-        else:
-            cp(A("TD", k_), IND(A("TRW"), oc))
+        cp(A("TD", k_), IND(A("CTi"), oc))
         tt(A("tD2", k_), IND(A("EW"), oc), A("J1", k_), OP.min)
         cp(A("ED", k_), A("tD2", k_))
         for a in range(0, K, 16):
@@ -527,138 +552,154 @@ def build():
     def tracklist(u):
         t = tile()
         for r in range(0, 16, 2):
-            mm([(A(t, sl(0, 56)), [(SUMk(r + q), A("W1", sl(16 * (r + q) + s_, 56, 256))) for q in range(2) for s_ in range(16)],
-                 "<" if r == 0 else ">" if r == 14 else "")])
-        ts(A("FR"), A(t, sl(0, 56)), 16.0 * 32 ** u - 0.5, OP.is_gt)
-        tt(A("FT"), A("FT"), A("FR"), OP.max)
-        worklist("FT", [(12 * u + j) % 56 for j in range(56)], 256, 256, "OT")
+            mm([(A(t, sl(0, 56)), [(SUMk(r + q), A("W1", sl(16 * (r + q) + s_, 56, 256))) for q in range(2) for s_ in range(16)]
+                 + ([(ID, A("FQ"))] if r == 0 else []), "<" if r == 0 else ">" if r == 14 else "")])
+        worklist("FT", [(12 * u + j) % 56 for j in range(56)], 256, 256, "OT", lambda c, m: A(t, sl(c, m)), 16.0 * 32 ** u - 0.5)
+        if u < 2:
+            act(A("FQ"), A("FT"), AF.Copy, scale=32768.0)
 
-    xw = A("XW", sl(XD, XG0 - XD))
+    xw = A("XW", sl(XD, XG - XD))
 
     def views(u):
         v, w, w2 = A("v"), A("w"), A("w2")
         act(v, IND(A("TVW"), A("OT")), AF.Identity)
-        if u != 1:
-            ts(A("vo"), v, 8064.0, OP.min)
-        else:
-            ts(w, v, 7167.5, OP.is_gt, -9360.0, OP.mult)
-            ts(w2, v, 8064.0, OP.min, 2192.0, OP.add)
-            tt(w, w, w2, OP.add)
-            cp(A("vo"), w)
+        ts(A("vo"), v, 8064.0, OP.min)
         for h in range(2):
             tt(A("w2", sl(128 * h, 128)), A("v", sl(128 * h, 128)), A("J2"), OP.min)
         cp(A("wo"), w2)
+        cp(A("OU", sl(1, 16)), A("OT"))
         act(A("xo"), IND(xw, A("OT")), AF.Identity)
 
-    def step2(u, j0, n, ondve):
+    def step2(u, j0, n, ondve, off):
         s = str(nchunk[0] % 2); nchunk[0] += 1; cnt["tag"] = "c%d" % nchunk[0]
-        N_ = sl(0, n); G = "G" + s; ot = A("OT", sl(j0 // 16, n // 16))
-        un, FF, xn, nh, ne = (A(x + s, N_) for x in ("un", "FF", "ft", "gd", "MM"))
-        w, w2, xo = (A(x, sl(j0, n)) for x in ("w", "w2", "xo"))
-        win = A("BW", sl(BO, BE - BO)) if u != 1 else A("BW", sl(0, BG0))
+        N_ = sl(0, n); G = "G"; g0 = 16 * j0; ot = A("OU", sl(j0 // 16 + 1, n // 16)) if j0 % 32 else A("OT", sl(j0 // 16, n // 16))
+        un, FF, nF, xn, nh, ne, w, w2, xo = (A(x, sl(j0, n)) for x in ("un", "FF", "nF", "ft", "gd", "MM", "w", "w2", "xo"))
+        win = A("BW", sl(BO, BE - BO))
         for h in range(0, n, 64):
             m = min(64, n - h)
-            act(A(G, sl(16 * h, 16 * m)), IND(win, A("vo", sl(j0 + h, m))), AF.Relu, bias=256.0, scale=-1.0)
-        gk = lambda k: A(G, sl(k, n, 16))
+            act(A(G, sl(g0 + 16 * h, 16 * m)), IND(win, A("vo", sl(j0 + h, m))), AF.Relu, bias=256.0, scale=-1.0)
+        gk = lambda k: A(G, sl(g0 + k, n, 16))
         t = tile()
         mm([(A(t, N_), [(SUMk(k), gk(k)) for k in range(16)])])
-        ts(un, A(t, N_), 0.5, OP.is_lt, 64.0, OP.mult)
-        t = tile(); off = CFG["off"][j0 > 0]; nF, ym = A("nF" + s, N_), A("ym" + s, N_)
-        mm([(A(t, N_), [(A("WL"), un)]), (A(t, sl(128, n)), [(ONES, un)])])
-        ts(FF, A(t, N_), 63.5 * 64, OP.is_gt, 256.0, OP.mult)
-        if off:
-            act(nF, FF, AF.Copy, scale=-1.0)
-        ts(nh, A(t, sl(128, n)), 13.5 * 64, OP.is_gt, 512.0, OP.mult)
-
-        def neg(ts_):
-            return [(NI, r) if l is ID else (ID, r) if l is NI else (l, nF if r is FF else FF) for l, r in ts_]
-        m_ = median(n, s, lambda k: [(ID, gk(k)), (BCk(k), FF)], True, off, neg)
-        ts(ym, m_, -1.0, OP.mult, 256.0, OP.add)
-        tt(xn, ym, nh, OP.max)
-        cnt["xn"] = cp(IND(xw, ot), xn)
-        tt(ne, xn, xo, OP.not_equal)
-        staged(n, lambda k: [(ID, gk(k)), (NI, m_)], lambda t, k0, m: act(A("AB" + s, sl(k0 * n, m * n)), A(t, sl(0, m * n)), AF.Abs))
-        th = badpass(CFG["bad2"], s, n)
+        if "u" in CFG["onact"]:
+            act(un, A(t, N_), AF.Relu, bias=64.0, scale=-4.0)
+        else:
+            ts(un, A(t, N_), 0.5, OP.is_lt, 64.0, OP.mult)
         t = tile()
-        mm([(A(t, N_), [(SUMk(k), A("AB" + s, sl(k * n, n))) for k in range(16)] + [(NI, un), (NI, nh)]), (A(t, sl(128, n)), [(ONES, ne)])])
+        mm([(A(t, N_), [(A("WL"), un)])])
+        ts(FF, A(t, N_), 63.5 * 64, OP.is_gt, 256.0, OP.mult)
+        t = tile()
+        mm([(A(t, N_), [(ONES, un)])])
+        if "h" in CFG["onact"]:
+            act(nh, A(t, N_), AF.Relu, bias=-13.0 * 512, scale=8.0)
+        else:
+            ts(nh, A(t, N_), 13.5 * 64, OP.is_gt, 512.0, OP.mult)
+        g4 = lambda q: A(G, sl(g0 + q, 4 * n, 4))
+        m_ = median(n, s, [(ID, G, g0)], FF, True, off, nF=nF)
+        t = tile()
+        mm([(A(t, N_), [(ID, nh), (NI, m_)])])
+        ts(xn, A(t, N_), 256.0, OP.add, 512.0, OP.min)
+        cnt["xn"] = cp(IND(xw, ot), xn)
+        if "n" in CFG["onact"]:
+            t = tile()
+            mm([(A(t, N_), [(ID, xn), (NI, xo)])])
+            act(ne, A(t, N_), AF.Abs)
+        else:
+            tt(ne, xn, xo, OP.not_equal)
+        misfits(j0, n, lambda q: [(ID, g4(q))], [(ID, xn)], -256.0, CFG["fit"][nchunk[0] - 1])
+        t = tile(); th = 4.5
+        mm([(A(t, N_), [(SUMk(k), plane(j0, k, n)) for k in range(16)] + [(NI, un), (NI, nh)]), (A(t, sl(128, n)), [(ONES, ne)])])
         ts(w, A(t, N_), th, OP.is_gt, EMPTY, OP.mult)
-        ts(w2, A(t, sl(128, n)), 0.5, OP.is_gt, 64.0 * (u + 1), OP.mult)
+        ts(w2, A(t, sl(128, n)), 0.5, OP.is_gt, 64.0 * 2 ** u, OP.mult)
         if ondve:
             tt(ne, w2, w, OP.add)
             for k0 in range(0, 16, 8):
-                op("dve", [("ts", A("RR" + s, sl(k, n, 16)), ne, A("DK", sl(k, 1)), None, OP.mult, None) for k in range(k0, k0 + 8)])
+                op("dve", [("ts", A("RR", sl(g0 + k, n, 16)), ne, A("DK", sl(k, 1)), None, OP.mult, None) for k in range(k0, k0 + 8)])
             for h in range(0, n, 32):
-                cp(IND(A("W1", sl(0, W2N)), A("wo", sl(j0 + h, 32))), A("RR" + s, sl(16 * h, 512)))
+                m = min(32, n - h)
+                cp(IND(A("W3"), A("wo", sl(j0 + h, m))), A("RR", sl(g0 + 16 * h, 16 * m)))
             return
         tt(w2, w2, w, OP.add)
         for k0 in range(0, 16, 4):
-            if CFG["spass"][0 if j0 == 0 else 2 if j0 + n == 256 else 1] == "a":
-                op("act", [("act", A("SS", sl(k, n, 16)), w2, AF.Copy, 0.0, A("DK", sl(k, 1))) for k in range(k0, k0 + 4)])
-            else:
-                op("dve", [("ts", A("SS", sl(k, n, 16)), w2, A("DK", sl(k, 1)), None, OP.mult, None) for k in range(k0, k0 + 4)])
-        for h in range(0, n, 16):
-            if (j0 + h) // 16 in CFG["kd"]:
-                cp(IND(A("W2"), A("wo", sl(j0 + h, 16))), A("SS", sl(16 * h, 256)))
-            else:
-                act(IND(A("W2"), A("wo", sl(j0 + h, 16))), A("SS", sl(16 * h, 256)), AF.Silu)
+            op("act", [("act", A("SS", sl(g0 + k, n, 16)), w2, AF.Copy, 0.0, A("DK", sl(k, 1))) for k in range(k0, k0 + 4)])
+        for h in range(0, n, 32):
+            m = min(32, n - h)
+            act(IND(A("W2"), A("wo", sl(j0 + h, m))), A("SS", sl(g0 + 16 * h, 16 * m)), AF.Silu)
 
     def decode(u):
-        nc = (176, 352, 448)[u]
-        for c0 in range(0, nc, 112):
-            m = min(112, nc - c0); C_ = sl(c0, m)
-            wb = 1792 * (c0 // 112 % 2)
-            if CFG["conv"][u][c0 // 112] == "a":
-                act(A("W2b", sl(wb, 16 * m)), A("W2", sl(16 * c0, 16 * m)), AF.Identity)
-            elif CFG["conv"][u][c0 // 112] == "d":
-                cp(A("W2b", sl(wb, 16 * m)), A("W2", sl(16 * c0, 16 * m)))
-            else:
-                dma(A("W2b", sl(wb, 16 * m)), A("W2", sl(16 * c0, 16 * m)), "gp", 2500.0 + 20 * m)
-            t = tile()
-            mm([(A(t, sl(0, m)), [(SUMk(k), A("W2b", sl(wb + k, m, 16))) for k in range(16)]
-                 + ([(SUMk(k), A("W1", sl(16 * c0 + k, m, 16))) for k in range(16)] if u == 2 and CFG["tail"] else []))])
-            ts(A("KL", C_), A(t, sl(0, m)), 4096.0, OP.is_gt, 8192.0, OP.mult)
-            act(A("tmpB", C_), A(t, sl(0, m)), AF.Abs, bias=A("PF", sl(8 + u, 1)))
-            tt(A("DD", sl(CD + c0, m)), A("DD", sl(CD + c0, m)), A("KL", C_), OP.max)
-            ts(A("EQ", C_), A("tmpB", C_), 8064.0, OP.is_equal)
-        t = tile(); a = nc // 16
-        mm([(A(t, sl(0, a)), [(SUMk(r), A("EQ", sl(r, a, 16))) for r in range(16)])])
-        ts(A("FR", sl(0, a)), A(t, sl(0, a)), 0.5, OP.is_gt)
-        tt(A("FC", sl(0, a)), A("FC", sl(0, a)), A("FR", sl(0, a)), OP.max)
+        nc = (176, 352, 448)[u]; bl = CFG["blocks"][u]; wb = 0; who = list(CFG["conv"][u])
+        for c0, m in zip(bl[::2], bl[1::2]):
+            C_ = sl(c0, m); wb = wb if wb + 16 * m <= 3584 else 0
+            for h in range(0, 16 * m, 896):
+                z = min(896, 16 * m - h); a, b = A("W2b", sl(wb + h, z)), A("W2", sl(16 * c0 + h, z)); e = who.pop(0)
+                if e == "a":
+                    act(a, b, AF.Identity)
+                elif e == "d":
+                    cp(a, b)
+                else:
+                    op("gp", [("sel", a, b)])
+            t = tile(); dd = A("DD", sl(CD + c0, m))
+            mm([(A(t, sl(0, m)), [(ID, dd)] + [(SUMk(k), A("W2b", sl(wb + k, m, 16))) for k in range(16)], "<")])
+            mm([(A(t, sl(0, m)), [(SUMk(k), A("W3", sl(16 * c0 + k, m, 16))) for k in range(16)], ">")])
+            wb += 16 * m; ch = 64.0 * 2 ** u
+            act(A("tmpB", C_), A(t, sl(0, m)), AF.Abs, bias=-EMPTY / 2 - 1.5 * ch)
+            ts(dd, A(t, sl(0, m)), 4096.0, OP.is_gt, EMPTY, OP.mult)
+            ts(A("EQ", C_), A("tmpB", C_), ch * ULP - EMPTY / 2, OP.add, ch * ULP, OP.is_equal)
 
-    def kill_border():
-        for c0, m in ((0, 32), (32, 24)):
-            t = tile()
-            mm([(A(t, sl(k, m, 16)), [(ID, A("BW", sl(BO + 16 * c0 + k, m, 16))), (BCk(k), A("DD", sl(CD + c0, m)))]) for k in range(16)])
-            act(A("BW", sl(BO + 16 * c0, 16 * m)), A(t, sl(0, 16 * m)), AF.Identity)
+        def flags(t, c0, a):
+            return A(t, sl(c0, a)), [(ID, A("FC", sl(c0, a)))] + [(SUMk(r), A("EQ", sl(16 * c0 + r, a, 16))) for r in range(16)]
+        t = tile()
+        if u == 0:
+            mm([flags(t, 10, 1), (A(t, sl(21, 1)), [(ID, A("FC", sl(21, 1)))])])
+            t2 = tile()
+            mm([flags(t2, 0, 10)])
+            ts(A("FC", sl(0, 10)), A(t2, sl(0, 10)), 0.5, OP.is_gt)
+        else:
+            mm([flags(t, 0, nc // 16)])
+        return lambda c, m: A(t, sl(c, m))
 
-    for u in range(3):
-        ms(A("PF", sl(8 + u, 1)), -(8064 + 64 * (u + 1)))
+    def kill_border(keep=None):
+        for q in range(4):
+            t = tile(); b = A("BW", sl(BO + q, 224, 4))
+            quad(t, 56, [(ID, b)], lambda j: [(BCk(q + 4 * j), A("DD", sl(CD, 56)))] + ([(ID, keep)] if keep else []))
+            act(b, A(t, sl(0, 224)), AF.Relu, bias=-65536.0 if keep else 0.0)
+
     ms(A("FC", sl(0, 11)), 0)
     flag_static(0, 0, 176)
     for u in range(3):
         cnt["tag"] = "k%d" % u
+        border = u == 2 and CFG["border"]
         if u:
-            decode(u - 1); kill_border(); camlist(u)
+            new = decode(u - 1)
+            if not border:
+                kill_border()
+            camlist(u, new)
             if u == 1:
-                exchange(3, "BW", BO, "SB", BG1)
+                came = cnt["arr"]; sent = exchange(3, "BW", BO, BG); ops[sent]["deps"][came] = False
+        if border:
+            t = tile(); keep, cap = A("EX", sl(0, 56)), A("EX", sl(64, 56))
+            mm([(A(t, sl(r, 4, 16)), [(BCk(r), A("SEL", sl(2, 4)))]) for r in range(16)])
+            ts(keep, A(t, sl(0, 56)), -65536.0, OP.mult, 65536.0, OP.add)
+            ts(cap, A(t, sl(0, 56)), 65791.0, OP.mult, -255.0, OP.add)
+            kill_border(keep)
+            step1(u, [(0, 56)], 176, keep, cap)
+            sent = exchange(5, "BW", BO, BG)
         cnt["tag"] = "t%d" % u
         tracklist(u)
         views(u)
-        if u == 2 and CFG["tail"]:
-            for h in range(8):
-                iota(A("W2", sl(896 * h, 896)), [[0, 896]], 0, 0)
+        j0 = 0
         for ci, segs in enumerate(CFG["s1"][u]):
             dyn = any(c0 < 0 for c0, m in segs)
-            step1(u, segs)
+            step1(u, segs, j0); j0 += sum(m for c0, m in segs)
             if u == 0 and ci == 0:
-                exchange(1, "BW", BO, "SB", BG0)
-            if u == 2 and dyn:
-                sent = exchange(5, "BW", BO, "SB", BG0)
-                for h in range(8 if CFG["tail"] else 0):
-                    ops[iota(A("W1", sl(896 * h, 896)), [[0, 896]], 0, 0)]["deps"].setdefault(sent, False)
+                sent = exchange(1, "BW", BO, BG)
+            if u == 2 and dyn and not border:
+                exchange(5, "BW", BO, BG)
+        for i in looks if u < 2 else []:
+            ops[sent]["deps"].setdefault(i, False)
         j0 = 0
-        for n in CFG["s2"][u]:
-            step2(u, j0, n, u == 2 and CFG["tail"] and j0 + n == 256); j0 += n
+        for n, off in zip(CFG["s2"][u], CFG["off2"][u]):
+            step2(u, j0, n, j0 >= CFG["ondve"][u], off); j0 += n
         tt(IND(A("TVW"), A("OT")), A("v"), A("w"), OP.max)
         cnt["tag"] = "f%d" % u
         if u < 2:
@@ -666,144 +707,173 @@ def build():
             for i in fs[len(fs) - CFG["hold"][u]:]:
                 ops[i]["deps"].setdefault(cnt["xn"], False)
         if u < 2:
-            exchange(2 * u + 2, "XW", XO, "SX", XG1 if u == 0 else XG0)
+            exchange(2 * u + 2, "XW", XO, XG)
     P8 = slice(0, 8); cnt["tag"] = "z"
     dma(A("yx"), A("XW", sl(XO, NT)))
-    ts(A("SX"), A("TVW", sl(256, NT)), 8064.0, OP.is_lt)
+    ts(A("AB", sl(0, NT)), A("TVW", sl(256, NT)), 8064.0, OP.is_lt)
     ts(A("FR"), A("FT"), 32.0, OP.mult)
     for h in range(2):
         t = tile()
-        mm([(A(t, sl(r, 28, 16), p=P8), [(A("ONES", sl(0, 8, 16)), A("SX", sl(448 * h + r, 28, 16))),
-                                         (A("BC", sl(128 * r, 8, 16)), A("FR", sl(28 * h, 28)))]) for r in range(16)])
+        mm([(A(t, sl(r, 28, 16), p=P8), [(A("O8"), A("AB", sl(448 * h + r, 28, 16))),
+                                         (A("PX", sl(r, 8, 16)), A("FR", sl(28 * h, 28)))]) for r in range(16)])
         act(A("IDS", sl(448 * h, 448), p=P8), A(t, sl(0, 448), p=P8), AF.Identity)
-    dma(A("yt"), A("IDS", p=P8))
-    decode(2)
+    dma(A("yt"), A("IDS", p=P8), xor=False)
+    ts(A("FQ", sl(0, 28)), decode(2)(0, 28), 0.5, OP.is_gt, 32.0, OP.mult)
+    t = tile(); dx = A("EX", sl(0, 112))
+    mm([(A(t, sl(0, 112)), [(PX, A("DD", sl(CD + 336, 112)))])])
+    cp(dx, A(t, sl(0, 112)))
     for q in range(4):
-        c0 = 336 + 32 * q; m = min(32, 448 - c0); t = tile()
-        mm([(A(t, sl(k, m, 16)), [(ID, A("BW", sl(BO + 5376 + 512 * q + k, m, 16))), (BCk(k), A("DD", sl(CD + c0, m)))]) for k in range(16)])
-        ts(A("RR1", sl(512 * q, 16 * m)), A(t, sl(0, 16 * m)), 512.0, OP.min)
-    dma(A("yb"), A("RR1", sl(0, 1792)))
-    ts(A("EQ"), A("DD", sl(CD, NC)), 1.0, OP.is_lt)
-    ts(A("FR", sl(0, 28)), A("FC"), 32.0, OP.mult)
+        t = tile()
+        quad(t, 112, [(PX, A("BW", sl(BO + 5376 + q, 448, 4)))], lambda j: [(BCk(q + 4 * j), dx)])
+        ts(A("G", sl(q, 448, 4)), A(t, sl(0, 448)), 512.0, OP.min)
+    dma(A("yb"), A("G", sl(0, 1792)), xor=False)
+    ts(A("AB", sl(1024, NC)), A("DD", sl(CD, NC)), 1.0, OP.is_lt)
     t = tile()
-    mm([(A(t, sl(r, 28, 16), p=P8), [(A("ONES", sl(0, 8, 16)), A("EQ", sl(r, 28, 16))),
-                                     (A("BC", sl(128 * r, 8, 16)), A("FR", sl(0, 28)))]) for r in range(16)])
+    mm([(A(t, sl(r, 28, 16), p=P8), [(A("O8"), A("AB", sl(1024 + r, 28, 16))), (A("PX", sl(r, 8, 16)), A("FQ", sl(0, 28)))]) for r in range(16)])
     act(A("tmpB", p=P8), A(t, sl(0, 448), p=P8), AF.Identity)
-    dma(A("yc"), A("tmpB", p=P8))
+    dma(A("yc"), A("tmpB", p=P8), "act", xor=False)
     return ops
 
 
-WAKE = 180.0
-URGE = {'c6aS0b': -6, 'c14aZ1a': 20, 'ig': 20, 'c5aG0': 6, 't2': 20, 'c9dRa': -20, 'iaSX': 20, 'c14dFa': -20, 'idtE': 20, 'c12dRb': -20, 't2pk': 20,
-        'c1dp': 20, 'c6aG1': 20, 'c3aW2s': -20, 'c9aAB0': 20, 'igW1': -20, 'c4dFb': -6, 'c3aG0': 20, 'c1aRR0': -6, 'c1aAB0': 20, 'c6pp': -6,
-        'c3dFb': 20, 'c10aW2s': 20, 'c5dp': -6, 'c9aS0b': 20, 'c13dFa': 20, 'c15aAB0': 20}
-
-
-def backward(ops, deps, fin):
-    n = len(ops); ns = [0] * n; rt = [0.0] * n; et = {}; out = [0.0] * n
+def forward(E, cost, pre, post, npred, succ, prio, tiles, users):
+    n = len(E); nd = list(npred); rt = list(pre); start = [0.0] * n; fin = [0.0] * n
+    ready = {e: [] for e in sorted(set(E))}; et = {e: 0.0 for e in ready}
     for i in range(n):
-        for j in deps[i]:
-            ns[j] += 1
-    ready = [i for i in range(n) if ns[i] == 0]
-    while ready:
-        cand = [(max(rt[i] + ops[i]["lat"], et.get(ops[i]["e"], 0.0)), i) for i in ready]
-        m, i0 = min(cand)
-        st, i = max([c for c in cand if c[0] <= m + CFG["win"] and ops[c[1]]["e"] == ops[i0]["e"]], key=lambda c: fin[c[1]])
-        out[i] = et[ops[i]["e"]] = st + ops[i]["cost"]; ready.remove(i)
-        for j in deps[i]:
-            rt[j] = max(rt[j], out[i] + WAKE); ns[j] -= 1
-            if ns[j] == 0:
-                ready.append(j)
-    return out
-
-
-def schedule(ops, rounds=8):
-    n = len(ops); base = [dict(o["deps"]) for o in ops]; prio = [0.0] * n
-    for i in range(n - 1, -1, -1):
-        prio[i] += ops[i]["cost"] + ops[i]["lat"]
-        for j in base[i]:
-            prio[j] = max(prio[j], prio[i] + WAKE)
-    best = None
-    for r in range(rounds):
-        for o, b in zip(ops, base):
-            o["deps"] = dict(b)
-        res = forward(ops, [x + (1e5 if o["sem"] else 0) + 1e3 * URGE.get(o["tag"], 0) + 1e3 * URGE.get(o["tag"][:2], 0) for x, o in zip(prio, ops)])
-        if best is None or max(res[3]) < max(best[0][3]):
-            best = (res, [o["deps"] for o in ops])
-        prio = backward(ops, base, res[3])
-    for o, b in zip(ops, best[1]):
-        o["deps"] = b
-    return best[0]
-
-
-def forward(ops, prio):
-    n = len(ops); succ = [[] for _ in range(n)]
-    for i, o in enumerate(ops):
-        for j in o["deps"]:
-            succ[j].append(i)
-    users = {}
-    for i, o in enumerate(ops):
-        for t in o["tiles"]:
-            users.setdefault(t, []).append(i)
-    left = {t: len(v) for t, v in users.items()}
-    free = {"p": [["P%d" % i, None] for i in range(NPB)], "k": [["K%d" % i, None] for i in range(8 - NPB)]}
-    bank = {}; fin = [0.0] * n; start = [0.0] * n; etime = {}; order = []
-    nd = [len(o["deps"]) for o in ops]; ready = [i for i in range(n) if nd[i] == 0]; rt = [0.0] * n
-
-    def tend(t):
-        return max(fin[j] for j in users[t]) + WAKE if t else 0.0
-    while ready:
-        cand = []
-        for i in ready:
-            o = ops[i]; st = max(rt[i], etime.get(o["e"], 0.0)); pick = None
-            new = [t for t in o["tiles"] if t not in bank]
-            if new:
-                fl = free[new[0][0]]
-                if not fl:
-                    continue
-                pick = min(fl, key=lambda b: tend(b[1])); st = max(st, tend(pick[1]))
-            cand.append((st, i, pick, new))
-        m = min(c[0] for c in cand)
-        e0 = [c for c in cand if c[0] == m][0]
-        st, i, pick, new = max([c for c in cand if c[0] <= m + CFG["win"] and ops[c[1]]["e"] == ops[e0[1]]["e"]], key=lambda c: prio[c[1]])
-        o = ops[i]
-        if pick:
-            free[new[0][0]].remove(pick); bank[new[0]] = pick[0]
-            for j in (users[pick[1]] if pick[1] else []):
-                o["deps"].setdefault(j, False)
-        start[i] = st; etime[o["e"]] = st + o["cost"]; fin[i] = st + o["cost"] + o["lat"]
-        order.append(i); ready.remove(i)
-        for t in o["tiles"]:
-            left[t] -= 1
-            if left[t] == 0:
-                free[t[0]].append([bank[t], t])
-        for j in succ[i]:
-            same = ops[j]["e"] == o["e"] == "pe" and not ops[j]["deps"][i]
-            rt[j] = max(rt[j], fin[i] + (0.0 if same else WAKE)); nd[j] -= 1
+        if nd[i] == 0:
+            ready[E[i]].append(i)
+    bank = {}; extra = {}; order = []; left = {t: len(v) for t, v in users.items()}
+    free = {"p": [[0.0, "P%d" % i, None] for i in range(NPB)], "k": [[0.0, "K%d" % i, None] for i in range(8 - NPB)]}
+    look, marg = CFG["look"], CFG["marg"]
+    while len(order) < n:
+        be = None; bm = 1e18; fb = {k: min(v)[0] if v else None for k, v in free.items()}
+        for e, L in ready.items():
+            c = []; t0 = et[e]
+            for i in L:
+                t = rt[i] if rt[i] > t0 else t0
+                x = tiles[i]
+                if x and x not in bank:
+                    f = fb[x[0]]
+                    if f is None:
+                        continue
+                    if f > t:
+                        t = f
+                c.append((t, i))
+            if c:
+                m = min(c)[0]
+                if m < bm:
+                    bm = m; be = c
+        if be is None:
+            return None
+        st, i = max((c for c in be if c[0] <= bm + 20.0), key=lambda c: prio[c[1]])
+        hi = [c for c in be if c[0] - bm < look * cost[i] and prio[c[1]] > prio[i] + marg]
+        if hi:
+            st, i = max(hi, key=lambda c: prio[c[1]])
+            fit = [c for c in be if c[0] + cost[c[1]] <= st + 20.0]
+            if fit:
+                st, i = max(fit, key=lambda c: prio[c[1]])
+        x = tiles[i]
+        if x:
+            if x not in bank:
+                fl = free[x[0]]; b = max(y for y in fl if y[0] <= st); fl.remove(b); bank[x] = b[1]
+                if b[2]:
+                    extra[i] = users[b[2]]
+            left[x] -= 1
+        e = E[i]; start[i] = st; et[e] = st + cost[i]; f = fin[i] = st + cost[i] + post[i]; order.append(i); ready[e].remove(i)
+        if x and left[x] == 0:
+            free[x[0]].append([max(fin[j] for j in users[x]) + WAKE, bank[x], x])
+        for j, g_ in succ[i]:
+            if f + g_ + pre[j] > rt[j]:
+                rt[j] = f + g_ + pre[j]
+            nd[j] -= 1
             if nd[j] == 0:
-                ready.append(j)
-    assert len(order) == n
-    return order, bank, start, fin
+                ready[E[j]].append(j)
+    return order, bank, start, fin, extra
+
+
+def replay(E, cost, lat, pred, wake, res):
+    fin = [0.0] * len(E); et = {}; extra = res[4]
+    for i in res[0]:
+        t = et.get(E[i], 0.0)
+        for j, g_ in pred[i]:
+            x = fin[j] + wake if g_ else fin[j]
+            if x > t:
+                t = x
+        for j in extra.get(i, ()):
+            if fin[j] + wake > t:
+                t = fin[j] + wake
+        t += cost[i]; et[E[i]] = t; fin[i] = t + lat[i]
+    return max(fin)
+
+
+def schedule(ops):
+    n = len(ops); E = [o["e"] for o in ops]; lat = [o["lat"] for o in ops]; zero = [0.0] * n
+    succ = [[] for _ in range(n)]; pred = [[] for _ in range(n)]
+    for i, o in enumerate(ops):
+        for j, raw in o["deps"].items():
+            g_ = WAKE if waits(ops, i, j) else 0.0
+            succ[j].append((i, g_)); pred[i].append((j, g_))
+    tiles = [o["tiles"][0] if o["tiles"] else None for o in ops]; users = {}
+    for i in range(n):
+        if tiles[i]:
+            users.setdefault(tiles[i], []).append(i)
+    mc = [([price(o, m) for o in ops], [x * m["lat"] for x in lat], m["wake"]) for m in FIGURES]
+    cost = mc[0][0]; prio = [0.0] * n
+    for i in range(n - 1, -1, -1):
+        prio[i] += cost[i] + lat[i]
+        for j, g_ in pred[i]:
+            prio[j] = max(prio[j], prio[i] + g_)
+    first = [1e6 if o["sem"] else CFG["boost"] if cost[i] < CFG["small"] and any(E[j] != E[i] for j, g_ in succ[i]) else 0.0 for i, o in enumerate(ops)]
+    st = {"best": None, "ref": None}; npred = [len(x) for x in pred]
+
+    def attempt(p):
+        res = forward(E, cost, zero, lat, npred, succ, [a + b for a, b in zip(p, first)], tiles, users)
+        if res:
+            ts = [replay(E, c, l, pred, w, res) for c, l, w in mc]
+            st["ref"] = st["ref"] or ts; v = sum(a / b for a, b in zip(ts, st["ref"]))
+            if st["best"] is None or v <= st["best"][0]:
+                st["best"] = (v, res, ts, p)
+        return res
+    for r in range(CFG["rounds"]):
+        res = attempt(prio)
+        if res is None:
+            break
+        prio = forward(E, cost, lat, zero, [len(x) for x in succ], pred, res[3], [None] * n, {})[3]
+    groups = {}
+    for i, o in enumerate(ops):
+        for g_ in (o["tag"], o["ph"], o["ph"][:-1]):
+            groups.setdefault(g_, []).append(i)
+    names = sorted(groups); s = CFG["seed"]
+    for r in range(CFG["tries"]):
+        p = list(st["best"][3] if st["best"] else prio)
+        for k in range(2):
+            s = (s * 1103515245 + 12345) % 2147483648; g_ = names[(s >> 8) % len(names)]
+            s = (s * 1103515245 + 12345) % 2147483648; d = (-12000, -4000, -1200, -400, 400, 1200, 4000, 12000)[(s >> 8) % 8]
+            for i in groups[g_]:
+                p[i] += d
+        attempt(p)
+    res = st["best"][1]
+    for i, js in res[4].items():
+        for j in js:
+            ops[i]["deps"].setdefault(j, False)
+    return res + (st["best"][2],)
 
 
 PLAN = {}
 
 
 def lanes(T, topo, src):
-    r = T.rank_of(src); dst = {d: T.cores[r ^ d] for d in range(1, 8)}
-    far = [d for d in dst if topo.chip(dst[d]) != topo.chip(src)]; used = 0; m = {}
-    for d in far:
-        e = [x for x in topo.engines(src, dst[d]) if not used >> x & 1][0]
-        m[d] = 1 << e; used |= m[d]
-    farall = 0
-    for d in far:
-        farall |= topo.mask(src, dst[d])
+    r = T.rank_of(src); dst = {d: T.cores[r ^ d] for d in range(1, 8)}; me = topo.chip(src)
+    far = [d for d in dst if topo.chip(dst[d]) != me]
+    far.sort(key=lambda d: topo.mates(me, topo.chip(dst[d])) + topo.same_plane(me, topo.chip(dst[d])))
+    es = topo.engines(src, dst[far[0]]); k = len(es) // 2; calls = []
+    for part in (far[:k], far[k:]):
+        w = 1 << ((len(es) // len(part)).bit_length() - 1)
+        calls.append({d: sum(1 << x for x in es[w * j:w * j + w]) for j, d in enumerate(part)})
     near = [d for d in dst if d not in far]
     for j, d in enumerate(near):
-        es = [x for x in topo.engines(src, dst[d]) if not farall >> x & 1][j::len(near)]
-        k = 1 << (len(es).bit_length() - 1)
-        m[d] = sum(1 << x for x in es[:k])
-    return m
+        own = [x for x in topo.engines(src, dst[d]) if x not in es][j::len(near)]
+        calls[1][d] = sum(1 << x for x in own[:1 << (len(own).bit_length() - 1)])
+    return calls
 
 
 def rank_program(g, core, T, topo):
@@ -817,8 +887,8 @@ def rank_program(g, core, T, topo):
     ops = PLAN["ops"]; order, bank = PLAN["s"][:2]
     Q = {"pe": g.tensor, "dve": g.vector, "act": g.scalar, "gp": g, "sp": g.sync}
     mine = lanes(T, topo, core)
-    nsent = sum(bin(x).count("1") for x in mine.values())
-    narr = sum(bin(lanes(T, topo, T.cores[rank ^ d])[d]).count("1") for d in range(1, 8))
+    nsent = sum(bin(x).count("1") for m in mine for x in m.values())
+    narr = sum(bin(m.get(d, 0)).count("1") for d in range(1, 8) for m in lanes(T, topo, T.cores[rank ^ d]))
 
     def R(x):
         if not isap(x):
@@ -839,7 +909,7 @@ def rank_program(g, core, T, topo):
             continue
         for j in sorted(o["deps"], key=lambda j: -place[j]):
             s, v = tok[j]
-            if seen[e].get(s, 0) < v:
+            if seen[e].get(s, 0) < v and waits(ops, i, j):
                 wait(e, s, v)
                 for s2, v2 in known.get(j, {}).items():
                     seen[e][s2] = max(seen[e].get(s2, 0), v2)
@@ -848,15 +918,24 @@ def rank_program(g, core, T, topo):
         for c in o["calls"]:
             k = c[0]; a = [R(x) for x in c[1:]]
             if k == "dma":
-                q.dma_start(a[0], a[1]).then_inc(T.sem[o["sem"][0]], 16); tok[i] = o["sem"]
+                if not c[3]:
+                    q.dma_start(a[0], a[1]).then_inc(T.sem[o["sem"][0]], 16); tok[i] = o["sem"]
+                    continue
+                run = rank & -rank or 8
+                for b in range(0, 8, run):
+                    x = [("ap", y[1], sl(16 * (b ^ rank if y[1] in IOS else b), 16 * run), y[3] or (slice(None),)) for y in c[1:3]]
+                    q.dma_start(R(x[0]), R(x[1])).then_inc(T.sem[o["sem"][0]], 16)
+                tok[i] = (o["sem"][0], 16 * 8 // run)
                 continue
             if k == "send":
-                tr = []
-                for d in range(1, 8):
-                    rid, pid, _ = topo.addr(T.cores[rank ^ d])
-                    tr.append(RemoteDMATransfer(dst_ids=[DstId(rid=rid, pnc=pid)], dma_engine_mask=mine[d], remote_sem=T.sem["arr%d" % c[2]],
-                                                src=T[c[1][1]][:, GH * (d - 1):GH * d], dst=T[c[3]][:, c[4] + GH * (d - 1):c[4] + GH * d]))
-                q.remote_dma_fused(tr, local_sem=T.sem[o["sem"][0]]); tok[i] = (o["sem"][0], nsent)
+                for m in mine:
+                    tr = []
+                    for d in m:
+                        rid, pid, _ = topo.addr(T.cores[rank ^ d]); a0 = region(c[1])[1] + GH * (d - 1); b0 = c[4] + GH * (d - 1)
+                        tr.append(RemoteDMATransfer(dst_ids=[DstId(rid=rid, pnc=pid)], dma_engine_mask=m[d], remote_sem=T.sem["arr%d" % c[2]],
+                                                    src=T[c[3]][:, a0:a0 + GH], dst=T[c[3]][:, b0:b0 + GH]))
+                    q.remote_dma_fused(tr, local_sem=T.sem[o["sem"][0]])
+                tok[i] = (o["sem"][0], nsent)
                 continue
             if k == "mm":
                 x = q.matmul(a[0], a[1], a[2], a[3], a[4])
@@ -872,6 +951,11 @@ def rank_program(g, core, T, topo):
                 x = q.tensor_tensor_scan(a[0], a[1], a[2], a[3], a[4], a[5])
             elif k == "iota":
                 x = q.iota(a[0], a[1], a[2], a[3]) if DTYPE[c[1][1]] == I32 else q.iota(a[0], a[1], a[2], a[3], allow_small_or_imprecise_dtypes=True)
+            elif k == "iotax":
+                x = q.iota(a[0], [[-32 if rank & 2 else 32, 2], [-16 if rank & 1 else 16, 2], [1, 16]], (64 * a[1]) ^ (16 * rank), 0,
+                           allow_small_or_imprecise_dtypes=True)
+            elif k == "sel":
+                x = q.affine_select(a[0], a[1], [[0, region(c[1])[3]]], OP.is_ge, 0.0, 0, 0)
             elif c[1][0] == "ind":
                 x = q.activation(a[0], a[1], a[2])
             else:

import numpy as np
from concourse.bass import DstId, RemoteDMATransfer
from concourse.mybir import AluOpType as OP, ActivationFunctionType as AF

NC, NT, GH = 448, 896, 128
F32, BF, I32, U16 = "float32", "bfloat16", "int32", "uint16"
XD, XO, XG, XE = 0, 256, 1152, 2048
BD, BO, BG, BN, BE = 0, 1280, 8448, 9344, 9360
CD = 80
W1N, W2N = 14336 + 256, 8064 + 512
EMPTY = 8704.0
ULP = 1.5 * 2 ** 23

CFG = dict(
    s1=[[[(0, 64)], [(64, 112)]],
        [[(176, 96)], [(272, 64), (-1, 16)]],
        [[(-1, 80)], [(352, 96)]]],
    s2=[[80, 80, 96], [80, 80, 96], [80, 80, 96]],
    look=1.0, marg=6000.0, boost=0.0, small=150.0, rounds=6, tries=1500, seed=1,
    fit="adaad" "adaad" "daaad" "d", lw=56, conv=("aaaap", "aaapapa", "apaaapaa"), np_sets=2, w1=(3, 13), ondve=(160, 160, 160),
    exact=True, hold=(0, 0), obq="sp", onact="hn", border=False, blocks=((160, 16, 0, 64, 64, 96), (0, 112, 112, 112, 224, 128), (224, 224, 0, 224)), off2=((0, 1, 1, 1), (0, 1, 1, 1), (0, 1, 1, 1)),
)

SCRATCH = {}
SHAPE = {}


def _decl(name, shape, dt, where="sbuf"):
    SCRATCH[name] = (where, [128] + list(shape), dt)
    SHAPE[name] = list(shape)


for _n, _s, _d in [
    ("OB", [7168], BF), ("XW", [XE], BF), ("BW", [BE], BF), ("W1", [W1N], BF), ("W2", [W2N], F32), ("W2b", [3584], BF), ("W3", [W2N], BF), ("PY", [128], F32),
    ("CTi", [CD + NC], I32), ("TVi", [896], I32), ("NV", [128], BF), ("EW", [CD + NC], F32), ("DD", [CD + NC], BF),
    ("TVW", [256 + NT], F32), ("TRu", [NC], U16), ("EOu", [NC], U16), ("tmpB", [NC], F32),
    ("COL", [144], BF), ("PI", [8], I32), ("PF", [16], F32), ("KX", [1], F32), ("KEY", [16], F32), ("DK", [16], F32),
    ("K16", [16], F32), ("SUM", [144], BF), ("BC", [2048], BF), ("ID", [128], BF), ("PX", [128], BF), ("O8", [8], BF), ("EX", [128], BF), ("NI", [128], BF), ("ONES", [128], BF),
    ("H17", [512], BF), ("WL", [128], BF), ("NU", [128], BF), ("mt", [128], BF), ("mt2", [128], BF),
    ("J2", [128], F32), ("J1", [128], F32), ("DM", [256], BF), ("RS", [256], BF), ("ONE", [64], F32), ("DJ", [256], F32),
    ("IDS", [NT], F32), ("LW", [2 * NT], F32), ("LM", [256], F32), ("LS", [256], F32), ("Li", [CD], I32), ("OT", [16], U16), ("OU", [18], U16),
    ("OC", [8], U16), ("PO", [56], U16), ("FT", [56], BF), ("FC", [28], BF), ("FR", [56], BF), ("FQ", [56], BF), ("RK", [56], F32), ("RK2", [56], F32),
    ("SEL", [56], BF), ("IT", [56], F32), ("CS", [3, 256], BF), ("v", [256], F32), ("w", [256], F32), ("w2", [256], F32), ("vo", [256], U16), ("wo", [256], U16),
    ("xo", [256], BF), ("DGl", [CD], BF), ("tE", [128], F32), ("G", [4096], BF), ("RR", [4096], BF), ("AB", [4096], BF),
    ("un", [256], BF), ("FF", [256], BF), ("ft", [256], BF), ("gd", [256], BF), ("MM", [256], BF), ("nF", [256], BF),
    ("PP", [CD], U16), ("OP_", [CD], U16), ("TD", [CD], U16), ("ED", [CD], U16),
    ("tD", [CD], F32), ("tD2", [CD], F32), ("DG", [CD], BF), ("DN", [CD], BF), ("SS", [2560], F32), ("EQ", [NC], BF),
]:
    _decl(_n, _s, _d)
for _s in "01":
    for _n, _sh, _d in [("S0a", [512], BF), ("S0b", [512], BF), ("FO", [1152], BF), ("Fa", [1152], BF), ("Fb", [1152], BF)]:
        _decl(_n + _s, _sh, _d)
    for _c in "ab":
        _decl("Z" + _s + _c, [128, 4], BF)
        _decl("Q" + _s + _c, [128, 6], BF)
NPB = 2 * CFG["np_sets"]
for _i in range(NPB):
    _decl("P%d" % _i, [128, 4], F32, "psum")
for _i in range(8 - NPB):
    _decl("K%d" % _i, [512], F32, "psum")
DTYPE = {k: v[2] for k, v in SCRATCH.items()}
IOS = {"obs": [7168], "x0": [896], "ct": [448], "tv": [896], "yx": [896], "yb": [1792], "yc": [448], "yt": [896]}
SHAPE.update(IOS)
NDMA = 20
SEMAPHORES = ["pe", "dve", "act", "gp"] + ["d%d" % i for i in range(NDMA)] + ["snt%d" % i for i in range(6)] + ["arr%d" % i for i in range(6)]


def sl(a, n, s=1):
    return slice(a, a + (n - 1) * s + 1, s)


def A(name, *idx, p=None):
    return ("ap", name, p, idx)


def IND(win, off):
    return ("ind", win, off)


def shp(name):
    return SHAPE[name] if name in SHAPE else ([128, 4] if name[0] == "p" else [512])


def region(ap):
    s = shp(ap[1]); idx = list(ap[3]) + [slice(None)] * (len(s) - len(ap[3]))
    lo = hi = 0; n = 1; st = 1
    for d in range(len(s) - 1, -1, -1):
        i = idx[d]
        r = range(*i.indices(s[d])) if isinstance(i, slice) else range(i, i + 1)
        lo += r[0] * st; hi += r[-1] * st; n *= len(r); st *= s[d]
    return ap[1], lo, hi + 1, n


def bits(ap):
    name, lo, hi, n = region(ap)
    if n == hi - lo or not CFG["exact"]:
        return ((1 << (hi - lo)) - 1) << lo
    z = np.zeros(shp(name), np.uint8); z[tuple(ap[3])] = 1
    return int.from_bytes(np.packbits(z.reshape(-1), bitorder="little").tobytes(), "little")


def isap(x):
    return isinstance(x, tuple) and len(x) > 0 and x[0] in ("ap", "ind")


def psum(ap):
    return ap[0] == "ap" and ap[1] not in SHAPE


def two(ap):
    return DTYPE.get(ap[1], F32) in (BF, U16)


WAKE = 240.0
FIGURES = [dict(f=1.05, fix=5, gat=1.3, sca=2.6, wake=240, lat=1.1), dict(f=1.15, fix=0, gat=1.1, sca=1.8, wake=280, lat=0.9),
           dict(f=1.4, fix=10, gat=1.8, sca=4.5, wake=160, lat=1.3)]


def price(o, m):
    e = o["e"]; tot = 0.0
    for c in o["calls"]:
        k = c[0]; out = c[1]; ins = [x for x in c[2:] if isap(x)]
        sc = out[0] == "ind"; ga = any(x[0] == "ind" for x in ins)
        n = 16 * region(out[2])[3] if sc else region(out)[3]
        if k == "mm":
            tot += max(min(64, region(c[2])[3]), n) * 0.417 * m["f"] * (1 if two(c[3]) else 4)
        elif k in ("dma", "send", "recv"):
            tot += (5200 if c[3] else 650) if k == "dma" else 2400 if k == "send" else 0
        elif e == "gp":
            tot += (150 + 2 * n * 0.83) * m["f"]
        elif sc or ga:
            tot += (55 + n * (m["sca"] if sc else m["gat"]) * 0.83) * m["f"]
        else:
            f = 1.0
            if k == "tt":
                f = 1.0 if psum(ins[0]) or psum(ins[1]) else 2.0
            elif e == "dve" and all(two(x) for x in [out] + ins if region(x)[3] > 1):
                f = 0.5
            tot += (m["fix"] + max(64, n * f) * 0.83) * m["f"]
    return tot


def waits(ops, i, j):
    return not ops[i]["e"] == ops[j]["e"] == "pe"


def build():
    ops = []; recs = {}; cnt = {"t": 0, "d": 0, "tag": "i"}

    def tile(kind="k"):
        cnt["t"] += 1
        return "%s%d_" % (kind, cnt["t"])

    def touch(i, ap, wr, deps):
        name, lo, hi, n = region(ap)
        if name in IOS:
            return
        L = recs.setdefault(name, []); keep = []
        ps = name not in SHAPE; mk = bits(ap)
        for r in L:
            j, w, a = r
            if j != i:
                if a & mk and (w or wr):
                    deps[j] = deps.get(j, False) or (w and not wr)
                elif ps and ops[j]["e"] != ops[i]["e"]:
                    deps[j] = deps.get(j, False)
                if wr and not ps:
                    a &= ~mk
            if a:
                keep.append((j, w, a))
        keep.append((i, wr, mk)); recs[name] = keep

    def op(e, calls, lat=0.0, sem=None):
        i = len(ops); o = dict(e=e, calls=calls, deps={}, lat=lat, sem=sem, tiles=[]); ops.append(o)
        for c in calls:
            k = c[0]; out = c[1]; ins = [x for x in c[2:] if isap(x)]
            if k == "mm" and not c[4]:
                ins = ins + [out]
            for x in ins:
                for y in ((x[1], x[2]) if x[0] == "ind" else (x,)):
                    touch(i, y, False, o["deps"])
            if out[0] == "ind":
                touch(i, out[2], False, o["deps"]); touch(i, out[1], True, o["deps"])
            elif k != "send":
                touch(i, out, True, o["deps"])
            else:
                touch(i, out, False, o["deps"])
            for x in [out] + ins:
                if psum(x) and x[1] not in o["tiles"]:
                    o["tiles"].append(x[1])
        w_ = calls[0][1]; o["ph"] = cnt["tag"] + e[0]
        o["tag"] = "%s%s%s" % (cnt["tag"], e[0], (w_[1][1] + "s" if w_[0] == "ind" else w_[1][0] if psum(w_) else w_[1])[:3])
        return i

    def ts(out, a, s1, o0, s2=None, o1=None):
        return op("dve", [("ts", out, a, s1, s2, o0, o1)])

    def tt(out, a, b, o):
        return op("dve", [("tt", out, a, b, o)])

    def cp(out, a):
        return op("dve", [("cp", out, a)])

    def ms(out, v):
        return op("dve", [("ms", out, float(v))])

    def act(out, a, f, bias=0.0, scale=1.0):
        return op("act", [("act", out, a, f, bias, scale)])

    def iota(out, pat, base, cm):
        return op("gp", [("iota", out, pat, base, cm)])

    def mm(groups):
        c = []
        for g_ in groups:
            out, terms = g_[0], g_[1]
            for j, (l, r) in enumerate(terms):
                c.append(("mm", out, l, r, j == 0 and "<" in (g_ + ("<>",))[2], j == len(terms) - 1 and ">" in (g_ + ("<>",))[2]))
        return op("pe", c)

    def dma(out, a, q="sp", lat=2000.0, xor=True):
        cnt["d"] += 1
        return op(q, [("dma", out, a, xor)], lat=lat, sem=("d%d" % (cnt["d"] - 1), 16))

    def SUMk(k):
        return A("SUM", sl(15 - k, 128))

    def BCk(k):
        return A("BC", sl(128 * k, 128))
    ID, NI, ONES = A("ID"), A("NI"), A("ONES")

    def exchange(x, src, off, dst):
        s = op("gp", [("send", A(src, sl(off, 896)), x, src, dst)], lat=4500.0, sem=("snt%d" % x, 0))
        r = op("arr", [("recv", A(src, sl(dst, 896)))], lat=500.0, sem=("arr%d" % x, 0))
        ops[r]["deps"][s] = False; cnt["arr"] = r
        return s

    dma(A("RR", sl(0, NT)), A("x0"), xor=False)
    CT = A("CTi", sl(CD, NC))
    dma(CT, A("ct"), xor=False)
    dma(A("OB", sl(0, 2816)), A("obs", sl(0, 2816)), CFG["obq"], lat=3500.0)
    dma(A("TVi"), A("tv"))
    dma(A("OB", sl(2816, 4352)), A("obs", sl(2816, 4352)), lat=6000.0)
    iota(A("KX"), [[0, 1]], 0, 1)
    for h in range(2):
        op("gp", [("iotax", A("mt", sl(64 * h, 64)), h)])
    PX = A("PX")
    ts(PX, A("mt"), A("KX"), OP.is_equal)
    ts(A("PY"), A("mt"), A("KX"), OP.is_equal)
    for h in range(2):
        t = tile()
        mm([(A(t, sl(0, 448)), [(PX, A("RR", sl(448 * h, 448)))])])
        (cp if h else lambda a, b: act(a, b, AF.Identity))(A("XW", sl(XO + 448 * h, 448)), A(t, sl(0, 448)))
    exchange(0, "XW", XO, XG)
    iota(A("PI", sl(0, 1)), [[0, 1]], 0, 1)
    iota(A("COL"), [[1, 144]], 0, 0)
    COL = A("COL", sl(0, 128))
    iota(A("K16"), [[1, 16]], 0, 0)
    p_ = A("PI", sl(0, 1))
    ts(ID, COL, A("KX", sl(0, 1)), OP.is_equal)
    ts(A("PI", sl(4, 1)), p_, 15, OP.bitwise_and)
    PK, PG = A("PF", sl(4, 1)), A("PF", sl(5, 1))
    cp(PK, A("PI", sl(4, 1)))
    ts(PG, A("KX", sl(0, 1)), PK, OP.subtract)
    ts(A("O8"), A("mt", sl(0, 8, 16)), PG, OP.is_equal)
    ts(A("KEY"), A("K16"), PG, OP.add)
    ts(A("DK"), A("K16"), PK, OP.is_equal)
    ts(A("NI"), ID, -1.0, OP.mult)
    ts(A("mt"), COL, PG, OP.is_ge)
    ts(A("mt2"), COL, A("KEY", sl(15, 1)), OP.is_le)
    tt(ONES, A("mt"), A("mt2"), OP.mult)
    ts(A("SUM"), A("COL", sl(0, 144)), A("KEY", sl(15, 1)), OP.is_equal)
    for k in range(16):
        act(BCk(k), ONES, AF.Copy, scale=A("DK", sl(k, 1)))
    p32 = A("KX", sl(0, 1))
    ts(A("mt"), COL, p32, OP.is_le, -1.0, OP.mult)
    tt(A("mt"), A("mt"), ONES, OP.mult)
    ts(A("mt2"), ID, -2048.0, OP.mult)
    tt(A("NU"), A("mt"), A("mt2"), OP.min)
    act(A("NV"), A("NU"), AF.Copy, scale=-1.0)
    ts(A("mt2"), COL, p32, OP.is_gt, 1.0, OP.mult)
    ts(A("mt"), COL, p32, OP.is_lt, -1.0, OP.mult)
    tt(A("mt"), A("mt"), A("mt2"), OP.add)
    tt(A("mt"), A("mt"), ONES, OP.mult)
    ts(A("mt2"), ID, 63.0, OP.mult)
    tt(A("WL"), A("mt2"), A("mt"), OP.subtract)
    act(A("H17", sl(256, 128)), ID, AF.Copy, scale=17.0)
    act(A("H17", sl(384, 128)), ID, AF.Copy, scale=-17.0)
    tt(A("H17", sl(0, 128)), ONES, A("H17", sl(256, 128)), OP.add)
    tt(A("H17", sl(128, 128)), ONES, A("H17", sl(384, 128)), OP.add)
    iota(A("J2"), [[0, 4], [16, 32]], 8064, 0)
    ts(A("J2"), A("J2"), PK, OP.add)
    iota(A("J1"), [[0, 8], [16, 16]], 14336, 0)
    ts(A("J1"), A("J1"), PK, OP.add)
    iota(A("DJ"), [[1, 256]], 0, 0)
    iota(A("RS"), [[0, 16], [1, 16]], 0, 0)
    ts(A("DM"), A("RS"), PK, OP.is_equal)
    ts(A("RS"), A("RS"), 0.5, OP.is_gt)
    iota(A("IT"), [[16, 56]], NT, 0)
    ts(A("IT"), A("IT"), PK, OP.add)
    ms(A("ONE"), 1)
    for u in range(3):
        ms(A("CS", u), 32 ** u)
    ms(A("Fa0", sl(0, 128, 9)), -30000); ms(A("Fa1", sl(0, 128, 9)), -30000)
    for h in range(16):
        if h < CFG["w1"][0]:
            ms(A("W1", sl(896 * h, 896)), 0)
        elif h < CFG["w1"][1]:
            act(A("W1", sl(896 * h, 896)), A("W1", sl(0, 896)), AF.Copy)
        else:
            iota(A("W1", sl(896 * h, 896)), [[0, 896]], 0, 0)
    ms(A("W1", sl(14336, 256)), 0)
    ms(A("FQ"), 0); ms(A("FC"), 1); ms(A("DD"), 0)
    ms(A("XW", sl(XD, 256)), 512); ms(A("TVW", sl(0, 256)), EMPTY)
    ms(A("CTi", sl(0, CD)), 0); ms(A("EW", sl(0, CD)), 60000)
    iota(A("BW", sl(BD, 1280)), [[0, 1280]], 512, 0); ms(A("BW", sl(BN, 16)), 512)
    for h in range(2):
        iota(A("LW", sl(NT * h, NT)), [[0, NT]], 0, 0)
    for h in range(4):
        iota(A("BW", sl(BO + 2816 + 1088 * h, 1088)), [[0, 1088]], 512, 0)
    for w in ("W2", "W3"):
        for h in range(8):
            iota(A(w, sl(1072 * h, 1072)), [[0, 1072]], 0, 0)
    ts(A("SS", sl(0, NT)), A("TVi"), 8063.5, OP.is_gt, EMPTY - 8064, OP.mult)
    tt(A("TVW", sl(256, NT)), A("TVi"), A("SS", sl(0, NT)), OP.add)
    t = tile(); ct = A(t, sl(0, NC))
    cp(A("tmpB"), CT)
    mm([(ct, [(A("PY"), A("tmpB"))])])
    cp(CT, ct)
    ts(A("tmpB"), ct, 14335.5, OP.is_gt, 60000.0, OP.mult)
    tt(A("EW", sl(CD, NC)), ct, A("tmpB"), OP.max)
    ts(CT, CT, 4, OP.arith_shift_right)
    cp(A("TRu", sl(0, 176)), A("CTi", sl(CD, 176)))
    cp(A("TRu", sl(176, 272)), A("CTi", sl(CD + 176, 272)))

    def flag_static(u, c0, n):
        for a in range(c0, c0 + n, 128):
            m = min(128, c0 + n - a)
            tt(A("tE", sl(0, m)), A("EW", sl(CD + a, m)), A("J1", sl(0, m)), OP.min)
            cp(A("EOu", sl(a, m)), A("tE", sl(0, m)))
        return [cp(IND(A("W1"), A("EOu", sl(a, 16))), A("CS", u)) for a in range(c0, c0 + n, 16)]

    def worklist(F, cols, K, idbase, otile, new, th):
        n = len(cols); runs = []
        for j, c in enumerate(cols):
            if runs and runs[-1][1] + runs[-1][2] == c:
                runs[-1][2] += 1
            else:
                runs.append([j, c, 1])
        for j, c, m in runs:
            ts(A("FR", sl(j, m)), new(c, m), th, OP.is_gt)
            iota(A("IDS", sl(16 * j, 16 * m)), [[1, 16 * m]], idbase + 16 * c, 0)
        act(A("LW", sl(0, K)), A("DJ", sl(0, K)), AF.Identity)
        t = tile()
        op("pe", [("mm", A(t, sl(0, n)), ONES, A("FR", sl(0, n)), True, False), ("mm", A(t, sl(0, n)), A("NU"), A("FR", sl(0, n)), False, False),
                  ("mm", A(t, sl(1, n - 1)), A("NV"), A("FR", sl(0, n - 1)), False, True)])
        rk, rk2, se = A("RK", sl(0, n)), A("RK2", sl(0, n)), A("SEL", sl(0, n))
        op("dve", [("scan", rk, A("ONE", sl(0, n)), A(t, sl(0, n)), 2047.0, OP.mult, OP.add)])
        tt(rk2, rk, A("IT", sl(0, n)), OP.min)
        cp(A("PO", sl(0, n)), rk2)
        ts(se, rk, K - 0.5, OP.is_lt)
        for a in range(0, n, CFG["lw"]):
            m = min(CFG["lw"], n - a)
            act(IND(A("LW"), A("PO", sl(a, m))), A("IDS", sl(16 * a, 16 * m)), AF.Silu)
        tt(A("LM", sl(0, K)), A("LW", sl(0, K)), A("DM", sl(0, K)), OP.mult)
        op("dve", [("scan", A("LS", sl(0, K)), A("RS", sl(0, K)), A("LM", sl(0, K)), 0.0, OP.mult, OP.add)])
        ts(A(otile, sl(0, K // 16)), A("LS", sl(15, K // 16, 16)), 0.25, OP.add)
        for j, c, m in runs:
            tt(A(F, sl(c, m)), A("FR", sl(j, m)), A("SEL", sl(j, m)), OP.subtract)

    def quad(t, n, whole, each, start=True, stop=True):
        pt = t[0] == "p"
        al = A(t, slice(0, n)) if pt else A(t, sl(0, 4 * n))
        c = [(al, l, r) for l, r in whole]
        c += [(A(t, slice(0, n), j) if pt else A(t, sl(j, n, 4)), l, r) for j in range(4) for l, r in each(j)]
        return op("pe", [("mm", o_, l, r, start and x == 0, stop and x == len(c) - 1) for x, (o_, l, r) in enumerate(c)])

    def median(n, s, srcs, FF, flip=False, off=0, direct=None, nF=None):
        N_ = slice(0, n); P = {}
        whole = lambda q: [(l, A(b, sl(a + q, 4 * n, 4))) for l, b, a in srcs]
        each = lambda k: [(BCk(k), FF)] if FF else []
        wire = lambda k: [(l, A(b, sl(a + k, n, 16))) for l, b, a in srcs] + each(k)
        neg = lambda ts_: [(NI, r) if l is ID else (ID, r) if l is NI else (l, nF if r is FF else FF) for l, r in ts_]
        if off and FF:
            act(nF, FF, AF.Copy, scale=-1.0)
        if cnt.get("flip" + s) != flip:
            cnt["flip" + s] = flip
            ms(A("Fb" + s, sl(0, 128, 9)), 30000 if flip else -30000)
        for h, c in enumerate("ab" if off else ""):
            up = (c == "b") == flip

            def layer(xs, ys, buf):
                t = tile()
                mm([(A(t, sl(j, n, 4)), xs[j] + neg(ys[j])) for j in range(4)])
                act(A(buf, N_) if buf[0] == "Z" else A(buf, sl(0, 4 * n)), A(t, sl(0, 4 * n)), AF.Relu)
                d = [A(buf, N_, j) if buf[0] == "Z" else A(buf, sl(j, n, 4)) for j in range(4)]
                mn = [xs[j] + [(NI, d[j])] for j in range(4)]; mx = [ys[j] + [(ID, d[j])] for j in range(4)]
                return (mx, mn) if up else (mn, mx)
            lo, hi = layer([wire(2 * h + 4 * j) for j in range(4)], [wire(2 * h + 1 + 4 * j) for j in range(4)], "S0" + c + s)
            pw, sw = [lo[0], hi[1], lo[2], hi[3]], [lo[1], hi[0], lo[3], hi[2]]
            if off == 2:
                lo, hi = layer(pw, sw, "Z" + s + c)
                pw, sw = [lo[0], lo[1], hi[2], hi[3]], [hi[0], lo[2], hi[1], lo[3]]
            t = tile()
            mm([(A(t, sl(j, n, 4)), sw[j]) for j in range(4)])
            if off == 1:
                act(A("Z" + s + c, N_), A(t, sl(0, 4 * n)), AF.Identity)
            else:
                op("act", [("act", A("Q" + s + c, N_, slice(j, j + 5, 4)), A(t, sl(j, 2 * n, 2)), AF.Identity, 0.0, 1.0) for j in range(2)])
            P[c] = tile("p")
            mm([(A(P[c], N_, j), pw[j]) for j in range(4)])
        for h, c in enumerate("" if off else "ab"):
            P[c] = tile("p")
            quad(P[c], n, whole(2 * h), lambda j: each(2 * h + 4 * j))
            if not direct:
                t = tile()
                quad(t, n, whole(2 * h + 1), lambda j: each(2 * h + 1 + 4 * j))
                act(A("S0" + c + s, sl(0, 4 * n)), A(t, sl(0, 4 * n)), AF.Identity)
        seq = {}
        for h, c in enumerate("ab"):
            lo, hi = (OP.min, OP.max) if (c == "b") != flip else (OP.max, OP.min)
            p = lambda a, b=None, st=1: A(P[c], N_, a if b is None else slice(a, b, st))
            q = lambda a, b=None, st=1: A("Q" + s + c, N_, a if b is None else slice(a, b, st))
            z = lambda a, b=None, st=1: A("Z" + s + c, N_, a if b is None else slice(a, b, st))
            f = lambda a: A("F" + c + s, sl(a, n, 9))
            s0 = lambda a, m: A(direct, sl(2 * h + 1 + 4 * a, m * n, 16 // m)) if direct else A("S0" + c + s, sl(a, m * n, 4 // m))
            seq[c] = [
                ([(z(1, 4, 2), p(0, 4, 2), s0(0, 2), hi), (z(0, 4, 2), p(1, 4, 2), s0(1, 2), lo)],
                 [(p(0, 4, 2), s0(0, 2), lo), (p(1, 4, 2), s0(1, 2), hi)]),
                ([(q(0, 5, 4), p(0, 2), z(0, 2), hi), (q(1, 6, 4), p(2, 4), z(2, 4), lo)], [(p(0, 2), z(0, 2), lo), (p(2, 4), z(2, 4), hi)]),
                ([(q(3), p(1), q(0), hi), (q(2), p(2), q(5), lo)], [(p(1), q(0), lo), (p(2), q(5), hi)]),
                ([(z(0, 3), p(0, 3), q(1, 4), hi), (f(8), p(3), q(4), hi), (f(1), p(0), q(1), lo)], [(p(1, 4), q(2, 5), lo)]),
                ([(q(0, 2), p(2, 4), z(0, 2), lo)], [(p(2, 4), z(0, 2), hi)]),
                ([(f(2), p(1), q(0), lo), (f(4), p(2), q(1), lo), (f(6), p(3), z(2), lo),
                  (f(3), p(1), q(0), hi), (f(5), p(2), q(1), hi), (f(7), p(3), z(2), hi)], [])]
        for L in range(off, 6):
            for c in "ab":
                outs, stay = seq[c][L]
                for x in outs:
                    tt(*x)
                for x in stay:
                    tt(x[0], *x)
        n9 = sl(0, 9 * n)
        if flip:
            op("dve", [("scan", A("FO" + s, n9), A("Fa" + s, n9), A("Fb" + s, n9), 30000.0, OP.min, OP.max)])
        else:
            op("dve", [("scan", A("FO" + s, n9), A("Fa" + s, n9), A("Fb" + s, n9), -30000.0, OP.max, OP.min)])
        return A("FO" + s, sl(8, n, 9))

    def plane(b0, k, n):
        return A("AB", sl(16 * b0 + 4 * n * (k % 4) + k // 4, n, 4))

    def misfits(b0, n, whole, each, bias, how):
        for q in range(4):
            t = tile(); a = A("AB", sl(16 * b0 + 4 * n * q, 4 * n))
            quad(t, n, whole(q), lambda j: each)
            if how == "d":
                ts(a, A(t, sl(0, 4 * n)), 16 * ULP + bias, OP.add, 16 * ULP, OP.not_equal)
            else:
                act(a, A(t, sl(0, 4 * n)), AF.Abs, bias=bias)
                if q % 2:
                    a = A("AB", sl(16 * b0 + 4 * n * (q - 1), 8 * n))
                    ts(a, a, 8.5, OP.is_gt)

    nchunk = [0]; looks = []

    def step1(u, segs, b0, keep=None, cap=None):
        s = str(nchunk[0] % 2); nchunk[0] += 1; cnt["tag"] = "c%d" % nchunk[0]
        n = sum(m for _, m in segs); N_ = sl(0, n); G = "G"; g0 = 16 * b0
        win = A("XW", sl(XO, 1792))
        pos = []; j = 0
        for c0, m in segs:
            pos.append((c0, m, j)); j += m
        dyn = [x for x in pos if x[0] < 0]
        for c0, m, j in pos:
            looks.append(act(A(G, sl(g0 + 16 * j, 16 * m)), IND(win, A("TRu", sl(c0, m)) if c0 >= 0 else A("TD", sl(0, m))), AF.Identity))
        if len(segs) > 1:
            for c0, m, j in pos:
                if c0 >= 0:
                    act(A("W2b", sl(16 * j, 16 * m)), A("OB", sl(16 * c0, 16 * m)), AF.Identity)
        for c0, m, j in dyn:
            act(A("W2b", sl(16 * j, 16 * m)), IND(A("OB"), A("OP_", sl(0, m))), AF.Identity)
        ob, o0 = ("W2b", 0) if dyn else ("OB", 16 * segs[0][0])
        gk = lambda k: A(G, sl(g0 + k, n, 16))
        un, FF, ft, MM = (A(x, sl(b0, n)) for x in ("un", "FF", "ft", "MM"))
        dg = A("DG" if len(segs) > 1 or keep else "DGl", N_); old = dyn or keep
        if keep:
            cp(dg, A("DD", sl(CD + segs[0][0], n)))
        elif dyn and len(segs) > 1:
            ms(dg, 0)
            for c0, m, j in dyn:
                cp(A("DG", sl(j, m)), A("DGl", sl(0, m)))
        if u > 0:
            t = tile()
            mm([(A(t, N_), [(SUMk(k), gk(k)) for k in range(16)] + ([(ID, dg)] if old else []))])
            ts(un, A(t, N_), 4095.0, OP.is_gt, 64.0, OP.mult)
            t = tile()
            mm([(A(t, N_), [(A("WL"), un)])])
            ts(FF, A(t, N_), 63.5 * 64, OP.is_gt, -16384.0, OP.mult)
            if old:
                tt(FF, FF, dg, OP.add)
        g4 = lambda q: A(G, sl(g0 + q, 4 * n, 4))
        o4 = lambda q: A(ob, sl(o0 + q, 4 * n, 4))
        P = median(n, s, [(ID, G, g0), (NI, ob, o0)], FF if u > 0 else None)
        misfits(b0, n, lambda q: [(ID, o4(q)), (NI, g4(q))], [(ID, P)], 0.0, CFG["fit"][nchunk[0] - 1])
        for q in range(4):
            t = tile()
            quad(t, n, [(ID, o4(q))], lambda j: [(ID, P)] + ([(ID, keep)] if keep else []))
            act(A("RR", sl(g0 + 4 * n * q, 4 * n)), A(t, sl(0, 4 * n)), AF.Relu, bias=255.0, scale=-1.0)
        t = tile(); th = 4.5
        mm([(A(t, N_), [(SUMk(k), plane(b0, k, n)) for k in range(16)] + ([(ID, un)] if u > 0 else []))])
        ts(ft, A(t, N_), th, OP.is_lt, 64.0, OP.mult)
        t = tile(); H = lambda j: A("H17", sl(128 * j, 128))
        e1 = [(H(3), un)] if u > 0 else []; e2 = [(H(2), un)] if u > 0 else []
        mm([(A(t, N_), [(H(0), ft)] + e2 + ([(NI, dg)] if old else []))] + ([] if keep else [(A(t, sl(128, n)), [(H(1), ft)] + e1)]))
        ts(MM, A(t, N_), 22.5 * 64, OP.is_lt, 32768.0, OP.mult)
        if keep:
            tt(MM, MM, cap, OP.min)
        for c0, m, j in [] if keep else pos:
            if c0 >= 0:
                ts(A("DD", sl(CD + c0, m)), A(t, sl(128 + j, m)), 5.5 * 64, OP.is_gt, EMPTY, OP.mult)
            else:
                ts(A("DN", sl(0, m)), A(t, sl(128 + j, m)), 5.5 * 64, OP.is_gt, EMPTY, OP.mult)
                tt(A("DN", sl(0, m)), A("DN", sl(0, m)), A("DGl", sl(0, m)), OP.max)
                cp(IND(A("DD"), A("OC", sl(0, m // 16))), A("DN", sl(0, m)))

        for q in range(4):
            t = tile()
            quad(t, n, [(NI, A("RR", sl(g0 + 4 * n * q, 4 * n)))] + ([(ID, A("BW", sl(BO + q, 4 * n, 4)))] if keep else []),
                 lambda j: [(BCk(q + 4 * j), MM)])
            for c0, m, j in pos:
                act(A("BW", sl(BO + 16 * c0 + q, 4 * m, 4)) if c0 >= 0 else A("W2b", sl(2048 + q, 4 * m, 4)), A(t, sl(4 * j, 4 * m)), AF.Relu, bias=255.0)
        for c0, m, j in dyn:
            cp(IND(A("BW", sl(BD, BG - BD)), A("PP", sl(0, m))), A("W2b", sl(2048, 16 * m)))

    def camlist(u, new):
        K = 16 if u == 1 else CD
        worklist("FC", [10, 21] if u == 1 else [20, 21] + list(range(20)), K, CD, "OC", new, 0.5)
        ms(A("FC", sl(11, 10)) if u == 1 else A("FC", sl(22, 6)), 0)
        k_ = sl(0, K); oc = A("OC", sl(0, K // 16))
        cp(A("DGl", k_), IND(A("DD"), oc))
        cp(A("Li", k_), A("LW", k_))
        ts(A("tD", k_), A("Li", k_), 16.0, OP.mult, PK, OP.add)
        cp(A("PP", k_), A("tD", k_))
        ts(A("OP_", k_), A("tD", k_), -1280.0, OP.add, 0.0, OP.max)
        cp(A("TD", k_), IND(A("CTi"), oc))
        tt(A("tD2", k_), IND(A("EW"), oc), A("J1", k_), OP.min)
        cp(A("ED", k_), A("tD2", k_))
        for a in range(0, K, 16):
            cp(IND(A("W1"), A("ED", sl(a, 16))), A("CS", u))

    def tracklist(u):
        t = tile()
        for r in range(0, 16, 2):
            mm([(A(t, sl(0, 56)), [(SUMk(r + q), A("W1", sl(16 * (r + q) + s_, 56, 256))) for q in range(2) for s_ in range(16)]
                 + ([(ID, A("FQ"))] if r == 0 else []), "<" if r == 0 else ">" if r == 14 else "")])
        worklist("FT", [(12 * u + j) % 56 for j in range(56)], 256, 256, "OT", lambda c, m: A(t, sl(c, m)), 16.0 * 32 ** u - 0.5)
        if u < 2:
            act(A("FQ"), A("FT"), AF.Copy, scale=32768.0)

    xw = A("XW", sl(XD, XG - XD))

    def views(u):
        v, w, w2 = A("v"), A("w"), A("w2")
        act(v, IND(A("TVW"), A("OT")), AF.Identity)
        ts(A("vo"), v, 8064.0, OP.min)
        for h in range(2):
            tt(A("w2", sl(128 * h, 128)), A("v", sl(128 * h, 128)), A("J2"), OP.min)
        cp(A("wo"), w2)
        cp(A("OU", sl(1, 16)), A("OT"))
        act(A("xo"), IND(xw, A("OT")), AF.Identity)

    def step2(u, j0, n, ondve, off):
        s = str(nchunk[0] % 2); nchunk[0] += 1; cnt["tag"] = "c%d" % nchunk[0]
        N_ = sl(0, n); G = "G"; g0 = 16 * j0; ot = A("OU", sl(j0 // 16 + 1, n // 16)) if j0 % 32 else A("OT", sl(j0 // 16, n // 16))
        un, FF, nF, xn, nh, ne, w, w2, xo = (A(x, sl(j0, n)) for x in ("un", "FF", "nF", "ft", "gd", "MM", "w", "w2", "xo"))
        win = A("BW", sl(BO, BE - BO))
        for h in range(0, n, 64):
            m = min(64, n - h)
            act(A(G, sl(g0 + 16 * h, 16 * m)), IND(win, A("vo", sl(j0 + h, m))), AF.Relu, bias=256.0, scale=-1.0)
        gk = lambda k: A(G, sl(g0 + k, n, 16))
        t = tile()
        mm([(A(t, N_), [(SUMk(k), gk(k)) for k in range(16)])])
        if "u" in CFG["onact"]:
            act(un, A(t, N_), AF.Relu, bias=64.0, scale=-4.0)
        else:
            ts(un, A(t, N_), 0.5, OP.is_lt, 64.0, OP.mult)
        t = tile()
        mm([(A(t, N_), [(A("WL"), un)])])
        ts(FF, A(t, N_), 63.5 * 64, OP.is_gt, 256.0, OP.mult)
        t = tile()
        mm([(A(t, N_), [(ONES, un)])])
        if "h" in CFG["onact"]:
            act(nh, A(t, N_), AF.Relu, bias=-13.0 * 512, scale=8.0)
        else:
            ts(nh, A(t, N_), 13.5 * 64, OP.is_gt, 512.0, OP.mult)
        g4 = lambda q: A(G, sl(g0 + q, 4 * n, 4))
        m_ = median(n, s, [(ID, G, g0)], FF, True, off, nF=nF)
        t = tile()
        mm([(A(t, N_), [(ID, nh), (NI, m_)])])
        ts(xn, A(t, N_), 256.0, OP.add, 512.0, OP.min)
        cnt["xn"] = cp(IND(xw, ot), xn)
        if "n" in CFG["onact"]:
            t = tile()
            mm([(A(t, N_), [(ID, xn), (NI, xo)])])
            act(ne, A(t, N_), AF.Abs)
        else:
            tt(ne, xn, xo, OP.not_equal)
        misfits(j0, n, lambda q: [(ID, g4(q))], [(ID, xn)], -256.0, CFG["fit"][nchunk[0] - 1])
        t = tile(); th = 4.5
        mm([(A(t, N_), [(SUMk(k), plane(j0, k, n)) for k in range(16)] + [(NI, un), (NI, nh)]), (A(t, sl(128, n)), [(ONES, ne)])])
        ts(w, A(t, N_), th, OP.is_gt, EMPTY, OP.mult)
        ts(w2, A(t, sl(128, n)), 0.5, OP.is_gt, 64.0 * 2 ** u, OP.mult)
        if ondve:
            tt(ne, w2, w, OP.add)
            for k0 in range(0, 16, 8):
                op("dve", [("ts", A("RR", sl(g0 + k, n, 16)), ne, A("DK", sl(k, 1)), None, OP.mult, None) for k in range(k0, k0 + 8)])
            for h in range(0, n, 32):
                m = min(32, n - h)
                cp(IND(A("W3"), A("wo", sl(j0 + h, m))), A("RR", sl(g0 + 16 * h, 16 * m)))
            return
        tt(w2, w2, w, OP.add)
        for k0 in range(0, 16, 4):
            op("act", [("act", A("SS", sl(g0 + k, n, 16)), w2, AF.Copy, 0.0, A("DK", sl(k, 1))) for k in range(k0, k0 + 4)])
        for h in range(0, n, 32):
            m = min(32, n - h)
            act(IND(A("W2"), A("wo", sl(j0 + h, m))), A("SS", sl(g0 + 16 * h, 16 * m)), AF.Silu)

    def decode(u):
        nc = (176, 352, 448)[u]; bl = CFG["blocks"][u]; wb = 0; who = list(CFG["conv"][u])
        for c0, m in zip(bl[::2], bl[1::2]):
            C_ = sl(c0, m); wb = wb if wb + 16 * m <= 3584 else 0
            for h in range(0, 16 * m, 896):
                z = min(896, 16 * m - h); a, b = A("W2b", sl(wb + h, z)), A("W2", sl(16 * c0 + h, z)); e = who.pop(0)
                if e == "a":
                    act(a, b, AF.Identity)
                elif e == "d":
                    cp(a, b)
                else:
                    op("gp", [("sel", a, b)])
            t = tile(); dd = A("DD", sl(CD + c0, m))
            mm([(A(t, sl(0, m)), [(ID, dd)] + [(SUMk(k), A("W2b", sl(wb + k, m, 16))) for k in range(16)], "<")])
            mm([(A(t, sl(0, m)), [(SUMk(k), A("W3", sl(16 * c0 + k, m, 16))) for k in range(16)], ">")])
            wb += 16 * m; ch = 64.0 * 2 ** u
            act(A("tmpB", C_), A(t, sl(0, m)), AF.Abs, bias=-EMPTY / 2 - 1.5 * ch)
            ts(dd, A(t, sl(0, m)), 4096.0, OP.is_gt, EMPTY, OP.mult)
            ts(A("EQ", C_), A("tmpB", C_), ch * ULP - EMPTY / 2, OP.add, ch * ULP, OP.is_equal)

        def flags(t, c0, a):
            return A(t, sl(c0, a)), [(ID, A("FC", sl(c0, a)))] + [(SUMk(r), A("EQ", sl(16 * c0 + r, a, 16))) for r in range(16)]
        t = tile()
        if u == 0:
            mm([flags(t, 10, 1), (A(t, sl(21, 1)), [(ID, A("FC", sl(21, 1)))])])
            t2 = tile()
            mm([flags(t2, 0, 10)])
            ts(A("FC", sl(0, 10)), A(t2, sl(0, 10)), 0.5, OP.is_gt)
        else:
            mm([flags(t, 0, nc // 16)])
        return lambda c, m: A(t, sl(c, m))

    def kill_border(keep=None):
        for q in range(4):
            t = tile(); b = A("BW", sl(BO + q, 224, 4))
            quad(t, 56, [(ID, b)], lambda j: [(BCk(q + 4 * j), A("DD", sl(CD, 56)))] + ([(ID, keep)] if keep else []))
            act(b, A(t, sl(0, 224)), AF.Relu, bias=-65536.0 if keep else 0.0)

    ms(A("FC", sl(0, 11)), 0)
    flag_static(0, 0, 176)
    for u in range(3):
        cnt["tag"] = "k%d" % u
        border = u == 2 and CFG["border"]
        if u:
            new = decode(u - 1)
            if not border:
                kill_border()
            camlist(u, new)
            if u == 1:
                came = cnt["arr"]; sent = exchange(3, "BW", BO, BG); ops[sent]["deps"][came] = False
        if border:
            t = tile(); keep, cap = A("EX", sl(0, 56)), A("EX", sl(64, 56))
            mm([(A(t, sl(r, 4, 16)), [(BCk(r), A("SEL", sl(2, 4)))]) for r in range(16)])
            ts(keep, A(t, sl(0, 56)), -65536.0, OP.mult, 65536.0, OP.add)
            ts(cap, A(t, sl(0, 56)), 65791.0, OP.mult, -255.0, OP.add)
            kill_border(keep)
            step1(u, [(0, 56)], 176, keep, cap)
            sent = exchange(5, "BW", BO, BG)
        cnt["tag"] = "t%d" % u
        tracklist(u)
        views(u)
        j0 = 0
        for ci, segs in enumerate(CFG["s1"][u]):
            dyn = any(c0 < 0 for c0, m in segs)
            step1(u, segs, j0); j0 += sum(m for c0, m in segs)
            if u == 0 and ci == 0:
                sent = exchange(1, "BW", BO, BG)
            if u == 2 and dyn and not border:
                exchange(5, "BW", BO, BG)
        for i in looks if u < 2 else []:
            ops[sent]["deps"].setdefault(i, False)
        j0 = 0
        for n, off in zip(CFG["s2"][u], CFG["off2"][u]):
            step2(u, j0, n, j0 >= CFG["ondve"][u], off); j0 += n
        tt(IND(A("TVW"), A("OT")), A("v"), A("w"), OP.max)
        cnt["tag"] = "f%d" % u
        if u < 2:
            fs = flag_static(u + 1, *((176, 160), (352, 96))[u])
            for i in fs[len(fs) - CFG["hold"][u]:]:
                ops[i]["deps"].setdefault(cnt["xn"], False)
        if u < 2:
            exchange(2 * u + 2, "XW", XO, XG)
    P8 = slice(0, 8); cnt["tag"] = "z"
    dma(A("yx"), A("XW", sl(XO, NT)))
    ts(A("AB", sl(0, NT)), A("TVW", sl(256, NT)), 8064.0, OP.is_lt)
    ts(A("FR"), A("FT"), 32.0, OP.mult)
    for h in range(2):
        t = tile()
        mm([(A(t, sl(r, 28, 16), p=P8), [(A("O8"), A("AB", sl(448 * h + r, 28, 16))),
                                         (A("PX", sl(r, 8, 16)), A("FR", sl(28 * h, 28)))]) for r in range(16)])
        act(A("IDS", sl(448 * h, 448), p=P8), A(t, sl(0, 448), p=P8), AF.Identity)
    dma(A("yt"), A("IDS", p=P8), xor=False)
    ts(A("FQ", sl(0, 28)), decode(2)(0, 28), 0.5, OP.is_gt, 32.0, OP.mult)
    t = tile(); dx = A("EX", sl(0, 112))
    mm([(A(t, sl(0, 112)), [(PX, A("DD", sl(CD + 336, 112)))])])
    cp(dx, A(t, sl(0, 112)))
    for q in range(4):
        t = tile()
        quad(t, 112, [(PX, A("BW", sl(BO + 5376 + q, 448, 4)))], lambda j: [(BCk(q + 4 * j), dx)])
        ts(A("G", sl(q, 448, 4)), A(t, sl(0, 448)), 512.0, OP.min)
    dma(A("yb"), A("G", sl(0, 1792)), xor=False)
    ts(A("AB", sl(1024, NC)), A("DD", sl(CD, NC)), 1.0, OP.is_lt)
    t = tile()
    mm([(A(t, sl(r, 28, 16), p=P8), [(A("O8"), A("AB", sl(1024 + r, 28, 16))), (A("PX", sl(r, 8, 16)), A("FQ", sl(0, 28)))]) for r in range(16)])
    act(A("tmpB", p=P8), A(t, sl(0, 448), p=P8), AF.Identity)
    dma(A("yc"), A("tmpB", p=P8), "act", xor=False)
    return ops


def forward(E, cost, pre, post, npred, succ, prio, tiles, users):
    n = len(E); nd = list(npred); rt = list(pre); start = [0.0] * n; fin = [0.0] * n
    ready = {e: [] for e in sorted(set(E))}; et = {e: 0.0 for e in ready}
    for i in range(n):
        if nd[i] == 0:
            ready[E[i]].append(i)
    bank = {}; extra = {}; order = []; left = {t: len(v) for t, v in users.items()}
    free = {"p": [[0.0, "P%d" % i, None] for i in range(NPB)], "k": [[0.0, "K%d" % i, None] for i in range(8 - NPB)]}
    look, marg = CFG["look"], CFG["marg"]
    while len(order) < n:
        be = None; bm = 1e18; fb = {k: min(v)[0] if v else None for k, v in free.items()}
        for e, L in ready.items():
            c = []; t0 = et[e]
            for i in L:
                t = rt[i] if rt[i] > t0 else t0
                x = tiles[i]
                if x and x not in bank:
                    f = fb[x[0]]
                    if f is None:
                        continue
                    if f > t:
                        t = f
                c.append((t, i))
            if c:
                m = min(c)[0]
                if m < bm:
                    bm = m; be = c
        if be is None:
            return None
        st, i = max((c for c in be if c[0] <= bm + 20.0), key=lambda c: prio[c[1]])
        hi = [c for c in be if c[0] - bm < look * cost[i] and prio[c[1]] > prio[i] + marg]
        if hi:
            st, i = max(hi, key=lambda c: prio[c[1]])
            fit = [c for c in be if c[0] + cost[c[1]] <= st + 20.0]
            if fit:
                st, i = max(fit, key=lambda c: prio[c[1]])
        x = tiles[i]
        if x:
            if x not in bank:
                fl = free[x[0]]; b = max(y for y in fl if y[0] <= st); fl.remove(b); bank[x] = b[1]
                if b[2]:
                    extra[i] = users[b[2]]
            left[x] -= 1
        e = E[i]; start[i] = st; et[e] = st + cost[i]; f = fin[i] = st + cost[i] + post[i]; order.append(i); ready[e].remove(i)
        if x and left[x] == 0:
            free[x[0]].append([max(fin[j] for j in users[x]) + WAKE, bank[x], x])
        for j, g_ in succ[i]:
            if f + g_ + pre[j] > rt[j]:
                rt[j] = f + g_ + pre[j]
            nd[j] -= 1
            if nd[j] == 0:
                ready[E[j]].append(j)
    return order, bank, start, fin, extra


def replay(E, cost, lat, pred, wake, res):
    fin = [0.0] * len(E); et = {}; extra = res[4]
    for i in res[0]:
        t = et.get(E[i], 0.0)
        for j, g_ in pred[i]:
            x = fin[j] + wake if g_ else fin[j]
            if x > t:
                t = x
        for j in extra.get(i, ()):
            if fin[j] + wake > t:
                t = fin[j] + wake
        t += cost[i]; et[E[i]] = t; fin[i] = t + lat[i]
    return max(fin)


def schedule(ops):
    n = len(ops); E = [o["e"] for o in ops]; lat = [o["lat"] for o in ops]; zero = [0.0] * n
    succ = [[] for _ in range(n)]; pred = [[] for _ in range(n)]
    for i, o in enumerate(ops):
        for j, raw in o["deps"].items():
            g_ = WAKE if waits(ops, i, j) else 0.0
            succ[j].append((i, g_)); pred[i].append((j, g_))
    tiles = [o["tiles"][0] if o["tiles"] else None for o in ops]; users = {}
    for i in range(n):
        if tiles[i]:
            users.setdefault(tiles[i], []).append(i)
    mc = [([price(o, m) for o in ops], [x * m["lat"] for x in lat], m["wake"]) for m in FIGURES]
    cost = mc[0][0]; prio = [0.0] * n
    for i in range(n - 1, -1, -1):
        prio[i] += cost[i] + lat[i]
        for j, g_ in pred[i]:
            prio[j] = max(prio[j], prio[i] + g_)
    first = [1e6 if o["sem"] else CFG["boost"] if cost[i] < CFG["small"] and any(E[j] != E[i] for j, g_ in succ[i]) else 0.0 for i, o in enumerate(ops)]
    st = {"best": None, "ref": None}; npred = [len(x) for x in pred]

    def attempt(p):
        res = forward(E, cost, zero, lat, npred, succ, [a + b for a, b in zip(p, first)], tiles, users)
        if res:
            ts = [replay(E, c, l, pred, w, res) for c, l, w in mc]
            st["ref"] = st["ref"] or ts; v = sum(a / b for a, b in zip(ts, st["ref"]))
            if st["best"] is None or v <= st["best"][0]:
                st["best"] = (v, res, ts, p)
        return res
    for r in range(CFG["rounds"]):
        res = attempt(prio)
        if res is None:
            break
        prio = forward(E, cost, lat, zero, [len(x) for x in succ], pred, res[3], [None] * n, {})[3]
    groups = {}
    for i, o in enumerate(ops):
        for g_ in (o["tag"], o["ph"], o["ph"][:-1]):
            groups.setdefault(g_, []).append(i)
    names = sorted(groups); s = CFG["seed"]
    for r in range(CFG["tries"]):
        p = list(st["best"][3] if st["best"] else prio)
        for k in range(2):
            s = (s * 1103515245 + 12345) % 2147483648; g_ = names[(s >> 8) % len(names)]
            s = (s * 1103515245 + 12345) % 2147483648; d = (-12000, -4000, -1200, -400, 400, 1200, 4000, 12000)[(s >> 8) % 8]
            for i in groups[g_]:
                p[i] += d
        attempt(p)
    res = st["best"][1]
    for i, js in res[4].items():
        for j in js:
            ops[i]["deps"].setdefault(j, False)
    return res + (st["best"][2],)


PLAN = {}


def lanes(T, topo, src):
    r = T.rank_of(src); dst = {d: T.cores[r ^ d] for d in range(1, 8)}; me = topo.chip(src)
    far = [d for d in dst if topo.chip(dst[d]) != me]
    far.sort(key=lambda d: topo.mates(me, topo.chip(dst[d])) + topo.same_plane(me, topo.chip(dst[d])))
    es = topo.engines(src, dst[far[0]]); k = len(es) // 2; calls = []
    for part in (far[:k], far[k:]):
        w = 1 << ((len(es) // len(part)).bit_length() - 1)
        calls.append({d: sum(1 << x for x in es[w * j:w * j + w]) for j, d in enumerate(part)})
    near = [d for d in dst if d not in far]
    for j, d in enumerate(near):
        own = [x for x in topo.engines(src, dst[d]) if x not in es][j::len(near)]
        calls[1][d] = sum(1 << x for x in own[:1 << (len(own).bit_length() - 1)])
    return calls


def rank_program(g, core, T, topo):
    rank = T.rank_of(core)
    if rank is None:
        return
    if not PLAN:
        ops = build()
        PLAN["ops"] = ops
        PLAN["s"] = schedule(ops)
    ops = PLAN["ops"]; order, bank = PLAN["s"][:2]
    Q = {"pe": g.tensor, "dve": g.vector, "act": g.scalar, "gp": g, "sp": g.sync}
    mine = lanes(T, topo, core)
    nsent = sum(bin(x).count("1") for m in mine for x in m.values())
    narr = sum(bin(m.get(d, 0)).count("1") for d in range(1, 8) for m in lanes(T, topo, T.cores[rank ^ d]))

    def R(x):
        if not isap(x):
            return x
        if x[0] == "ind":
            return R(x[1]).indirect(R(x[2]))
        return T[bank.get(x[1], x[1])][(x[2] or slice(None),) + tuple(x[3])]
    count = {"pe": 0, "dve": 0, "act": 0, "gp": 0}; tok = {}; seen = {e: {} for e in Q}; allsem = {}
    place = {j: x for x, j in enumerate(order)}; known = {}

    def wait(e, s, v):
        if seen[e].get(s, 0) < v:
            Q[e].wait_ge(T.sem[s], v); seen[e][s] = v
    for i in order:
        o = ops[i]; e = o["e"]
        if e == "arr":
            tok[i] = (o["sem"][0], narr); allsem[o["sem"][0]] = narr
            continue
        for j in sorted(o["deps"], key=lambda j: -place[j]):
            s, v = tok[j]
            if seen[e].get(s, 0) < v and waits(ops, i, j):
                wait(e, s, v)
                for s2, v2 in known.get(j, {}).items():
                    seen[e][s2] = max(seen[e].get(s2, 0), v2)
        known[i] = dict(seen[e])
        q = Q[e]
        for c in o["calls"]:
            k = c[0]; a = [R(x) for x in c[1:]]
            if k == "dma":
                if not c[3]:
                    q.dma_start(a[0], a[1]).then_inc(T.sem[o["sem"][0]], 16); tok[i] = o["sem"]
                    continue
                run = rank & -rank or 8
                for b in range(0, 8, run):
                    x = [("ap", y[1], sl(16 * (b ^ rank if y[1] in IOS else b), 16 * run), y[3] or (slice(None),)) for y in c[1:3]]
                    q.dma_start(R(x[0]), R(x[1])).then_inc(T.sem[o["sem"][0]], 16)
                tok[i] = (o["sem"][0], 16 * 8 // run)
                continue
            if k == "send":
                for m in mine:
                    tr = []
                    for d in m:
                        rid, pid, _ = topo.addr(T.cores[rank ^ d]); a0 = region(c[1])[1] + GH * (d - 1); b0 = c[4] + GH * (d - 1)
                        tr.append(RemoteDMATransfer(dst_ids=[DstId(rid=rid, pnc=pid)], dma_engine_mask=m[d], remote_sem=T.sem["arr%d" % c[2]],
                                                    src=T[c[3]][:, a0:a0 + GH], dst=T[c[3]][:, b0:b0 + GH]))
                    q.remote_dma_fused(tr, local_sem=T.sem[o["sem"][0]])
                tok[i] = (o["sem"][0], nsent)
                continue
            if k == "mm":
                x = q.matmul(a[0], a[1], a[2], a[3], a[4])
            elif k == "tt":
                x = q.tensor_tensor(a[0], a[1], a[2], a[3])
            elif k == "ts":
                x = q.tensor_scalar(a[0], a[1], a[2], a[3], a[4]) if a[5] is None else q.tensor_scalar(a[0], a[1], a[2], a[3], a[4], a[5])
            elif k == "cp":
                x = q.tensor_copy(a[0], a[1])
            elif k == "ms":
                x = q.memset(a[0], a[1])
            elif k == "scan":
                x = q.tensor_tensor_scan(a[0], a[1], a[2], a[3], a[4], a[5])
            elif k == "iota":
                x = q.iota(a[0], a[1], a[2], a[3]) if DTYPE[c[1][1]] == I32 else q.iota(a[0], a[1], a[2], a[3], allow_small_or_imprecise_dtypes=True)
            elif k == "iotax":
                x = q.iota(a[0], [[-32 if rank & 2 else 32, 2], [-16 if rank & 1 else 16, 2], [1, 16]], (64 * a[1]) ^ (16 * rank), 0,
                           allow_small_or_imprecise_dtypes=True)
            elif k == "sel":
                x = q.affine_select(a[0], a[1], [[0, region(c[1])[3]]], OP.is_ge, 0.0, 0, 0)
            elif c[1][0] == "ind":
                x = q.activation(a[0], a[1], a[2])
            else:
                x = q.activation(a[0], a[1], a[2], bias=a[3], scale=a[4])
            if e != "pe" or c is o["calls"][-1]:
                x.then_inc(T.sem[e], 1); count[e] += 1
            tok[i] = (e, count[e])
        allsem[tok[i][0]] = max(allsem.get(tok[i][0], 0), tok[i][1])
    for s, v in allsem.items():
        g.wait_ge(T.sem[s], v)
